import numpy as np, ml_dtypes
CORES = [23,119,17,113]
N = 4
BF = ml_dtypes.bfloat16
def gentries(a):
    return np.ascontiguousarray(a.reshape(8, 16, -1).transpose(0, 2, 1)).reshape(8, -1)
def gtable(e):
    e = np.asarray(e); return np.ascontiguousarray(e.reshape(8, -1, 16).transpose(0, 2, 1)).reshape(128, -1).astype(np.int32)
S, C, B, U, RO, Q = 4096, 4096, 192, 64, 4, 9
L = B + U
def parts(rng):
    sk = (256 * (0.25 + 0.75 * rng.random((N, 8, 1, C))) * rng.random((N, 8, 16, C))).astype(np.int64); sk = np.minimum(sk, 255); sk[..., C - 1] = 0
    oc = np.where(rng.random((N, 8, S)) < 0.05, C - 1, rng.integers(0, C - 1, (N, 8, S)))
    cv = rng.integers(0, S, (N, 8, 16, S)); cd = np.ascontiguousarray(np.argsort(rng.random((N, 8, RO, S)), axis=-1)[..., :L * 16])
    return sk, oc, cv, cd
def fill(rng, share):
    u = rng.random((N, 8, 1, RO, B)); v = rng.random((N, 8, 1, RO, B))
    h = np.where(u < share, 9 + 31 * v, np.where(u < share + 0.1, 4 + 5 * v, np.where(u < share + 0.3, 0.0, 0.2 + 3.8 * v)))
    w = rng.random((N, 8, 16, RO, B)) * (rng.random((N, 8, 16, RO, B)) < 0.7)
    return np.minimum((80 * h * w).astype(np.int64), 4096)
def sums(sk, oc, cd):
    who = np.take_along_axis(oc, cd[:, :, 0, :B * 16], 2)
    return np.add.accumulate(np.take_along_axis(sk, who[:, :, None, :], 3).reshape(N, 8, 16, B, 16), axis=4)
def heavy(rng, sk, oc, cv, cd, nd):
    own = np.arange(S); j = np.arange(B)
    for g in rng.permutation(8)[:2]:
        left = []
        for q in range(N):
            v = rng.integers(200, 256, (16, C)); v[:, C - 1] = 0; e = rng.integers(L, C - 1, S)
            st = cd[q, g, 0].reshape(L, 16); late = st[B:].reshape(-1)
            cd[q, g, 1] = np.concatenate([rng.permutation(st[:B].reshape(-1)), rng.permutation(late)])
            cv[q, g] = rng.choice(np.setdiff1d(own, late), (16, S))
            p = rng.integers(10, 16, B); before = np.add.accumulate(v[:, e[st[:B]]], axis=2)[:, j, p - 1]
            x = 208 + (-before) % 16; want = before + x
            x[rng.integers(0, 16, B), j] -= rng.integers(0, 2, B)
            v[:, :B] = x; e[st[j, p]] = j
            big = rng.permutation(B)[:U // 2]; e[st[big[U // 8:], 8:]] = C - 1
            want[:, big] = 0; want[rng.integers(0, 16, U // 2), big] = 4096
            sk[q, g] = v; oc[q, g] = e; nd[q, g] = 0; nd[q, g, :, 0] = want
            end = np.add.reduce(v[:, e[st[:B]]], axis=2); u = np.nonzero(np.any(end < want, axis=0))[0][:U]
            left.append(np.maximum(want[:, u] - end[:, u], 0))
        for q in range(N):
            w = left[q - 1]; n = w.shape[1]; k = np.arange(n); z = np.argmax(w, axis=0); top = w[z, k]
            st = cd[q, g, 1].reshape(L, 16)[B:B + n]
            line = np.add.accumulate(sk[q, g][z[:, None], oc[q, g][st]], axis=1)
            p = np.add.reduce((line < top[:, None]).astype(np.int64), axis=1)
            before = np.where(p > 0, line[k, np.maximum(p - 1, 0)], 0)
            sk[q, g, z, B + k] = top - before - k % 2; oc[q, g, st[k, p]] = B + k
def pack(sk, oc, cv, cd, nd):
    return {"skill": np.ascontiguousarray(sk.reshape(N, 128, C)).astype(np.float32).astype(BF), "occ": oc.astype(np.int32), "cover": np.ascontiguousarray(cv.reshape(N, 128, S)).astype(np.int32),
            "cards": np.stack([gtable(a.reshape(8, -1)) for a in cd]), "need": np.ascontiguousarray(nd.reshape(N, 128, RO * B)).astype(np.float32).astype(BF)}
def setup_inputs(rng):
    sk, oc, cv, cd = parts(rng)
    return pack(sk, oc, cv, cd, fill(rng, rng.choice(np.array([0.03, 0.1, 0.2, 0.3]), (N, 8, 1, 1, 1))))
def setup_inputs_room(rng):
    sk, oc, cv, cd = parts(rng); nd = np.zeros((N, 8, 16, RO, B), np.int64); pre = sums(sk, oc, cd)
    nd[:, :, :, 0] = pre[..., 0] * (rng.random((N, 8, 1, B)) < 0.5)
    for q in range(N):
        for t in range(RO):
            size = rng.permutation(np.array([0, 1, U - 1, U, U + 1, B, U, 0]))
            for g in range(8):
                n = int(size[g]); lanes = rng.permutation(B)[:n]
                nd[q, g, :, t, lanes] = rng.integers(0, 256, (n, 16)); nd[q, g, rng.integers(0, 16, n), t, lanes] = 4096
    return pack(sk, oc, cv, cd, nd)
def setup_inputs_ties(rng):
    sk, oc, cv, cd = parts(rng)
    few = rng.integers(0, 3, sk.shape) * 16; m = np.arange(8)[None, :, None, None] % 2 == 0
    sk = np.where(m, few, sk // 16 * 16) * (rng.random((N, 8, 1, C)) > 0.1); sk[..., C - 1] = 0
    nd = fill(rng, 0.05); pre = sums(sk, oc, cd)
    p = rng.choice(np.array([0, 0, 1, 3, 7, 14, 15, 15]), (N, 8, B))
    w = np.take_along_axis(pre, p[:, :, None, :, None], 4)[..., 0]
    w = w + 16 * ((np.arange(16)[None, None, :, None] == rng.integers(0, 16, (N, 8, 1, B))) & (rng.random((N, 8, 1, B)) < 0.5))
    nd[:, :, :, 0] = w * (rng.random((N, 8, 1, B)) > 0.3)
    heavy(rng, sk, oc, cv, cd, nd)
    return pack(sk, oc, cv, cd, nd)
def setup_inputs_crowd(rng):
    sk, oc, cv, cd = parts(rng); h = B // 2; sk[..., 0] = 255; own = np.arange(S); o = rng.permutation(8)
    full = np.argsort(rng.random((N, 8, B)), axis=-1)[..., :U]
    for q in range(N):
        for g in range(8):
            card = cd[q, g, 0].reshape(L, 16)
            if g == o[0] or g == o[1]:
                k = rng.permutation(np.setdiff1d(own, card[full[q, g]].reshape(-1))); a, b = k[:L], k[L:2 * L]
                mid = rng.permutation(np.setdiff1d(own, k[:2 * L]))[:14 * L].reshape(L, 14)
                cd[q, g, 1] = np.concatenate([a[:, None], mid, b[:, None]], axis=1).reshape(-1)
                v = np.clip(sk[q, g], 16, 239); v[:, :16] = rng.integers(240, 256, (16, 16)); v[:, C - 1] = 0; sk[q, g] = v
                oc[q, g, a] = rng.integers(16, C - 1, L); oc[q, g, b] = rng.integers(0, 16, L)
                c = np.repeat(own[None, :], 16, axis=0)
                if g == o[0]: c[:, a] = b[rng.integers(0, 2, (16, L))]
                else: c[:, a] = np.where(np.arange(16)[:, None] >= rng.integers(0, 16, L)[None, :], b[None, :], a[None, :])
                cv[q, g] = c
            else:
                pool = card[h:h + 16, 15]; oc[q, g, pool[:8]] = 0
                c = pool[rng.integers(0, 16, (16, S))]; kind = rng.integers(0, 5, S)
                c[:15] = np.where(kind >= 3, own, c[:15]); c[15] = np.where(kind == 4, own, c[15]); cv[q, g] = c
    nd = fill(rng, 0.05); pre = sums(sk, oc, cd)
    nd[:, :, :, 0] = pre[..., 0] * (np.arange(B) < h); nd[:, o[:2]] = 0
    for q in range(N):
        for g in o[:2]:
            z = rng.integers(0, 16, U); l = full[q, g]; nd[q, g, z, 0, l] = pre[q, g, z, l, 15] // 16 * 16 + 16
            nd[q, g, rng.integers(0, 16, B), 1, np.arange(B)] = rng.integers(1, 17, B)
    return pack(sk, oc, cv, cd, nd)
def setup_inputs_bare(rng):
    sk, oc, cv, cd = parts(rng); h = rng.permutation(8)
    oc = np.where(rng.random((N, 8, S)) < rng.choice(np.array([0.4, 0.6, 0.8]), (N, 8, 1)), C - 1, oc); oc[:, h[0]] = C - 1
    ends = np.array([0, 1, S - 2, S - 1]); cv[:, h[2]] = rng.choice(ends, (N, 16, S)); oc[:, h[2], :2] = rng.integers(0, C - 1, (N, 2)); oc[:, h[2], S - 2:] = rng.integers(0, C - 1, (N, 2))
    nd = fill(rng, 0.05) * (rng.random((N, 8, 1, RO, B)) < 0.5); nd[::2, h[1]] = 0
    return pack(sk, oc, cv, cd, nd)
def setup_inputs_spread(rng):
    sk, oc, cv, cd = parts(rng)
    sk = np.minimum((np.exp2(8.2 * rng.random((N, 8, 1, C))) * rng.random((N, 8, 16, C))).astype(np.int64), 255); sk[..., C - 1] = 0
    oc = np.where(rng.random((N, 8, S)) < 0.1, C - 1, np.minimum(((C - 1) * rng.random((N, 8, S)) ** 3).astype(np.int64), C - 2))
    cv = np.minimum((S * rng.random((N, 8, 16, S)) ** 2).astype(np.int64), S - 1)
    nd = (np.minimum(np.exp2(12.2 * rng.random((N, 8, 1, RO, B))), 4096) * rng.choice(np.array([0.0, 0.25, 0.5, 1.0]), (N, 8, 16, RO, B))).astype(np.int64)
    return pack(sk, oc, cv, cd, nd * (rng.random((N, 8, 1, RO, B)) > 0.3))
def check_inputs(d):
    bad = []
    for k, hi in (("skill", 255), ("need", 4096), ("occ", C - 1), ("cover", S - 1), ("cards", S - 1)):
        x = np.asarray(d[k]).astype(np.float64)
        if not np.all((x >= 0) & (x <= hi) & (x == np.floor(x))): bad.append("range of " + k)
    if not np.all(np.asarray(d["skill"])[:, :, C - 1].astype(np.float32) == 0): bad.append("last column of skill")
    e = np.sort(np.asarray(d["cards"]).reshape(N, 8, 16, RO, L).transpose(0, 1, 3, 2, 4).reshape(N, 8, RO, 16 * L), axis=-1)
    if np.any(e[..., 1:] == e[..., :-1]): bad.append("equal stations on the cards of a round")
    return bad
def reference(skill, occ, cover, cards, need):
    sk = skill.astype(np.float32).astype(np.int64).reshape(N, 8, 16, C); cv = cover.astype(np.int64).reshape(N, 8, 16, S)
    cd = np.stack([gentries(a) for a in cards]).astype(np.int64).reshape(N, 8, RO, L, 16); nd = need.astype(np.float32).astype(np.int64).reshape(N, 8, 16, RO, B)
    oc = np.array(occ, dtype=np.int64); arrived = np.zeros((N, 8, 16, U), np.int64)
    for t in range(RO):
        sent = np.zeros((N, 8, 16, U), np.int64)
        for r in range(N):
            w = np.concatenate([nd[r, :, :, t], arrived[r]], axis=2)
            st = cd[r, :, t]; flat = st.reshape(8, -1)
            who = np.take_along_axis(oc[r], flat, 1)
            col = np.take_along_axis(sk[r], who[:, None, :], 2).reshape(8, 16, L, 16)
            pre = np.add.accumulate(col, axis=3)
            met = np.all(pre >= w[..., None], axis=1)
            zero = np.all(w == 0, axis=1)
            leave = ~np.concatenate([zero[..., None], met[..., :15]], axis=2)
            unmet = ~met[..., 15]; before = np.add.accumulate(unmet.astype(np.int64), axis=1) - unmet
            rest = np.maximum(w - pre[..., 15], 0); g, l = np.nonzero(unmet & (before < U))
            sent[(r + 1) % N][g, :, before[g, l]] = rest[g, :, l]
            np.put_along_axis(oc[r], flat, np.where(leave.reshape(8, -1), C - 1, who), 1)
            s = st[..., 0]; lost = leave[..., 0] & (who.reshape(8, L, 16)[..., 0] != C - 1)
            m = np.take_along_axis(cv[r], s[:, None, :], 2)
            a = np.take_along_axis(oc[r], m.reshape(8, -1), 1)
            ka = np.take_along_axis(sk[r], a[:, None, :], 2).reshape(8, 16, 16, L)
            a = a.reshape(8, 16, L); good = np.add.reduce((ka >= col[:, :, None, :, 0]).astype(np.int64), axis=1)
            fit = (a != C - 1) & (good >= Q); ok = lost & np.any(fit, axis=1)
            i = np.argmax(fit, axis=1)[:, None, :]
            src = np.take_along_axis(m, i, 1)[:, 0]; new = np.take_along_axis(a, i, 1)[:, 0]
            for g in range(8):
                lanes = np.nonzero(ok[g])[0]
                out, at = np.unique(src[g, lanes], return_index=True); lanes = lanes[at]
                oc[r, g, s[g, lanes]] = new[g, lanes]; oc[r, g, out] = C - 1
        arrived = sent
    return {"y": oc.astype(np.float32)}

@@ -1,0 +1,516 @@
+from concourse.mybir import AluOpType, ActivationFunctionType
+
+OP = AluOpType
+FN = ActivationFunctionType
+K0, TOL = 14, 7
+CH = [(0, 32), (32, 32), (64, 64), (128, 64), (192, 64)]
+VL = 176
+FG = [(0, 64), (64, 64), (128, 48)]
+SG3 = [(176, 32), (208, 32), (240, 16)]
+PART = [("P6", 0, 128), ("P4", 128, 128)]
+STEP1 = "v0 a1 b0 a2 b1 s0+s1 l0+l1+s2 r32 t0 t1 v3 l2+s3 q0 t2 v4 l3 t3 s4 q1 x0+y0 l4"
+STEP3 = "u0 L0+p0 P0 Q0 g0 g1 v0 c0 s0 g2 v1 s1 c3 c2 s2 m0 v2 f0 c1 c4 o0+C0 f1 o1"
+
+_sb = {
+    "OH": (4096, "float16"), "OLU": (256, "uint16"), "OCN": (256, "int32"), "OCH": (256, "float16"),
+    "SK": (4096, "bfloat16"), "COV": (4096, "int32"), "CI": (1024, "int32"), "CU": (1024, "uint16"), "CF": (1024, "float16"),
+    "ND": (768, "bfloat16"), "NN": (768, "bfloat16"), "LS": (128, "uint16"), "KS": (64, "float32"),
+    "WA": (4608, "float32"), "WB": (4608, "float32"), "OO": (4608, "float32"),
+    "ONE": (512, "bfloat16"), "I": (128, "bfloat16"), "NI": (128, "bfloat16"), "B": (128, "bfloat16"), "BB": (128, "bfloat16"),
+    "PX": (2048, "bfloat16"), "ZB": (144, "bfloat16"), "ZH": (144, "bfloat16"), "CM": (128, "bfloat16"),
+    "Z0": (144, "bfloat16"), "Z15": (144, "bfloat16"), "Z8": (144, "bfloat16"), "G8": (8, "bfloat16"), "G15": (8, "bfloat16"),
+    "TRI": (128, "bfloat16"), "UP": (128, "bfloat16"), "UN": (128, "bfloat16"), "UM": (128, "bfloat16"), "W3": (128, "bfloat16"),
+    "PI": (1, "int32"), "PA": (1, "int32"), "XC": (1, "float32"), "ZR": (256, "float32"), "LY": (16, "float32"), "KM": (16, "float32"),
+    "KD": (32, "float32"), "DM": (1024, "bfloat16"), "ON16": (16, "float32"), "ZZ": (256, "bfloat16"),
+    "D0": (528, "bfloat16"), "D1": (528, "bfloat16"), "D2": (1040, "bfloat16"), "D3": (1040, "bfloat16"), "D4": (1040, "float32"),
+    "R": (3072, "bfloat16"), "RF": (1024, "float32"), "IN1": (4096, "bfloat16"), "X": (4096, "float32"),
+    "NA": (64, "bfloat16"), "AR": (64, "float32"), "RR": (256, "float32"), "U01": (256, "bfloat16"), "UL": (16, "bfloat16"),
+    "UK": (16, "float32"), "UK2": (16, "float32"), "CY": (16, "float32"), "SP": (16, "float32"), "OF": (16, "float32"), "OU": (16, "uint16"),
+    "BS": (512, "bfloat16"), "BT": (256, "float32"), "BRF": (VL * 16, "float32"), "BRH": (4096 - VL * 16, "bfloat16"),
+    "CLF0": (256, "float16"), "CLU0": (256, "uint16"), "CLF1": (256, "float16"), "CLU1": (256, "uint16"),
+    "IN3": (VL * 16, "bfloat16"), "GA": (4096 - VL * 16, "bfloat16"), "SGN": (4096 - VL * 16, "bfloat16"),
+    "L1": (16, "float32"), "L2": (16, "float32"), "LOST": (16, "float32"),
+    "F": (256, "bfloat16"), "SM": (512, "float16"), "CR": (256, "float16"), "OKL": (16, "float32"), "OB": (16, "float32"),
+    "CLM": (16, "float32"), "R2": (32, "float32"), "R3": (32, "float32"), "R4": (32, "float32"), "OFS": (32, "uint16"), "MLU": (16, "uint16"),
+    "VB": (512, "float32"), "OV": (256, "float32"),
+    "DL": (256, "bfloat16"), "ZF": (256, "float32"), "OFN": (256, "float32"), "OI": (256, "int32"), "EF": (256, "float32"), "YF": (256, "float32"),
+}
+SCRATCH = {k: ("sbuf", [128, n], d) for k, (n, d) in _sb.items()}
+SCRATCH["E"] = ("sbuf", [128, 16, 256], "bfloat16")
+SCRATCH["MK"] = ("sbuf", [128, 16, 16], "bfloat16")
+SCRATCH["MD"] = ("sbuf", [128, 16, 16], "bfloat16")
+for _t in range(3):
+    SCRATCH["SW%d" % _t] = ("sbuf", [128, 512], "int32")
+    SCRATCH["AV%d" % _t] = ("sbuf", [128, 64], "int32")
+SCRATCH["TA"] = ("psum", [128, 1024], "float32")
+SCRATCH["TB"] = ("psum", [128, 1024], "float32")
+for _t in range(4, 8):
+    SCRATCH["P%d" % _t] = ("psum", [128, 512], "float32")
+PS = ("TA", "TB", "P4", "P5", "P6", "P7")
+SEMAPHORES = ["cV", "cS", "cT", "cG"] + ["arr%d" % t for t in range(3)] + ["loc%d" % t for t in range(3)] + ["d%d" % k for k in range(8)]
+
+
+def rank_program(g, core, T, topo):
+    rank = T.rank_of(core)
+    if rank is None:
+        return
+    queues = {"V": g.vector, "S": g.scalar, "T": g.tensor, "G": g, "Y": g.sync}
+    count = {"cV": 0, "cS": 0, "cT": 0, "cG": 0}
+    known = {q: {} for q in queues}
+    clocks = {}
+    log = {}
+    nd = [0]
+    hold = [None]
+
+    def A(name, a=0, b=None, s=1):
+        n = SCRATCH[name][1][1]
+        b = n if b is None else b
+        ap = T[name][:, a:b] if s == 1 else T[name][:, a:b:s]
+        return (ap, [(name, a, b, s)])
+
+    def ind(win, off):
+        return (win[0].indirect(off[0]), win[1] + off[1])
+
+    def keys(name, a, b, s=1):
+        if name in PS:
+            return [("%s.%d" % (name, k), 0, 512, 1, True) for k in range(a // 512, (b - 1) // 512 + 1)]
+        return [(name, a, b, s, False)]
+
+    def apart(a, b, s, x, y, z):
+        return x >= b or y <= a or (s == z and s > 1 and (a - x) % s != 0)
+
+    def need_event(q, ev):
+        if known[q].get(ev[0], 0) >= ev[1]:
+            return
+        queues[q].wait_ge(T.sem[ev[0]], ev[1])
+        k = known[q]
+        for s, v in clocks.get(ev, {}).items():
+            if k.get(s, 0) < v:
+                k[s] = v
+        if k.get(ev[0], 0) < ev[1]:
+            k[ev[0]] = ev[1]
+
+    def deps(q, reads, writes):
+        out = {}
+        for ops, w in ((reads, False), (writes, True)):
+            for o in ops:
+                for region in o[1]:
+                    for key, lo, hi, st, bank in keys(*region):
+                        for (x, y, ev, eq, ew, z) in log.get(key, []):
+                            if apart(lo, hi, st, x, y, z) or (eq == q == "T" and bank):
+                                continue
+                            if (ew or w or (bank and eq != q)) and out.get(ev[0], 0) < ev[1]:
+                                out[ev[0]] = ev[1]
+        return out
+
+    def record(q, ev, reads, writes):
+        for ops, w in ((reads, False), (writes, True)):
+            for o in ops:
+                for region in o[1]:
+                    for key, lo, hi, st, bank in keys(*region):
+                        keep = []
+                        for r in log.get(key, []):
+                            inside = lo <= r[0] and r[1] <= hi and (st == 1 or (st == r[5] and (lo - r[0]) % st == 0))
+                            if inside and r[3] == q and r[2][0] == ev[0] and (w or not r[4]):
+                                continue
+                            keep.append(r)
+                        keep.append((lo, hi, ev, q, w, st))
+                        log[key] = keep
+
+    def waits(q, reads, writes):
+        for s, v in sorted(deps(q, reads, writes).items(), key=lambda e: -e[1]):
+            need_event(q, (s, v))
+
+    def emit(q, fn, reads, writes):
+        if hold[0] is not None:
+            hold[0].append((q, fn, reads, writes))
+            return
+        waits(q, reads, writes)
+        sem = "c" + q
+        inst = fn()
+        count[sem] += 1
+        inst.then_inc(T.sem[sem], 1)
+        ev = (sem, count[sem])
+        clocks[ev] = dict(known[q])
+        record(q, ev, reads, writes)
+
+    def together(parts):
+        if len(parts) == 1:
+            return parts[0]()
+        lists = []
+        for f in parts:
+            hold[0] = []
+            f()
+            units = []
+            for call in hold[0]:
+                if call[0] == "V" or not units:
+                    units.append([])
+                units[-1].append(call)
+            lists.append(units)
+        hold[0] = None
+        while any(lists):
+            for units in lists:
+                if units:
+                    for call in units.pop(0):
+                        emit(*call)
+
+    def dma(q, out, in_, reads, writes):
+        waits(q, reads, writes)
+        ev = ("d%d" % nd[0], 16)
+        nd[0] += 1
+        queues[q].dma_start(out, in_).then_inc(T.sem[ev[0]], 16)
+        clocks[ev] = dict(known[q])
+        record("dma%d" % nd[0], ev, reads, writes)
+        return ev
+
+    V, S, TE = g.vector, g.scalar, g.tensor
+
+    def vts(out, i, s1, op0, s2=None, op1=None):
+        rd = [i] + [s for s in (s1, s2) if isinstance(s, tuple)]
+        a1 = s1[0] if isinstance(s1, tuple) else s1
+        a2 = s2[0] if isinstance(s2, tuple) else s2
+        if op1 is None:
+            emit("V", lambda: V.tensor_scalar(out[0], i[0], a1, None, op0), rd, [out])
+        else:
+            emit("V", lambda: V.tensor_scalar(out[0], i[0], a1, a2, op0, op1), rd, [out])
+
+    def vtt(out, i, j, op):
+        emit("V", lambda: V.tensor_tensor(out[0], i[0], j[0], op), [i, j], [out])
+
+    def vcp(out, i):
+        emit("V", lambda: V.tensor_copy(out[0], i[0]), [i], [out])
+
+    def vms(out, c):
+        emit("V", lambda: V.memset(out[0], c), [], [out])
+
+    def scan_(out, m, d, first):
+        emit("V", lambda: V.tensor_tensor_scan(out[0], m[0], d[0], first, OP.mult, OP.add), [m, d], [out])
+
+    def act(out, i, fn, bias=0.0, scale=1.0):
+        if bias == 0.0 and scale == 1.0:
+            emit("S", lambda: S.activation(out[0], i[0], fn), [i], [out])
+        else:
+            emit("S", lambda: S.activation(out[0], i[0], fn, bias=bias, scale=scale), [i], [out])
+
+    def mm(out, l, r, start=True, stop=True):
+        emit("T", lambda: TE.matmul(out[0], l[0], r[0], start, stop), [l, r], [out])
+
+    def sel(out, i, pattern, op, fill, base, mult):
+        emit("G", lambda: g.affine_select(out[0], i[0], pattern, op, fill, base, mult), [i], [out])
+
+    def gcp(out, i, n):
+        sel(out, i, [[0, n]], OP.is_ge, 0.0, 0, 0)
+
+    def iota(out, pattern, base, mult, small=True):
+        if small:
+            emit("G", lambda: g.iota(out[0], pattern, base, mult, allow_small_or_imprecise_dtypes=True), [], [out])
+        else:
+            emit("G", lambda: g.iota(out[0], pattern, base, mult), [], [out])
+
+    def EX(name, x):
+        return A(name, 15 - x, 143 - x)
+
+    def collect(out, name, rhs):
+        for x in range(16):
+            mm(out, EX(name, x), rhs(x), x == 0, x == 15)
+
+    dma("S", T.OCN[:, :], T.occ[:, :], [], [A("OCN")])
+    dma("S", T.CI[:, :], T.cards[:, :], [], [A("CI")])
+    skills = dma("S", T.SK[:, :], T.skill[:, :], [], [A("SK")])
+    dma("Y", T.ND[:, :], T.need[:, :], [], [A("ND")])
+    need_event("Y", skills)
+    dma("Y", T.COV[:, :], T.cover[:, :], [], [A("COV")])
+
+    iota(A("PI"), [[0, 1]], 0, 1, False)
+    vms(A("ONE"), 1.0)
+    for z in ("Z0", "ZB", "Z8", "Z15"):
+        vms(A(z), 0.0)
+    vms(A("CM"), -1.0 / 16)
+    sel(A("G8"), A("ONE", 0, 8), [[-16, 8]], OP.is_equal, 0.0, 0, 1)
+    iota(A("ZR"), [[0, 16], [1, 16]], 0, 0)
+    for k in range(4):
+        sel(A("PX", 512 * k, 512 * k + 512), A("ONE"), [[-1, 4], [-16, 8], [0, 16]], OP.is_equal, 0.0, -4 * k, 1)
+    iota(A("LY"), [[16, 16]], 0, 0)
+    sel(A("G15"), A("ONE", 0, 8), [[-16, 8]], OP.is_equal, 0.0, -15, 1)
+    sel(A("I"), A("ONE", 0, 128), [[-1, 128]], OP.is_equal, 0.0, 0, 1)
+    sel(A("UN"), A("ONE", 0, 128), [[-16, 8], [0, 16]], OP.is_ge, 0.0, 0, 1)
+    sel(A("B"), A("UN"), [[16, 8], [0, 16]], OP.is_ge, 0.0, 15, -1)
+    sel(A("UP"), A("B"), [[-1, 128]], OP.is_gt, 0.0, 0, 1)
+    for h in range(2):
+        sel(A("DM", 512 * h, 512 * h + 512), A("ONE"), [[0, 32], [1, 16]], OP.is_gt, 0.0, 0, 0)
+    sel(A("TRI"), A("B"), [[1, 128]], OP.is_gt, 0.0, 0, -1)
+    iota(A("VB", 256, 512), [[0, 256]], 0, 0)
+    iota(A("ON16"), [[0, 16]], 1, 0)
+    iota(A("ZZ"), [[0, 256]], 0, 0)
+    iota(A("NA"), [[0, 64]], 0, 0)
+    for t in range(3):
+        iota(A("SW%d" % t, 0, 64), [[0, 64]], 0, 0, False)
+    vcp(A("Z0", 15, 143, 16), A("G8"))
+    vts(A("Z8", 15, 143, 16), A("G8"), -8192.0, OP.mult)
+    vts(A("PA"), A("PI"), 15, OP.bitwise_and)
+    vcp(A("XC"), A("PA"))
+    mk = (T.MK[:, :, :], [("MK", 0, 16)])
+    for y in range(16):
+        vts((T.MK[:, y, :], [("MK", y, y + 1)]), A("ZR", 0, 16), A("XC"), OP.is_gt)
+    vts(A("OCH"), A("OCN"), -2048.0, OP.add)
+    for k in range(8):
+        ps, c = (("P6", 0), ("P7", 0), ("TA", 0), ("TA", 512), ("TB", 0), ("TB", 512), ("P4", 0), ("P6", 0))[k]
+        for h in range(2):
+            x = 2 * k + h
+            mm(A(ps, c + 256 * h, c + 256 * h + 256), A("PX", 128 * x, 128 * x + 128), A("OCH"))
+        if k % 2 == 0:
+            vcp(A("OH", 512 * k, 512 * k + 512), A(ps, c, c + 512))
+        else:
+            act(A("OH", 512 * k, 512 * k + 512), A(ps, c, c + 512), FN.Copy)
+    collect(A("P5", 0, 256), "Z0", lambda x: A("OH", x, 4096, 16))
+    vts(A("CF"), A("CI"), -2048.0, OP.add)
+    vcp(A("Z15", 15, 143, 16), A("G15"))
+    collect(A("P7", 0, 64), "Z0", lambda x: A("CF", x, 1024, 16))
+    collect(A("P7", 64, 128), "Z15", lambda x: A("CF", x, 1024, 16))
+    vcp(A("CU"), A("CI"))
+    vts(A("OLU"), A("P5", 0, 256), 2048.0, OP.add)
+    vts(A("KD", 0, 16), A("LY"), A("XC"), OP.add)
+    vts(A("KD", 16, 32), A("KD", 0, 16), 256.0, OP.add)
+    vts(A("KM"), A("KD", 0, 16), 256.0, OP.add)
+    vcp(A("ZB", 15, 143, 16), A("B", 0, 128, 16))
+    vts(A("BB"), A("B"), 1048576.0, OP.mult)
+    vts(A("ZH"), A("ZB"), 0.5, OP.mult)
+    vts(A("NI"), A("I"), -1.0, OP.mult)
+    vts(A("UM"), A("UP"), -1.0, OP.mult)
+    sel(A("W3"), A("UM"), [[-1, 128]], OP.not_equal, 1000.0, 0, 1)
+    vts(A("LS"), A("P7", 0, 128), 2048.0, OP.add)
+    vts(A("KS"), A("LS", 0, 64), 512.0, OP.add)
+    vts(A("NN"), A("ND"), -1024.0, OP.mult)
+    vms(A("SK", 4095, 4096), -14.0 / 1024)
+    for k in range(8):
+        o, i = A("WA", 512 + 512 * k, 1024 + 512 * k), ind(A("SK"), A("OLU", 32 * k, 32 * k + 32))
+        if k % 2 == 0:
+            vts(o, i, 1024.0, OP.mult, float(K0), OP.add)
+        else:
+            act(o, i, FN.Identity, float(K0), 1024.0)
+
+    def covers(t):
+        f, u = "CLF%d" % (t % 2), "CLU%d" % (t % 2)
+        vts(A(f), ind(A("COV"), A("LS", 16 * t, 16 * t + 16)), -2048.0, OP.add)
+        vts(A(u), A(f), 2048.0, OP.add)
+
+    def moved():
+        act(ind(A("OO"), A("OFS", 0, 16)), A("OV"), FN.Silu)
+
+    win = ["WA", "WB"]
+    for t in range(4):
+        W, N = win[t % 2], win[1 - t % 2]
+        wst, nst = A(W, 512, 4608), A(N, 512, 4608)
+        clf, clu = "CLF%d" % (t % 2), "CLU%d" % (t % 2)
+        brep = [(A("BRF", i, VL * 16, 16), A("BT", 0, VL), VL) for i in range(16)]
+        brep += [(A("BRH", i, 4096 - VL * 16, 16), A("BS", VL, 256), 256 - VL) for i in range(16)]
+
+        def Dc(c, a, b, s=1):
+            return A("D%d" % c, a, b, s)
+
+        def own(k):
+            if k == 0:
+                act(A("BS", 256, 512), ind(wst, A("LS", 64 + 16 * t, 80 + 16 * t)), FN.Copy)
+                return
+            act(A("BS", 0, 256), ind(wst, A("LS", 16 * t, 16 * t + 16)), FN.Copy)
+            act(A("BT"), A("BS", 0, 256), FN.Identity, -float(TOL))
+
+        def gather(c, q):
+            l0, n = CH[c]
+            o, i = Dc(c, 1, 1 + 16 * n), ind(wst, A("CU", 256 * t + l0, 256 * t + l0 + n))
+            if q == "V":
+                vcp(o, i)
+            else:
+                act(o, i, FN.Copy)
+
+        def repeat(k):
+            for j in range(k):
+                o, i, m = brep.pop(0)
+                gcp(o, i, m)
+
+        def psum(c, a, b, s=1):
+            name, off = (("TA", 0), ("TA", 512), ("TB", 0), ("TA", 0), ("TB", 0))[c]
+            return A(name, off + a, off + b, s)
+
+        def scan(c):
+            l0, n = CH[c]
+            if c < 4:
+                vcp(Dc(c, 0, 16 * n, 16), A("NN", 192 * t + l0, 192 * t + l0 + n))
+            elif t:
+                ev = ("arr%d" % (t - 1), len(topo.engines(T.cores[rank - 1], core)))
+                record("net", ev, [], [A("AV%d" % (t - 1))])
+                vts(Dc(4, 0, 1024, 16), A("AV%d" % (t - 1)), -1024.0, OP.mult)
+                vts(A("NA"), A("AV%d" % (t - 1)), -1024.0, OP.mult)
+            else:
+                vms(Dc(4, 0, 1024, 16), 0.0)
+            r = A("R", 16 * l0, 16 * l0 + 16 * n) if c < 4 else A("RF")
+            scan_(r, A("DM", 0, 16 * n), Dc(c, 0, 16 * n), 0.0)
+            vts(A("IN1", 16 * l0, 16 * l0 + 16 * n), r, -512.0, OP.is_ge, -15.5 / 16, OP.add)
+            for k in range(n // 32):
+                mm(psum(c, 512 * k, 512 * k + 512), A("BB"), A("IN1", 16 * l0 + 512 * k, 16 * l0 + 512 * k + 512))
+
+        def total(c):
+            l0, n = CH[c]
+            if t < 3:
+                for p in range(16):
+                    mm(A("P4", l0, l0 + n), A("I"), Dc(c, p, 16 * n, 16), p == 0, False)
+                mm(A("P4", l0, l0 + n), A("I"), A("BS", 256 + l0, 256 + l0 + n), False, True)
+
+        def leave(c):
+            l0, n = CH[c]
+            vtt(A("X", 16 * l0, 16 * l0 + 16 * n), Dc(c, 1, 1 + 16 * n), psum(c, 0, 16 * n), OP.min)
+            vtt(A("X", 16 * l0 + 15, 16 * l0 + 16 * n, 16), A("BS", 256 + l0, 256 + l0 + n), psum(c, 15, 16 * n, 16), OP.min)
+            act(ind(nst, A("CU", 256 * t + l0, 256 * t + l0 + n)), A("X", 16 * l0, 16 * l0 + 16 * n), FN.Silu)
+
+        def lost(k):
+            if k == 0:
+                collect(A("P5", 256, 268), "ZB", lambda x: A("NN", 192 * t + x, 192 * t + 192, 16))
+                collect(A("P5", 272, 288), "ZB", lambda x: A("BS", x, 256, 16))
+            else:
+                collect(A("P5", 268, 272), "ZB", lambda x: A("NA", x, 64, 16))
+
+        def rest(c):
+            if t < 3:
+                vtt(A("AR"), A("RF", 15, 1024, 16), A("BS", 448, 512), OP.add)
+                vts(A("RR", 192, 256), A("AR"), -1.0 / 1024, OP.mult, 0.0, OP.max)
+
+        def rest2(c):
+            if t < 3:
+                vts(A("RR", 0, 192), A("P4", 0, 192), -1.0 / 1024, OP.mult, 0.0, OP.max)
+                vts(A("U01"), A("RR"), 0.5, OP.is_gt)
+
+        def run(order, do):
+            for step in order.split():
+                together([(lambda s=s: do[s[0]](int(s[1:]))) for s in step.split("+")])
+
+        run(STEP1, {"v": lambda c: gather(c, "V"), "a": lambda c: gather(c, "S"), "b": own, "r": repeat, "s": scan, "t": total,
+                    "l": leave, "q": lost, "x": rest, "y": rest2})
+        if t == 0:
+            covers(0)
+
+        def unmet(c):
+            if t < 3:
+                collect(A("P5", 0, 16), "ZB", lambda x: A("U01", x, 256, 16))
+
+        def lost2(c):
+            vts(A("L1"), A("P5", 256, 272), -512.0, OP.is_lt)
+            vts(A("L2"), A("P5", 272, 288), float(TOL), OP.is_ge)
+            vtt(A("LOST"), A("L1"), A("L2"), OP.mult)
+
+        def slots(c):
+            if t < 3:
+                vts(A("UL"), A("P5", 0, 16), 0.5, OP.is_ge)
+                vts(A("UK"), A("P5", 0, 16), 0.5, OP.is_lt)
+                mm(A("P5", 16, 32), A("B"), A("UL"))
+                mm(A("P5", 32, 48), A("W3"), A("UL"))
+
+        def slots2(c):
+            if t < 3:
+                vtt(A("UK2"), A("UK"), A("KM"), OP.mult)
+                scan_(A("CY"), A("ON16"), A("P5", 16, 32), -1001.0)
+                vtt(A("SP"), A("P5", 32, 48), A("CY"), OP.add)
+                vtt(A("OF"), A("SP"), A("UK2"), OP.max)
+                vcp(A("OU"), A("OF"))
+
+        def slots3(c):
+            if t < 3:
+                vcp(ind(A("SW%d" % t), A("OU")), A("RR"))
+
+        def spsum(k):
+            return A(*(("TA", 0, 512), ("TA", 512, 1024), ("TB", 0, 16 * SG3[2][1]))[k])
+
+        def sgather(k):
+            l0, n = SG3[k]
+            ga, br = A("GA", 16 * (l0 - VL), 16 * (l0 - VL + n)), A("BRH", 16 * (l0 - VL), 16 * (l0 - VL + n))
+            act(ga, ind(nst, A(clu, l0, l0 + n)), FN.Copy)
+            mm(spsum(k), A("NI"), br, True, False)
+            mm(spsum(k), A("I"), ga, False, True)
+
+        def ssign(k):
+            l0, n = SG3[k]
+            act(A("SGN", 16 * (l0 - VL), 16 * (l0 - VL + n)), spsum(k), FN.Sign, float(TOL))
+
+        def fused(k):
+            l0, n = FG[k]
+            vtt(A("IN3", 16 * l0, 16 * (l0 + n)), ind(nst, A(clu, l0, l0 + n)), A("BRF", 16 * l0, 16 * (l0 + n)), OP.is_ge)
+
+        def counts(k):
+            for i in range(16):
+                if k == 0 or k == 3:
+                    h = 64 if k else 0
+                    mm(A("P6", h, h + 64), EX("ZB", i), A("IN3", 16 * h + i, 16 * h + 1024, 16), i == 0, i == 15)
+                elif k == 1:
+                    mm(A("P4", 0, VL - 128), EX("ZB", i), A("IN3", 2048 + i, VL * 16, 16), i == 0, False)
+                else:
+                    a, b = ((0, 64), (64, 256 - VL))[k == 4]
+                    mm(A("P4", VL - 128 + a, VL - 128 + b), EX("ZH", i), A("SGN", 16 * a + i, 16 * b, 16), i == 0, i == 15)
+            if k == 1:
+                mm(A("P4", 0, VL - 128), A("CM"), A("ONE", 0, VL - 128), False, True)
+
+        def fits(k):
+            p, l0, n = PART[k]
+            vts(A("F", l0, l0 + n), A(p, 0, n), (8.5, 0.5)[k], OP.is_ge)
+            mm(A(p, 256, 256 + n), A("TRI"), A("F", l0, l0 + n))
+
+        def first(k):
+            p, l0, n = PART[k]
+            vtt(A("SM", 256 + l0, 256 + l0 + n), A("F", l0, l0 + n), A(p, 256, 256 + n), OP.is_gt)
+            vtt(A("SM", l0, l0 + n), A("SM", 256 + l0, 256 + l0 + n), A(clf, l0, l0 + n), OP.mult)
+
+        def covers_next(c):
+            if t < 3:
+                covers(t + 1)
+
+        def moved_before(c):
+            if t:
+                moved()
+
+        run(STEP3, {"u": unmet, "g": sgather, "s": ssign, "v": fused, "c": counts, "f": fits, "o": first, "L": lost2, "p": slots,
+                    "P": slots2, "Q": slots3, "m": moved_before, "C": covers_next})
+        mm(A("P4", 0, 256), A("B"), A("SM", 0, 256))
+        collect(A("P5", 64, 96), "ZB", lambda x: A("SM", x, 512, 16))
+        act(A("CR"), A("P4", 0, 256), FN.Copy)
+        vtt(A("OKL"), A("P5", 80, 96), A("LOST"), OP.mult)
+        vts(A("MLU"), A("P5", 64, 80), 2048.0, OP.add)
+        act(A("VB", 0, 256), ind(nst, A("MLU")), FN.Copy)
+        if t == 0:
+            act(A("OO", 512, 4608), A("OH"), FN.Silu, 2080.0)
+        act(A("OV"), ind(A("OO", 512, 4608), A("MLU")), FN.Copy)
+        mm(A("P4", 0, 256), A("B"), A("ZZ"), True, False)
+        for y in range(16):
+            ey = (T.E[:, y, 0:256 - 16 * y], [("E", 256 * y, 256 * y + 256)])
+            vts(ey, A("CR", 16 * y, 256), A("P5", 64 + y, 65 + y), OP.is_equal, A("OKL", y, y + 1), OP.mult)
+            if y < 15:
+                mm(A("P4", 16 * y + 16, 256), A("B"), (T.E[:, y, 16:256 - 16 * y], ey[1]), False, False)
+        md = (T.MD[:, :, :], [("MD", 0, 16)])
+        vtt(md, (T.E[:, :, 0:16], [("E", 0, 4096)]), mk, OP.mult)
+        mm(A("P4", 0, 256), A("B"), md, False, True)
+        vts(A("OB"), A("OKL"), 8192.0, OP.mult, -8192.0, OP.add)
+        vts(A("CLM"), A("P5", 64, 80), 2560.0, OP.add)
+        vtt(A("R2", 0, 16), A("OB"), A("KS", 16 * t, 16 * t + 16), OP.add)
+        vtt(A("R2", 16, 32), A("OB"), A("CLM"), OP.add)
+        vcp(A("DL"), A("P4", 0, 256))
+        collect(A("P5", 128, 144), "Z8", lambda x: A("DL", x, 256, 16))
+        if t < 3:
+            dst = T.cores[(rank + 1) % len(T.cores)]
+            addr = topo.addr(dst)
+            src = A("SW%d" % t, 0, 64)
+            waits("G", [src], [])
+            g.remote_dma(out_ap=T["AV%d" % t][:, :], in_ap=src[0], remote_sem=T.sem["arr%d" % t], local_sem=T.sem["loc%d" % t],
+                         pid=addr[1], routing_id=addr[0], dma_engine_mask=topo.mask(core, dst))
+        vtt(A("R3", 0, 16), A("P5", 128, 144), A("R2", 0, 16), OP.add)
+        vtt(A("R3", 16, 32), A("P5", 128, 144), A("R2", 16, 32), OP.add)
+        vtt(A("R4"), A("R3"), A("KD"), OP.max)
+        vcp(A("OFS"), A("R4"))
+        vcp(ind(A(N), A("OFS")), A("VB"))
+    moved()
+    dma("Y", T.ZF[:, :], T.WA[0:128:16, 512:4608], [A("WA", 512, 4608)], [A("ZF")])
+    dma("Y", T.OFN[:, :], T.OO[0:128:16, 512:4608], [A("OO", 512, 4608)], [A("OFN")])
+    vts(A("EF"), A("ZF"), float(TOL), OP.is_lt, 4095.0, OP.mult)
+    vts(A("OI"), A("OFN"), -32.0, OP.add)
+    vtt(A("YF"), A("OI"), A("EF"), OP.max)
+    need_event("Y", dma("Y", T.y[:, :], T.YF[:, :], [A("YF")], []))
+    for t in range(3):
+        g.wait_ge(T.sem["loc%d" % t], len(topo.engines(core, T.cores[(rank + 1) % len(T.cores)])))
+    for s in ("cV", "cS", "cT", "cG"):
+        need_event("G", (s, count[s]))

@@ -2,43 +2,42 @@ from concourse.mybir import AluOpType, ActivationFunctionType
 
 OP = AluOpType
 FN = ActivationFunctionType
-K0, TOL = 14, 7
-CH = [(0, 32), (32, 32), (64, 64), (128, 64), (192, 64)]
-VL = 176
-FG = [(0, 64), (64, 64), (128, 48)]
-SG3 = [(176, 32), (208, 32), (240, 16)]
-PART = [("P6", 0, 128), ("P4", 128, 128)]
-STEP1 = "v0 a1 b0 a2 b1 s0+s1 l0+l1+s2 r32 t0 t1 v3 l2+s3 q0 t2 v4 l3 t3 s4 q1 x0+y0 l4"
-STEP3 = "u0 L0+p0 P0 Q0 g0 g1 v0 c0 s0 g2 v1 s1 c3 c2 s2 m0 v2 f0 c1 c4 o0+C0 f1 o1"
+MARK, THR, CAP = 7.0 / 64, 1.0 / 512, 32768.0
+MET = 16 * CAP - 8
+CH = [(0, 16, "V", "TA", 0), (16, 32, "S", "TA", 512), (48, 32, "V", "TB", 0), (80, 48, "V", "TA", 0), (128, 64, "V", "TB", 0),
+      (192, 32, "V", "TA", 0), (224, 32, "V", "TA", 512)]
+VL = 128
+FG = [(0, 64), (64, 64)]
+SG3 = [(128, 32, "TA", 0), (160, 32, "TA", 512), (192, 32, "TB", 0), (224, 32, "TB", 512)]
+CNT = [(0, 64), (64, 64), (128, 64), (192, 64)]
+PART = [(0, 128, "P6", "P7"), (128, 128, "P4", "P5")]
+CYC, CALL, HOP, PE, GATHER, SCATTER = 0.00083, 0.03, 0.11, 0.00042, 1.56, 3.0
+PW = max(p[1] for p in PART)
+EN = sum(p[1] * p[1] // 16 for p in PART)
 
 _sb = {
-    "OH": (4096, "float16"), "OLU": (256, "uint16"), "OCN": (256, "int32"), "OCH": (256, "float16"),
-    "SK": (4096, "bfloat16"), "COV": (4096, "int32"), "CI": (1024, "int32"), "CU": (1024, "uint16"), "CF": (1024, "float16"),
-    "ND": (768, "bfloat16"), "NN": (768, "bfloat16"), "LS": (128, "uint16"), "KS": (64, "float32"),
-    "WA": (4608, "float32"), "WB": (4608, "float32"), "OO": (4608, "float32"),
-    "ONE": (512, "bfloat16"), "I": (128, "bfloat16"), "NI": (128, "bfloat16"), "B": (128, "bfloat16"), "BB": (128, "bfloat16"),
-    "PX": (2048, "bfloat16"), "ZB": (144, "bfloat16"), "ZH": (144, "bfloat16"), "CM": (128, "bfloat16"),
-    "Z0": (144, "bfloat16"), "Z15": (144, "bfloat16"), "Z8": (144, "bfloat16"), "G8": (8, "bfloat16"), "G15": (8, "bfloat16"),
-    "TRI": (128, "bfloat16"), "UP": (128, "bfloat16"), "UN": (128, "bfloat16"), "UM": (128, "bfloat16"), "W3": (128, "bfloat16"),
-    "PI": (1, "int32"), "PA": (1, "int32"), "XC": (1, "float32"), "ZR": (256, "float32"), "LY": (16, "float32"), "KM": (16, "float32"),
-    "KD": (32, "float32"), "DM": (1024, "bfloat16"), "ON16": (16, "float32"), "ZZ": (256, "bfloat16"),
-    "D0": (528, "bfloat16"), "D1": (528, "bfloat16"), "D2": (1040, "bfloat16"), "D3": (1040, "bfloat16"), "D4": (1040, "float32"),
-    "R": (3072, "bfloat16"), "RF": (1024, "float32"), "IN1": (4096, "bfloat16"), "X": (4096, "float32"),
-    "NA": (64, "bfloat16"), "AR": (64, "float32"), "RR": (256, "float32"), "U01": (256, "bfloat16"), "UL": (16, "bfloat16"),
-    "UK": (16, "float32"), "UK2": (16, "float32"), "CY": (16, "float32"), "SP": (16, "float32"), "OF": (16, "float32"), "OU": (16, "uint16"),
-    "BS": (512, "bfloat16"), "BT": (256, "float32"), "BRF": (VL * 16, "float32"), "BRH": (4096 - VL * 16, "bfloat16"),
+    "OLU": (256, "uint16"), "OCN": (256, "int32"), "OCH": (256, "float16"), "WHO": (4096, "float16"), "OL0": (32, "uint16"),
+    "SK": (4112, "bfloat16"), "COV": (4096, "int32"), "CI": (1024, "int32"), "CU": (1024, "uint16"), "CF": (1024, "float16"), "CS": (1024, "uint16"),
+    "ND": (768, "bfloat16"), "LS": (128, "uint16"), "KS": (64, "float32"),
+    "WA": (4624, "float32"), "WB": (4624, "float32"), "OO": (4608, "float32"), "YR": (4608, "float32"),
+    "ONE": (512, "bfloat16"), "I": (128, "bfloat16"), "NI": (128, "bfloat16"), "B": (128, "bfloat16"), "BB": (128, "bfloat16"), "CB": (128, "bfloat16"),
+    "PX": (2048, "bfloat16"), "ZB": (144, "bfloat16"), "ZH": (144, "bfloat16"), "BH": (128, "bfloat16"), "PAT": (512, "bfloat16"),
+    "Z0": (144, "bfloat16"), "Z15": (144, "bfloat16"), "G8": (8, "bfloat16"), "G15": (8, "bfloat16"), "SH": (128, "bfloat16"), "S1": (128, "bfloat16"),
+    "TRI": (128, "bfloat16"), "UP": (128, "bfloat16"), "UN": (128, "bfloat16"), "W3": (128, "bfloat16"), "IB": (128, "bfloat16"),
+    "PI": (1, "int32"), "PA": (1, "int32"), "XC": (1, "float32"), "SC": (2, "float32"), "ZR": (16, "float32"), "XM": (16, "float32"), "LY": (32, "float32"),
+    "KM": (16, "float16"), "KD": (32, "float32"), "ON16": (16, "float32"), "ZZ": (512, "bfloat16"), "OFFS": (256, "bfloat16"),
+    "D": (4096 + 16 * len(CH), "bfloat16"), "NC": (4096, "float16"), "R": (4096, "float16"),
+    "X": (4096, "float32"), "RR": (256, "float16"), "UL": (17, "bfloat16"), "SP": (16, "float32"), "OF": (16, "float32"), "OU": (16, "uint16"),
+    "BS": (512, "bfloat16"), "BT": (256, "float16"), "BRF": (VL * 16, "float16"), "NL": (512, "bfloat16"),
     "CLF0": (256, "float16"), "CLU0": (256, "uint16"), "CLF1": (256, "float16"), "CLU1": (256, "uint16"),
-    "IN3": (VL * 16, "bfloat16"), "GA": (4096 - VL * 16, "bfloat16"), "SGN": (4096 - VL * 16, "bfloat16"),
-    "L1": (16, "float32"), "L2": (16, "float32"), "LOST": (16, "float32"),
-    "F": (256, "bfloat16"), "SM": (512, "float16"), "CR": (256, "float16"), "OKL": (16, "float32"), "OB": (16, "float32"),
-    "CLM": (16, "float32"), "R2": (32, "float32"), "R3": (32, "float32"), "R4": (32, "float32"), "OFS": (32, "uint16"), "MLU": (16, "uint16"),
+    "IN3": (4096, "bfloat16"), "GA": (4096 - VL * 16, "bfloat16"),
+    "SM": (256, "bfloat16"), "FC": (512, "float16"), "CR": (256, "float16"), "VC": (16, "float32"), "VAL": (32, "float32"),
+    "E": (EN, "bfloat16"), "EM": (EN, "bfloat16"), "EZ": (EN, "bfloat16"), "EX": (16, "bfloat16"),
+    "R3": (32, "float32"), "R4": (32, "float32"), "OFS": (32, "uint16"), "MLU": (16, "uint16"),
     "VB": (512, "float32"), "OV": (256, "float32"),
-    "DL": (256, "bfloat16"), "ZF": (256, "float32"), "OFN": (256, "float32"), "OI": (256, "int32"), "EF": (256, "float32"), "YF": (256, "float32"),
+    "ZF": (256, "float32"), "OFN": (256, "float32"), "OI": (256, "int32"), "EF": (256, "float32"), "YF": (256, "float32"),
 }
 SCRATCH = {k: ("sbuf", [128, n], d) for k, (n, d) in _sb.items()}
-SCRATCH["E"] = ("sbuf", [128, 16, 256], "bfloat16")
-SCRATCH["MK"] = ("sbuf", [128, 16, 16], "bfloat16")
-SCRATCH["MD"] = ("sbuf", [128, 16, 16], "bfloat16")
 for _t in range(3):
     SCRATCH["SW%d" % _t] = ("sbuf", [128, 512], "int32")
     SCRATCH["AV%d" % _t] = ("sbuf", [128, 64], "int32")
@@ -47,7 +46,28 @@ SCRATCH["TB"] = ("psum", [128, 1024], "float32")
 for _t in range(4, 8):
     SCRATCH["P%d" % _t] = ("psum", [128, 512], "float32")
 PS = ("TA", "TB", "P4", "P5", "P6", "P7")
-SEMAPHORES = ["cV", "cS", "cT", "cG"] + ["arr%d" % t for t in range(3)] + ["loc%d" % t for t in range(3)] + ["d%d" % k for k in range(8)]
+SEMAPHORES = ["cV", "cS", "cT", "cG"] + ["arr%d" % t for t in range(3)] + ["loc%d" % t for t in range(3)] + ["d%d" % k for k in range(12)]
+
+
+def issue_order(calls):
+    n = len(calls)
+    way = [0.0] * n
+    for k in range(n - 1, -1, -1):
+        way[k] += calls[k]["cost"] + calls[k]["lag"]
+        for p, hop in calls[k]["after"].items():
+            way[p] = max(way[p], way[k] + hop)
+    start, done, busy = [0.0] * n, [0.0] * n, {}
+    for k in sorted(range(n), key=lambda j: (-way[j], j)):
+        c = calls[k]
+        at = max([done[p] + hop for p, hop in c["after"].items()] + [0.0])
+        slots = busy.setdefault(c["q"], [])
+        i = 0
+        while i < len(slots) and slots[i][0] < at + c["cost"]:
+            at = max(at, slots[i][1])
+            i += 1
+        slots.insert(i, (at, at + c["cost"]))
+        start[k], done[k] = at, at + c["cost"] + c["lag"]
+    return sorted(range(n), key=lambda j: (start[j], j))
 
 
 def rank_program(g, core, T, topo):
@@ -55,21 +75,17 @@ def rank_program(g, core, T, topo):
     if rank is None:
         return
     queues = {"V": g.vector, "S": g.scalar, "T": g.tensor, "G": g, "Y": g.sync}
-    count = {"cV": 0, "cS": 0, "cT": 0, "cG": 0}
-    known = {q: {} for q in queues}
-    clocks = {}
+    calls = []
     log = {}
-    nd = [0]
-    hold = [None]
 
     def A(name, a=0, b=None, s=1):
         n = SCRATCH[name][1][1]
         b = n if b is None else b
         ap = T[name][:, a:b] if s == 1 else T[name][:, a:b:s]
-        return (ap, [(name, a, b, s)])
+        return (ap, [(name, a, b, s)], len(range(a, b, s)), False)
 
     def ind(win, off):
-        return (win[0].indirect(off[0]), win[1] + off[1])
+        return (win[0].indirect(off[0]), win[1] + off[1], 16 * off[2], True)
 
     def keys(name, a, b, s=1):
         if name in PS:
@@ -79,438 +95,382 @@ def rank_program(g, core, T, topo):
     def apart(a, b, s, x, y, z):
         return x >= b or y <= a or (s == z and s > 1 and (a - x) % s != 0)
 
-    def need_event(q, ev):
-        if known[q].get(ev[0], 0) >= ev[1]:
-            return
-        queues[q].wait_ge(T.sem[ev[0]], ev[1])
-        k = known[q]
-        for s, v in clocks.get(ev, {}).items():
-            if k.get(s, 0) < v:
-                k[s] = v
-        if k.get(ev[0], 0) < ev[1]:
-            k[ev[0]] = ev[1]
-
-    def deps(q, reads, writes):
-        out = {}
-        for ops, w in ((reads, False), (writes, True)):
-            for o in ops:
-                for region in o[1]:
-                    for key, lo, hi, st, bank in keys(*region):
-                        for (x, y, ev, eq, ew, z) in log.get(key, []):
-                            if apart(lo, hi, st, x, y, z) or (eq == q == "T" and bank):
-                                continue
-                            if (ew or w or (bank and eq != q)) and out.get(ev[0], 0) < ev[1]:
-                                out[ev[0]] = ev[1]
-        return out
-
-    def record(q, ev, reads, writes):
+    def emit(q, fn, reads, writes, cost, lag=0.0, kind="compute", after=()):
+        me, dep = len(calls), {p: HOP for p in after}
         for ops, w in ((reads, False), (writes, True)):
             for o in ops:
                 for region in o[1]:
                     for key, lo, hi, st, bank in keys(*region):
                         keep = []
                         for r in log.get(key, []):
-                            inside = lo <= r[0] and r[1] <= hi and (st == 1 or (st == r[5] and (lo - r[0]) % st == 0))
-                            if inside and r[3] == q and r[2][0] == ev[0] and (w or not r[4]):
-                                continue
+                            x, y, z, p, pq, pw = r
+                            if p != me and not apart(lo, hi, st, x, y, z) and (pw or w or (bank and pq != q)):
+                                if bank and pq == q == "T":
+                                    dep.setdefault(p, 0.0)
+                                else:
+                                    dep[p] = HOP
+                                if w and lo <= x and y <= hi and (st == 1 or st == z):
+                                    continue
                             keep.append(r)
-                        keep.append((lo, hi, ev, q, w, st))
+                        keep.append((lo, hi, st, me, q, w))
                         log[key] = keep
+        calls.append({"q": q, "fn": fn, "after": dep, "cost": cost, "lag": lag, "kind": kind})
+        return me
 
-    def waits(q, reads, writes):
-        for s, v in sorted(deps(q, reads, writes).items(), key=lambda e: -e[1]):
-            need_event(q, (s, v))
+    def issue():
+        count = {"cV": 0, "cS": 0, "cT": 0, "cG": 0}
+        known = {q: {} for q in queues}
+        clocks, event, nd = {}, {}, [0]
 
-    def emit(q, fn, reads, writes):
-        if hold[0] is not None:
-            hold[0].append((q, fn, reads, writes))
-            return
-        waits(q, reads, writes)
-        sem = "c" + q
-        inst = fn()
-        count[sem] += 1
-        inst.then_inc(T.sem[sem], 1)
-        ev = (sem, count[sem])
-        clocks[ev] = dict(known[q])
-        record(q, ev, reads, writes)
+        def need(q, ev):
+            if known[q].get(ev[0], 0) >= ev[1]:
+                return
+            queues[q].wait_ge(T.sem[ev[0]], ev[1])
+            k = known[q]
+            for s, v in list(clocks.get(ev, {}).items()) + [ev]:
+                k[s] = max(k.get(s, 0), v)
 
-    def together(parts):
-        if len(parts) == 1:
-            return parts[0]()
-        lists = []
-        for f in parts:
-            hold[0] = []
-            f()
-            units = []
-            for call in hold[0]:
-                if call[0] == "V" or not units:
-                    units.append([])
-                units[-1].append(call)
-            lists.append(units)
-        hold[0] = None
-        while any(lists):
-            for units in lists:
-                if units:
-                    for call in units.pop(0):
-                        emit(*call)
+        for k in issue_order(calls):
+            c = calls[k]
+            q = c["q"]
+            if c["kind"] == "arrival":
+                event[k] = c["fn"]
+                continue
+            want = {}
+            for p, hop in c["after"].items():
+                if hop and p in event:
+                    want[event[p][0]] = max(want.get(event[p][0], 0), event[p][1])
+            for s, v in sorted(want.items(), key=lambda e: -e[1]):
+                need(q, (s, v))
+            inst = c["fn"]()
+            if c["kind"] == "remote":
+                continue
+            if c["kind"] == "dma":
+                ev = ("d%d" % nd[0], 16)
+                nd[0] += 1
+                inst.then_inc(T.sem[ev[0]], 16)
+            else:
+                count["c" + q] += 1
+                ev = ("c" + q, count["c" + q])
+                inst.then_inc(T.sem[ev[0]], 1)
+            event[k] = ev
+            clocks[ev] = dict(known[q])
+        for k in range(nd[0]):
+            need("Y", ("d%d" % k, 16))
+        for s in count:
+            need("G", (s, count[s]))
 
-    def dma(q, out, in_, reads, writes):
-        waits(q, reads, writes)
-        ev = ("d%d" % nd[0], 16)
-        nd[0] += 1
-        queues[q].dma_start(out, in_).then_inc(T.sem[ev[0]], 16)
-        clocks[ev] = dict(known[q])
-        record("dma%d" % nd[0], ev, reads, writes)
-        return ev
+    def dma(out, in_, reads, writes, lag, after=()):
+        return emit("Y", lambda: g.sync.dma_start(out, in_), reads, writes, 0.05, lag, "dma", after)
 
     V, S, TE = g.vector, g.scalar, g.tensor
+
+    def cost(out, ins, rate=None):
+        if out[3] or (ins and ins[0][3]):
+            return 0.06 + out[2] * (SCATTER if out[3] else GATHER) * CYC
+        if rate is None:
+            rate = 0.5 if all(SCRATCH[o[1][0][0]][2] in ("bfloat16", "float16", "uint16") for o in [out] + ins) else 1.0
+        return CALL + max(64, out[2] * rate) * CYC
 
     def vts(out, i, s1, op0, s2=None, op1=None):
         rd = [i] + [s for s in (s1, s2) if isinstance(s, tuple)]
         a1 = s1[0] if isinstance(s1, tuple) else s1
         a2 = s2[0] if isinstance(s2, tuple) else s2
         if op1 is None:
-            emit("V", lambda: V.tensor_scalar(out[0], i[0], a1, None, op0), rd, [out])
+            emit("V", lambda: V.tensor_scalar(out[0], i[0], a1, None, op0), rd, [out], cost(out, [i]))
         else:
-            emit("V", lambda: V.tensor_scalar(out[0], i[0], a1, a2, op0, op1), rd, [out])
+            emit("V", lambda: V.tensor_scalar(out[0], i[0], a1, a2, op0, op1), rd, [out], cost(out, [i]))
 
     def vtt(out, i, j, op):
-        emit("V", lambda: V.tensor_tensor(out[0], i[0], j[0], op), [i, j], [out])
+        emit("V", lambda: V.tensor_tensor(out[0], i[0], j[0], op), [i, j], [out], cost(out, [i, j], 1.0))
 
     def vcp(out, i):
-        emit("V", lambda: V.tensor_copy(out[0], i[0]), [i], [out])
+        emit("V", lambda: V.tensor_copy(out[0], i[0]), [i], [out], cost(out, [i]))
 
     def vms(out, c):
-        emit("V", lambda: V.memset(out[0], c), [], [out])
+        emit("V", lambda: V.memset(out[0], c), [], [out], cost(out, []))
 
-    def scan_(out, m, d, first):
-        emit("V", lambda: V.tensor_tensor_scan(out[0], m[0], d[0], first, OP.mult, OP.add), [m, d], [out])
+    def scan_(out, m, d, first, op0=OP.mult, op1=OP.add):
+        emit("V", lambda: V.tensor_tensor_scan(out[0], m[0], d[0], first, op0, op1), [m, d], [out], cost(out, [m, d]))
 
-    def act(out, i, fn, bias=0.0, scale=1.0):
+    def act(out, i, fn, bias=0.0, scale=1.0, more=0.0):
         if bias == 0.0 and scale == 1.0:
-            emit("S", lambda: S.activation(out[0], i[0], fn), [i], [out])
+            emit("S", lambda: S.activation(out[0], i[0], fn), [i], [out], cost(out, [i], 1.0) + more)
         else:
-            emit("S", lambda: S.activation(out[0], i[0], fn, bias=bias, scale=scale), [i], [out])
+            emit("S", lambda: S.activation(out[0], i[0], fn, bias=bias, scale=scale), [i], [out], cost(out, [i], 1.0) + more)
 
     def mm(out, l, r, start=True, stop=True):
-        emit("T", lambda: TE.matmul(out[0], l[0], r[0], start, stop), [l, r], [out])
+        emit("T", lambda: TE.matmul(out[0], l[0], r[0], start, stop), [l, r], [out], 0.005 + max(64, r[2]) * PE)
 
     def sel(out, i, pattern, op, fill, base, mult):
-        emit("G", lambda: g.affine_select(out[0], i[0], pattern, op, fill, base, mult), [i], [out])
+        emit("G", lambda: g.affine_select(out[0], i[0], pattern, op, fill, base, mult), [i], [out], 0.17 + 2 * out[2] * CYC)
 
     def gcp(out, i, n):
         sel(out, i, [[0, n]], OP.is_ge, 0.0, 0, 0)
 
     def iota(out, pattern, base, mult, small=True):
         if small:
-            emit("G", lambda: g.iota(out[0], pattern, base, mult, allow_small_or_imprecise_dtypes=True), [], [out])
+            emit("G", lambda: g.iota(out[0], pattern, base, mult, allow_small_or_imprecise_dtypes=True), [], [out], 0.13 + 2 * out[2] * CYC)
         else:
-            emit("G", lambda: g.iota(out[0], pattern, base, mult), [], [out])
+            emit("G", lambda: g.iota(out[0], pattern, base, mult), [], [out], 0.13 + 2 * out[2] * CYC)
 
     def EX(name, x):
         return A(name, 15 - x, 143 - x)
 
-    def collect(out, name, rhs):
-        for x in range(16):
-            mm(out, EX(name, x), rhs(x), x == 0, x == 15)
+    def collect(out, name, rhs, first=0):
+        for x in range(first, 16):
+            mm(out, EX(name, x), rhs(x), x == first, x == 15)
 
-    dma("S", T.OCN[:, :], T.occ[:, :], [], [A("OCN")])
-    dma("S", T.CI[:, :], T.cards[:, :], [], [A("CI")])
-    skills = dma("S", T.SK[:, :], T.skill[:, :], [], [A("SK")])
-    dma("Y", T.ND[:, :], T.need[:, :], [], [A("ND")])
-    need_event("Y", skills)
-    dma("Y", T.COV[:, :], T.cover[:, :], [], [A("COV")])
+    d0 = dma(T.OCN[:, :], T.occ[:, :], [], [A("OCN")], 2.6)
+    d1 = dma(T.CI[:, 0:256], T.cards[:, 0:256], [], [A("CI", 0, 256)], 3.2)
+    d2 = dma(T.SK[:, 0:4096], T.skill[:, :], [], [A("SK", 0, 4096)], 8.4)
+    d3 = dma(T.ND[:, :], T.need[:, :], [], [A("ND")], 9.3)
+    d4 = dma(T.COV[:, :], T.cover[:, :], [], [A("COV")], 12.5, [d2])
+    d5 = dma(T.CI[:, 256:1024], T.cards[:, 256:1024], [], [A("CI", 256, 1024)], 14.5, [d2])
+    for a, b in ((d0, d1), (d1, d2), (d2, d3), (d3, d4), (d4, d5)):
+        calls[b]["after"].setdefault(a, -calls[a]["lag"])
 
-    iota(A("PI"), [[0, 1]], 0, 1, False)
     vms(A("ONE"), 1.0)
-    for z in ("Z0", "ZB", "Z8", "Z15"):
-        vms(A(z), 0.0)
-    vms(A("CM"), -1.0 / 16)
-    sel(A("G8"), A("ONE", 0, 8), [[-16, 8]], OP.is_equal, 0.0, 0, 1)
-    iota(A("ZR"), [[0, 16], [1, 16]], 0, 0)
-    for k in range(4):
-        sel(A("PX", 512 * k, 512 * k + 512), A("ONE"), [[-1, 4], [-16, 8], [0, 16]], OP.is_equal, 0.0, -4 * k, 1)
-    iota(A("LY"), [[16, 16]], 0, 0)
-    sel(A("G15"), A("ONE", 0, 8), [[-16, 8]], OP.is_equal, 0.0, -15, 1)
-    sel(A("I"), A("ONE", 0, 128), [[-1, 128]], OP.is_equal, 0.0, 0, 1)
+    iota(A("PI"), [[0, 1]], 0, 1, False)
+    iota(A("ZR"), [[1, 16]], 0, 0)
     sel(A("UN"), A("ONE", 0, 128), [[-16, 8], [0, 16]], OP.is_ge, 0.0, 0, 1)
     sel(A("B"), A("UN"), [[16, 8], [0, 16]], OP.is_ge, 0.0, 15, -1)
-    sel(A("UP"), A("B"), [[-1, 128]], OP.is_gt, 0.0, 0, 1)
-    for h in range(2):
-        sel(A("DM", 512 * h, 512 * h + 512), A("ONE"), [[0, 32], [1, 16]], OP.is_gt, 0.0, 0, 0)
-    sel(A("TRI"), A("B"), [[1, 128]], OP.is_gt, 0.0, 0, -1)
-    iota(A("VB", 256, 512), [[0, 256]], 0, 0)
-    iota(A("ON16"), [[0, 16]], 1, 0)
-    iota(A("ZZ"), [[0, 256]], 0, 0)
-    iota(A("NA"), [[0, 64]], 0, 0)
-    for t in range(3):
-        iota(A("SW%d" % t, 0, 64), [[0, 64]], 0, 0, False)
-    vcp(A("Z0", 15, 143, 16), A("G8"))
-    vts(A("Z8", 15, 143, 16), A("G8"), -8192.0, OP.mult)
+    sel(A("G8"), A("ONE", 0, 8), [[-16, 8]], OP.is_equal, 0.0, 0, 1)
+    for k in range(4):
+        act(A("NC", 512 * k, 512 * k + 512), A("ONE"), FN.Silu, 0.0, CAP, 0.0 if k else 1.3)
+    for k in range(4, 8):
+        vms(A("NC", 512 * k, 512 * k + 512), CAP)
+    for z in ("Z0", "ZB", "Z15"):
+        vms(A(z), 0.0)
     vts(A("PA"), A("PI"), 15, OP.bitwise_and)
+    vms(A("D", 0, None, 16), 2 * CAP)
     vcp(A("XC"), A("PA"))
-    mk = (T.MK[:, :, :], [("MK", 0, 16)])
-    for y in range(16):
-        vts((T.MK[:, y, :], [("MK", y, y + 1)]), A("ZR", 0, 16), A("XC"), OP.is_gt)
+    vms(A("SK", 4096, 4112), CAP / 8)
+    vts(A("XM"), A("ZR"), A("XC"), OP.is_equal)
+    vcp(A("Z0", 15, 143, 16), A("G8"))
+    for x in range(16):
+        vts(A("PX", 128 * x, 128 * x + 128), A("B"), A("XM", x, x + 1), OP.mult)
+    sel(A("I"), A("ONE", 0, 128), [[-1, 128]], OP.is_equal, 0.0, 0, 1)
+    sel(A("PAT"), A("ONE"), [[0, 32], [1, 16]], OP.is_equal, 0.0, -15, 0)
+    iota(A("LY"), [[16, 32]], 0, 0)
+    sel(A("G15"), A("ONE", 0, 8), [[-16, 8]], OP.is_equal, 0.0, -15, 1)
+    iota(A("WB", 4608, 4624), [[0, 16]], int(2 * CAP), 0)
+    iota(A("WA", 4608, 4624), [[0, 16]], int(2 * CAP), 0)
+    sel(A("UP"), A("B"), [[-1, 128]], OP.is_gt, 0.0, 0, 1)
+    sel(A("TRI"), A("B"), [[1, 128]], OP.is_gt, 0.0, 0, -1)
+    sel(A("SH"), A("B"), [[1, 128]], OP.is_equal, 0.0, -1, -1)
+    iota(A("VB"), [[0, 512]], 0, 0)
+    iota(A("ON16"), [[0, 16]], 1, 0)
+    iota(A("ZZ"), [[0, 512]], 0, 0)
+    iota(A("UL"), [[0, 17]], 0, 0)
+    iota(A("OFFS", 0, VL), [[0, VL]], -8, 0)
+    iota(A("OFFS", VL, 256), [[0, 256 - VL]], 0, 0)
+    for t in range(3):
+        iota(A("SW%d" % t, 0, 64), [[0, 64]], -2048, 0, False)
+    for k in range(9):
+        iota(A("YR", 512 * k, 512 * k + 512), [[0, 512]], 0, 0)
+    vts(A("SC", 0, 1), A("XM", 0, 1), 2048.0, OP.mult, 2048.0, OP.add)
+    vts(A("CB"), A("B"), A("XM", 0, 1), OP.mult, -2 * CAP, OP.mult)
+    vts(A("S1"), A("B"), A("XM", 1, 2), OP.mult, -16384 * CAP, OP.mult)
+    vts(A("PAT"), A("PAT"), A("XM", 1, 2), OP.max)
+    vts(A("BB"), A("B"), 1024.0, OP.mult)
+    vtt(A("CB"), A("CB"), A("S1"), OP.add)
+    vcp(A("ZB", 15, 143, 16), A("B", 0, 128, 16))
+    vcp(A("Z15", 15, 143, 16), A("G15"))
+    vts(A("KD"), A("LY"), A("XC"), OP.add)
+    vts(A("ZH"), A("ZB"), 0.5, OP.mult)
+    vts(A("BH"), A("B"), -0.5, OP.mult)
+    vts(A("KM"), A("KD", 0, 16), 256.0, OP.add)
+    vts(A("NI"), A("I"), -1.0, OP.mult)
+    vts(A("IB"), A("I"), -2048.0, OP.mult)
+    vtt(A("W3"), A("B"), A("UP"), OP.subtract)
+    vts(A("EX"), A("XM"), -1024.0, OP.mult, 1.0, OP.add)
+    eat = [sum(p[1] * p[1] // 16 for p in PART[:k]) for k in range(len(PART))]
+    for e, (l0, n, p, row) in zip(eat, PART):
+        iota(A("EM", e, e + n * n // 16), [[0, n * n // 16]], 1, 0)
+        iota(A("E", e, e + n * n // 16), [[0, n * n // 16]], 0, 0)
+        for y in range(n // 16):
+            gcp(A("EM", e + (n + 16) * y, e + (n + 16) * y + 16), A("EX"), 16)
+        iota(A("EM", e, e + n * n // 16, n), [[0, n // 16]], 0, 0)
     vts(A("OCH"), A("OCN"), -2048.0, OP.add)
+    vcp(A("CU", 0, 256), A("CI", 0, 256))
+    banks = (("P6", 0), ("P7", 0), ("TA", 0), ("TA", 512), ("TB", 0), ("TB", 512), ("P4", 0), ("P5", 0))
     for k in range(8):
-        ps, c = (("P6", 0), ("P7", 0), ("TA", 0), ("TA", 512), ("TB", 0), ("TB", 512), ("P4", 0), ("P6", 0))[k]
+        ps, c = banks[k]
         for h in range(2):
             x = 2 * k + h
             mm(A(ps, c + 256 * h, c + 256 * h + 256), A("PX", 128 * x, 128 * x + 128), A("OCH"))
+        o = A("OO", 512 + 512 * k, 1024 + 512 * k)
         if k % 2 == 0:
-            vcp(A("OH", 512 * k, 512 * k + 512), A(ps, c, c + 512))
+            vts(o, A(ps, c, c + 512), 2080.0, OP.add)
         else:
-            act(A("OH", 512 * k, 512 * k + 512), A(ps, c, c + 512), FN.Copy)
-    collect(A("P5", 0, 256), "Z0", lambda x: A("OH", x, 4096, 16))
-    vts(A("CF"), A("CI"), -2048.0, OP.add)
-    vcp(A("Z15", 15, 143, 16), A("G15"))
-    collect(A("P7", 0, 64), "Z0", lambda x: A("CF", x, 1024, 16))
-    collect(A("P7", 64, 128), "Z15", lambda x: A("CF", x, 1024, 16))
-    vcp(A("CU"), A("CI"))
-    vts(A("OLU"), A("P5", 0, 256), 2048.0, OP.add)
-    vts(A("KD", 0, 16), A("LY"), A("XC"), OP.add)
-    vts(A("KD", 16, 32), A("KD", 0, 16), 256.0, OP.add)
-    vts(A("KM"), A("KD", 0, 16), 256.0, OP.add)
-    vcp(A("ZB", 15, 143, 16), A("B", 0, 128, 16))
-    vts(A("BB"), A("B"), 1048576.0, OP.mult)
-    vts(A("ZH"), A("ZB"), 0.5, OP.mult)
-    vts(A("NI"), A("I"), -1.0, OP.mult)
-    vts(A("UM"), A("UP"), -1.0, OP.mult)
-    sel(A("W3"), A("UM"), [[-1, 128]], OP.not_equal, 1000.0, 0, 1)
-    vts(A("LS"), A("P7", 0, 128), 2048.0, OP.add)
-    vts(A("KS"), A("LS", 0, 64), 512.0, OP.add)
-    vts(A("NN"), A("ND"), -1024.0, OP.mult)
-    vms(A("SK", 4095, 4096), -14.0 / 1024)
-    for k in range(8):
-        o, i = A("WA", 512 + 512 * k, 1024 + 512 * k), ind(A("SK"), A("OLU", 32 * k, 32 * k + 32))
+            act(o, A(ps, c, c + 512), FN.Identity, 2080.0)
+    for k in range(4):
+        o, i = A("WHO", 1024 * k, 1024 * k + 1024), ind(A("OO", 512, 4608), A("CU", 64 * k, 64 * k + 64))
         if k % 2 == 0:
-            vts(o, i, 1024.0, OP.mult, float(K0), OP.add)
+            vts(o, i, -2080.0, OP.add)
         else:
-            act(o, i, FN.Identity, float(K0), 1024.0)
+            act(o, i, FN.Identity, -2080.0)
+    for k in range(4):
+        collect(A("P%d" % (4 + k), 0, 64), "Z0", lambda x: A("WHO", 1024 * k + x - 1, 1024 * k + 1024, 16), 1)
+        vts(A("OLU", 64 * k, 64 * k + 64), A("P%d" % (4 + k), 0, 64), A("SC", 0, 1), OP.add)
+    for h in range(2):
+        collect(A("TB", 512 * h, 512 * h + 8), "Z0", lambda x: A("WHO", 2048 * h + 16 * x + 15, 2048 * h + 2048, 256))
+        vts(A("OL0", 16 + 8 * h, 24 + 8 * h), A("TB", 512 * h, 512 * h + 8), 2048.0, OP.add)
+    collect(A("TB", 512, 528), "Z0", lambda x: A("WHO", 16 * x, 4096, 256))
+    vts(A("OL0", 0, 16), A("TB", 512, 528), 2048.0, OP.add)
+    vms(A("SK", 4095, 4096), -MARK / 16)
+
+    def cards(t):
+        a, b = 256 * t, 256 * t + 256
+        act(A("CF", a, b), A("CI", a, b), FN.Identity, -2048.0)
+        collect(A("P7", 256, 272), "Z0", lambda x: A("CF", a + x, b, 16))
+        if t:
+            collect(A("P7", 272, 288), "Z15", lambda x: A("CF", a + x, b, 16))
+            mm(A("P7", 0, 256), A("SH"), A("CF", a, b))
+            vts(A("CU", a, b), A("CF", a, b), 2048.0, OP.add)
+            vts(A("CS", a, b), A("P7", 0, 256), A("SC", 0, 1), OP.add)
+            vts(A("LS", 32 * t, 32 * t + 32), A("P7", 256, 288), 2048.0, OP.add)
+        else:
+            vts(A("LS", 0, 16), A("P7", 256, 272), 2048.0, OP.add)
+        act(A("KS", 16 * t, 16 * t + 16), A("P7", 256, 272), FN.Identity, 2560.0)
 
     def covers(t):
         f, u = "CLF%d" % (t % 2), "CLU%d" % (t % 2)
-        vts(A(f), ind(A("COV"), A("LS", 16 * t, 16 * t + 16)), -2048.0, OP.add)
+        act(A(f), ind(A("COV"), A("LS", 32 * t, 32 * t + 16)), FN.Identity, -2048.0)
         vts(A(u), A(f), 2048.0, OP.add)
 
-    def moved():
-        act(ind(A("OO"), A("OFS", 0, 16)), A("OV"), FN.Silu)
+    def needs(t):
+        act(A("NC", 0, 3072, 16), A("ND", 192 * t, 192 * t + 192), FN.Identity, CAP, -16.0)
 
+    needs(0)
+    cards(0)
+    covers(0)
     win = ["WA", "WB"]
+    sent = None
     for t in range(4):
         W, N = win[t % 2], win[1 - t % 2]
-        wst, nst = A(W, 512, 4608), A(N, 512, 4608)
+        wst, nst = A(W, 512, 4624), A(N, 512, 4608)
         clf, clu = "CLF%d" % (t % 2), "CLU%d" % (t % 2)
-        brep = [(A("BRF", i, VL * 16, 16), A("BT", 0, VL), VL) for i in range(16)]
-        brep += [(A("BRH", i, 4096 - VL * 16, 16), A("BS", VL, 256), 256 - VL) for i in range(16)]
 
-        def Dc(c, a, b, s=1):
-            return A("D%d" % c, a, b, s)
-
-        def own(k):
-            if k == 0:
-                act(A("BS", 256, 512), ind(wst, A("LS", 64 + 16 * t, 80 + 16 * t)), FN.Copy)
-                return
-            act(A("BS", 0, 256), ind(wst, A("LS", 16 * t, 16 * t + 16)), FN.Copy)
-            act(A("BT"), A("BS", 0, 256), FN.Identity, -float(TOL))
-
-        def gather(c, q):
-            l0, n = CH[c]
-            o, i = Dc(c, 1, 1 + 16 * n), ind(wst, A("CU", 256 * t + l0, 256 * t + l0 + n))
-            if q == "V":
-                vcp(o, i)
+        def fetch(o, lst, q):
+            if t == 0 and q == "V":
+                vts(o, ind(A("SK"), lst), 16.0, OP.mult, MARK, OP.add)
+            elif t == 0:
+                act(o, ind(A("SK"), lst), FN.Identity, MARK, 16.0)
+            elif q == "V":
+                vcp(o, ind(wst, lst))
             else:
-                act(o, i, FN.Copy)
+                act(o, ind(wst, lst), FN.Copy)
 
-        def repeat(k):
-            for j in range(k):
-                o, i, m = brep.pop(0)
-                gcp(o, i, m)
-
-        def psum(c, a, b, s=1):
-            name, off = (("TA", 0), ("TA", 512), ("TB", 0), ("TA", 0), ("TB", 0))[c]
-            return A(name, off + a, off + b, s)
-
-        def scan(c):
-            l0, n = CH[c]
-            if c < 4:
-                vcp(Dc(c, 0, 16 * n, 16), A("NN", 192 * t + l0, 192 * t + l0 + n))
-            elif t:
-                ev = ("arr%d" % (t - 1), len(topo.engines(T.cores[rank - 1], core)))
-                record("net", ev, [], [A("AV%d" % (t - 1))])
-                vts(Dc(4, 0, 1024, 16), A("AV%d" % (t - 1)), -1024.0, OP.mult)
-                vts(A("NA"), A("AV%d" % (t - 1)), -1024.0, OP.mult)
-            else:
-                vms(Dc(4, 0, 1024, 16), 0.0)
-            r = A("R", 16 * l0, 16 * l0 + 16 * n) if c < 4 else A("RF")
-            scan_(r, A("DM", 0, 16 * n), Dc(c, 0, 16 * n), 0.0)
-            vts(A("IN1", 16 * l0, 16 * l0 + 16 * n), r, -512.0, OP.is_ge, -15.5 / 16, OP.add)
-            for k in range(n // 32):
-                mm(psum(c, 512 * k, 512 * k + 512), A("BB"), A("IN1", 16 * l0 + 512 * k, 16 * l0 + 512 * k + 512))
-
-        def total(c):
-            l0, n = CH[c]
-            if t < 3:
-                for p in range(16):
-                    mm(A("P4", l0, l0 + n), A("I"), Dc(c, p, 16 * n, 16), p == 0, False)
-                mm(A("P4", l0, l0 + n), A("I"), A("BS", 256 + l0, 256 + l0 + n), False, True)
-
-        def leave(c):
-            l0, n = CH[c]
-            vtt(A("X", 16 * l0, 16 * l0 + 16 * n), Dc(c, 1, 1 + 16 * n), psum(c, 0, 16 * n), OP.min)
-            vtt(A("X", 16 * l0 + 15, 16 * l0 + 16 * n, 16), A("BS", 256 + l0, 256 + l0 + n), psum(c, 15, 16 * n, 16), OP.min)
+        if t == 3:
+            dma(T.OFN[:, :], T.OO[0:128:16, 512:4608], [A("OO", 512, 4608)], [A("OFN")], 2.6)
+            vts(A("OI"), A("OFN"), -32.0, OP.add)
+        lst, at = ("LS", 32 * t) if t else ("OL0", 0)
+        for h in range(2):
+            fetch(A("BS", 256 + 128 * h, 384 + 128 * h), A(lst, at + 16 + 8 * h, at + 24 + 8 * h), "S")
+        fetch(A("BS", 0, 256), A(lst, at, at + 16), "S")
+        act(A("BT"), A("BS", 0, 256), FN.Relu, -8.0)
+        for i in range(16):
+            gcp(A("BRF", i, VL * 16, 16), A("BT", 0, VL), VL)
+        if t:
+            av = A("AV%d" % (t - 1))
+            emit("N", ("arr%d" % (t - 1), len(topo.engines(T.cores[rank - 1], core))), [], [av], 0.0, 0.0, "arrival", [sent])
+            vts(A("NC", 3072, 4096, 16), av, -16.0, OP.mult)
+        for c, (l0, n, q, ps, off) in enumerate(CH):
+            d = 16 * (l0 + c)
+            fetch(A("D", d, d + 16 * n), A("CS", 256 * t + l0, 256 * t + l0 + n) if t else A("OLU", l0, l0 + n), q)
+            halves = [(a, min(32, n - a)) for a in range(0, n, 32)]
+            for a, m in halves:
+                mm(A(ps, off + 16 * a, off + 16 * (a + m)), A("CB"), A("PAT", 0, 16 * m), True, False)
+            scan_(A("R", 16 * l0, 16 * (l0 + n)), A("D", d, d + 16 * n), A("NC", 16 * l0, 16 * (l0 + n)), 0.0, OP.add, OP.min)
+            for a, m in halves:
+                mm(A(ps, off + 16 * a, off + 16 * (a + m)), A("BB"), A("R", 16 * (l0 + a), 16 * (l0 + a + m)), False, False)
+                mm(A(ps, off + 16 * a + 15, off + 16 * (a + m), 16), A("I"), A("BS", 256 + l0 + a, 256 + l0 + a + m), False, True)
+            vtt(A("X", 16 * l0, 16 * l0 + 16 * n), A("D", d + 1, d + 1 + 16 * n), A(ps, off, off + 16 * n), OP.add)
             act(ind(nst, A("CU", 256 * t + l0, 256 * t + l0 + n)), A("X", 16 * l0, 16 * l0 + 16 * n), FN.Silu)
-
-        def lost(k):
-            if k == 0:
-                collect(A("P5", 256, 268), "ZB", lambda x: A("NN", 192 * t + x, 192 * t + 192, 16))
-                collect(A("P5", 272, 288), "ZB", lambda x: A("BS", x, 256, 16))
-            else:
-                collect(A("P5", 268, 272), "ZB", lambda x: A("NA", x, 64, 16))
-
-        def rest(c):
-            if t < 3:
-                vtt(A("AR"), A("RF", 15, 1024, 16), A("BS", 448, 512), OP.add)
-                vts(A("RR", 192, 256), A("AR"), -1.0 / 1024, OP.mult, 0.0, OP.max)
-
-        def rest2(c):
-            if t < 3:
-                vts(A("RR", 0, 192), A("P4", 0, 192), -1.0 / 1024, OP.mult, 0.0, OP.max)
-                vts(A("U01"), A("RR"), 0.5, OP.is_gt)
-
-        def run(order, do):
-            for step in order.split():
-                together([(lambda s=s: do[s[0]](int(s[1:]))) for s in step.split("+")])
-
-        run(STEP1, {"v": lambda c: gather(c, "V"), "a": lambda c: gather(c, "S"), "b": own, "r": repeat, "s": scan, "t": total,
-                    "l": leave, "q": lost, "x": rest, "y": rest2})
-        if t == 0:
-            covers(0)
-
-        def unmet(c):
-            if t < 3:
-                collect(A("P5", 0, 16), "ZB", lambda x: A("U01", x, 256, 16))
-
-        def lost2(c):
-            vts(A("L1"), A("P5", 256, 272), -512.0, OP.is_lt)
-            vts(A("L2"), A("P5", 272, 288), float(TOL), OP.is_ge)
-            vtt(A("LOST"), A("L1"), A("L2"), OP.mult)
-
-        def slots(c):
-            if t < 3:
-                vts(A("UL"), A("P5", 0, 16), 0.5, OP.is_ge)
-                vts(A("UK"), A("P5", 0, 16), 0.5, OP.is_lt)
-                mm(A("P5", 16, 32), A("B"), A("UL"))
-                mm(A("P5", 32, 48), A("W3"), A("UL"))
-
-        def slots2(c):
-            if t < 3:
-                vtt(A("UK2"), A("UK"), A("KM"), OP.mult)
-                scan_(A("CY"), A("ON16"), A("P5", 16, 32), -1001.0)
-                vtt(A("SP"), A("P5", 32, 48), A("CY"), OP.add)
-                vtt(A("OF"), A("SP"), A("UK2"), OP.max)
-                vcp(A("OU"), A("OF"))
-
-        def slots3(c):
-            if t < 3:
-                vcp(ind(A("SW%d" % t), A("OU")), A("RR"))
-
-        def spsum(k):
-            return A(*(("TA", 0, 512), ("TA", 512, 1024), ("TB", 0, 16 * SG3[2][1]))[k])
-
-        def sgather(k):
-            l0, n = SG3[k]
-            ga, br = A("GA", 16 * (l0 - VL), 16 * (l0 - VL + n)), A("BRH", 16 * (l0 - VL), 16 * (l0 - VL + n))
-            act(ga, ind(nst, A(clu, l0, l0 + n)), FN.Copy)
-            mm(spsum(k), A("NI"), br, True, False)
-            mm(spsum(k), A("I"), ga, False, True)
-
-        def ssign(k):
-            l0, n = SG3[k]
-            act(A("SGN", 16 * (l0 - VL), 16 * (l0 - VL + n)), spsum(k), FN.Sign, float(TOL))
-
-        def fused(k):
-            l0, n = FG[k]
-            vtt(A("IN3", 16 * l0, 16 * (l0 + n)), ind(nst, A(clu, l0, l0 + n)), A("BRF", 16 * l0, 16 * (l0 + n)), OP.is_ge)
-
-        def counts(k):
-            for i in range(16):
-                if k == 0 or k == 3:
-                    h = 64 if k else 0
-                    mm(A("P6", h, h + 64), EX("ZB", i), A("IN3", 16 * h + i, 16 * h + 1024, 16), i == 0, i == 15)
-                elif k == 1:
-                    mm(A("P4", 0, VL - 128), EX("ZB", i), A("IN3", 2048 + i, VL * 16, 16), i == 0, False)
-                else:
-                    a, b = ((0, 64), (64, 256 - VL))[k == 4]
-                    mm(A("P4", VL - 128 + a, VL - 128 + b), EX("ZH", i), A("SGN", 16 * a + i, 16 * b, 16), i == 0, i == 15)
-            if k == 1:
-                mm(A("P4", 0, VL - 128), A("CM"), A("ONE", 0, VL - 128), False, True)
-
-        def fits(k):
-            p, l0, n = PART[k]
-            vts(A("F", l0, l0 + n), A(p, 0, n), (8.5, 0.5)[k], OP.is_ge)
-            mm(A(p, 256, 256 + n), A("TRI"), A("F", l0, l0 + n))
-
-        def first(k):
-            p, l0, n = PART[k]
-            vtt(A("SM", 256 + l0, 256 + l0 + n), A("F", l0, l0 + n), A(p, 256, 256 + n), OP.is_gt)
-            vtt(A("SM", l0, l0 + n), A("SM", 256 + l0, 256 + l0 + n), A(clf, l0, l0 + n), OP.mult)
-
-        def covers_next(c):
-            if t < 3:
-                covers(t + 1)
-
-        def moved_before(c):
-            if t:
-                moved()
-
-        run(STEP3, {"u": unmet, "g": sgather, "s": ssign, "v": fused, "c": counts, "f": fits, "o": first, "L": lost2, "p": slots,
-                    "P": slots2, "Q": slots3, "m": moved_before, "C": covers_next})
-        mm(A("P4", 0, 256), A("B"), A("SM", 0, 256))
-        collect(A("P5", 64, 96), "ZB", lambda x: A("SM", x, 512, 16))
-        act(A("CR"), A("P4", 0, 256), FN.Copy)
-        vtt(A("OKL"), A("P5", 80, 96), A("LOST"), OP.mult)
-        vts(A("MLU"), A("P5", 64, 80), 2048.0, OP.add)
-        act(A("VB", 0, 256), ind(nst, A("MLU")), FN.Copy)
-        if t == 0:
-            act(A("OO", 512, 4608), A("OH"), FN.Silu, 2080.0)
-        act(A("OV"), ind(A("OO", 512, 4608), A("MLU")), FN.Copy)
-        mm(A("P4", 0, 256), A("B"), A("ZZ"), True, False)
-        for y in range(16):
-            ey = (T.E[:, y, 0:256 - 16 * y], [("E", 256 * y, 256 * y + 256)])
-            vts(ey, A("CR", 16 * y, 256), A("P5", 64 + y, 65 + y), OP.is_equal, A("OKL", y, y + 1), OP.mult)
-            if y < 15:
-                mm(A("P4", 16 * y + 16, 256), A("B"), (T.E[:, y, 16:256 - 16 * y], ey[1]), False, False)
-        md = (T.MD[:, :, :], [("MD", 0, 16)])
-        vtt(md, (T.E[:, :, 0:16], [("E", 0, 4096)]), mk, OP.mult)
-        mm(A("P4", 0, 256), A("B"), md, False, True)
-        vts(A("OB"), A("OKL"), 8192.0, OP.mult, -8192.0, OP.add)
-        vts(A("CLM"), A("P5", 64, 80), 2560.0, OP.add)
-        vtt(A("R2", 0, 16), A("OB"), A("KS", 16 * t, 16 * t + 16), OP.add)
-        vtt(A("R2", 16, 32), A("OB"), A("CLM"), OP.add)
-        vcp(A("DL"), A("P4", 0, 256))
-        collect(A("P5", 128, 144), "Z8", lambda x: A("DL", x, 256, 16))
+        mm(A("P6", 256, 512), A("B"), A("NC", 0, 4096, 16))
+        vts(A("NL", 256, 512), A("BS", 0, 256), THR, OP.is_lt)
+        vts(A("NL", 0, 256), A("P6", 256, 512), MET, OP.is_ge)
         if t < 3:
+            mm(A("P4", 0, 256), A("I"), A("R", 15, 4096, 16), True, False)
+            mm(A("P4", 0, 256), A("I"), A("BS", 256, 512), False, True)
+            vts(A("RR"), A("P4", 0, 256), CAP, OP.min, -1.0 / 16, OP.mult)
+            collect(A("P5", 0, 16), "ZB", lambda x: A("RR", x, 256, 16))
+            vts(A("UL", 1, 17), A("P5", 0, 16), 0.5 - CAP, OP.is_gt)
+            mm(A("P5", 16, 32), A("W3"), A("UL", 1, 17), True, False)
+            mm(A("P5", 16, 32), A("UP"), A("UL", 0, 16), False, True)
+            mm(A("P5", 32, 48), A("IB"), A("UL", 1, 17), True, False)
+            mm(A("P5", 32, 48), A("I"), A("KM"), False, True)
+            scan_(A("SP"), A("ON16"), A("P5", 16, 32), -1.0)
+            vtt(A("OF"), A("SP"), A("P5", 32, 48), OP.max)
+            vcp(A("OU"), A("OF"))
+            vcp(ind(A("SW%d" % t), A("OU")), A("RR"))
             dst = T.cores[(rank + 1) % len(T.cores)]
-            addr = topo.addr(dst)
-            src = A("SW%d" % t, 0, 64)
-            waits("G", [src], [])
-            g.remote_dma(out_ap=T["AV%d" % t][:, :], in_ap=src[0], remote_sem=T.sem["arr%d" % t], local_sem=T.sem["loc%d" % t],
-                         pid=addr[1], routing_id=addr[0], dma_engine_mask=topo.mask(core, dst))
-        vtt(A("R3", 0, 16), A("P5", 128, 144), A("R2", 0, 16), OP.add)
-        vtt(A("R3", 16, 32), A("P5", 128, 144), A("R2", 16, 32), OP.add)
-        vtt(A("R4"), A("R3"), A("KD"), OP.max)
-        vcp(A("OFS"), A("R4"))
-        vcp(ind(A(N), A("OFS")), A("VB"))
-    moved()
-    dma("Y", T.ZF[:, :], T.WA[0:128:16, 512:4608], [A("WA", 512, 4608)], [A("ZF")])
-    dma("Y", T.OFN[:, :], T.OO[0:128:16, 512:4608], [A("OO", 512, 4608)], [A("OFN")])
-    vts(A("EF"), A("ZF"), float(TOL), OP.is_lt, 4095.0, OP.mult)
-    vts(A("OI"), A("OFN"), -32.0, OP.add)
-    vtt(A("YF"), A("OI"), A("EF"), OP.max)
-    need_event("Y", dma("Y", T.y[:, :], T.YF[:, :], [A("YF")], []))
+            rid, pid = topo.addr(dst)[:2]
+            sent = emit("G", lambda t=t, dst=dst, rid=rid, pid=pid: g.remote_dma(
+                out_ap=T["AV%d" % t][:, :], in_ap=T["SW%d" % t][:, 0:64], remote_sem=T.sem["arr%d" % t], local_sem=T.sem["loc%d" % t],
+                pid=pid, routing_id=rid, dma_engine_mask=topo.mask(core, dst)), [A("SW%d" % t, 0, 64)], [], 1.0, 6.0, "remote")
+        else:
+            dma(T.ZF[:, :], T[N][0:128:16, 512:4608], [nst], [A("ZF")], 2.6)
+            vts(A("EF"), A("ZF"), THR, OP.is_lt, 4095.0, OP.mult)
+            vtt(A("YF"), A("OI"), A("EF"), OP.max)
+            dma(T.YR[0:128:16, 512:4608], T.YF[:, :], [A("YF")], [A("YR")], 2.6)
+            for l0, n, p, row in PART:
+                iota(A("VB", 2 * l0 + n, 2 * l0 + 2 * n), [[0, n]], 4095, 0)
+
+        for l0, n in FG:
+            vtt(A("IN3", 16 * l0, 16 * (l0 + n)), ind(nst, A(clu, l0, l0 + n)), A("BRF", 16 * l0, 16 * (l0 + n)), OP.is_gt)
+        for l0, n, ps, off in SG3:
+            mm(A(ps, off, off + 16 * n), A("I"), A("ZZ", 0, 16 * n), True, False)
+            for i in range(16):
+                mm(A(ps, off + i, off + 16 * n, 16), A("NI"), A("BT", l0, l0 + n), False, False)
+            ga = A("GA", 16 * (l0 - VL), 16 * (l0 - VL + n))
+            act(ga, ind(nst, A(clu, l0, l0 + n)), FN.Copy)
+            mm(A(ps, off, off + 16 * n), A("I"), ga, False, True)
+            act(A("IN3", 16 * l0, 16 * (l0 + n)), A(ps, off, off + 16 * n), FN.Sign, -THR)
+        for e, (l0, n, p, row) in zip(eat, PART):
+            y0, ny = l0 // 16, n // 16
+            mm(A(p, 0, n), A("I"), A("OFFS", l0, l0 + n), True, False)
+            mm(A(p, 0, n), A("IB"), A("NL", l0, l0 + n), False, False)
+            mm(A(p, 0, n), A("IB"), A("NL", 256 + l0, 256 + l0 + n), False, False)
+            for a, m in CNT:
+                for i in range(16):
+                    if l0 <= a < l0 + n:
+                        mm(A(p, a - l0, a - l0 + m), EX("ZB" if a < VL else "ZH", i), A("IN3", 16 * a + i, 16 * (a + m), 16), False, i == 15 and a + m == l0 + n)
+            f = A("FC", 2 * l0 + n, 2 * l0 + 2 * n)
+            vts(f, A(p, 0, n), 0.5, OP.is_ge, 8192.0, OP.mult)
+            mm(A(p, 256, 256 + n), A("TRI"), f)
+            vtt(A("SM", l0, l0 + n), f, A(p, 256, 256 + n), OP.is_gt)
+            vtt(A("FC", 2 * l0, 2 * l0 + n), A("SM", l0, l0 + n), A(clf, l0, l0 + n), OP.mult)
+            mm(A(row, 0, n), A("BH"), A("SM", l0, l0 + n), True, False)
+            mm(A(row, 0, n), A("B"), A("FC", 2 * l0, 2 * l0 + n), False, True)
+            collect(A(p, 448, 448 + 2 * ny), "ZB", lambda x: A("FC", 2 * l0 + x, 2 * l0 + 2 * n, 16))
+            act(A("CR", l0, l0 + n), A(row, 0, n), FN.Identity, 0.5)
+            mlu = A("MLU", y0, y0 + ny)
+            vts(mlu, A(p, 448, 448 + ny), 2048.0, OP.add)
+            vts(A("VC", y0, y0 + ny), A(p, 448, 448 + ny), 2560.0, OP.add)
+            ok = A(p, 448 + ny, 448 + 2 * ny)
+            vtt(A("VAL", 2 * y0, 2 * y0 + ny), A("KS", 16 * t + y0, 16 * t + y0 + ny), ok, OP.min)
+            vtt(A("VAL", 2 * y0 + ny, 2 * y0 + 2 * ny), A("VC", y0, y0 + ny), ok, OP.min)
+            for y in range(ny):
+                vts(A("E", e + n * y, e + n * y + 16 * y + 16), A("CR", l0, l0 + 16 * y + 16), A(p, 448 + y, 449 + y), OP.is_equal, 8192.0, OP.mult)
+            scan_(A("EZ", e, e + n * ny), A("EM", e, e + n * ny), A("E", e, e + n * ny), 0.0)
+            for h in range(2):
+                vtt(A("R3", 2 * y0 + h * ny, 2 * y0 + h * ny + ny), A("VAL", 2 * y0 + h * ny, 2 * y0 + h * ny + ny), A("EZ", e + n - 1, e + n * ny, n), OP.min)
+            vtt(A("R4", 2 * y0, 2 * y0 + 2 * ny), A("R3", 2 * y0, 2 * y0 + 2 * ny), A("KD", 2 * y0, 2 * y0 + 2 * ny), OP.max)
+            vcp(A("OFS", 2 * y0, 2 * y0 + 2 * ny), A("R4", 2 * y0, 2 * y0 + 2 * ny))
+            src = N if t < 3 else "YR"
+            act(A("VB", 2 * l0, 2 * l0 + n), ind(A(src, 512, 4608), mlu), FN.Copy)
+            vcp(ind(A(src, 0, 4608), A("OFS", 2 * y0, 2 * y0 + 2 * ny)), A("VB", 2 * l0, 2 * l0 + 2 * n))
+        if t < 3:
+            act(A("OV"), ind(A("OO", 512, 4608), A("MLU")), FN.Copy)
+            for l0, n, p, row in PART:
+                act(ind(A("OO"), A("OFS", l0 // 8, l0 // 8 + n // 16)), A("OV", l0, l0 + n), FN.Silu)
+            cards(t + 1)
+            covers(t + 1)
+            needs(t + 1)
+    dma(T.y[:, :], T.YR[0:128:16, 512:4608], [A("YR")], [], 2.6)
+    issue()
     for t in range(3):
         g.wait_ge(T.sem["loc%d" % t], len(topo.engines(core, T.cores[(rank + 1) % len(T.cores)])))
-    for s in ("cV", "cS", "cT", "cG"):
-        need_event("G", (s, count[s]))

@@ -2,18 +2,17 @@ from concourse.mybir import AluOpType, ActivationFunctionType
 
 OP = AluOpType
 FN = ActivationFunctionType
-MARK, THR, CAP = 7.0 / 64, 1.0 / 512, 32768.0
+MARK, THR, CAP = 15.0 / 64, 1.0 / 2048, 32768.0
 MET = 16 * CAP - 8
-CH = [(0, 16, "V", "TA", 0), (16, 32, "S", "TA", 512), (48, 32, "V", "TB", 0), (80, 48, "V", "TA", 0), (128, 64, "V", "TB", 0),
-      (192, 32, "V", "TA", 0), (224, 32, "V", "TA", 512)]
-VL = 128
-FG = [(0, 64), (64, 64)]
-SG3 = [(128, 32, "TA", 0), (160, 32, "TA", 512), (192, 32, "TB", 0), (224, 32, "TB", 512)]
-CNT = [(0, 64), (64, 64), (128, 64), (192, 64)]
+CH = [(0, 16, "V", "TA", 0), (16, 32, "S", "TA", 512), (48, 16, "V", "TA", 0)] + [(l, 32, "V", "TA", 512 - 16 * l % 1024) for l in range(64, 256, 32)]
+VL = 144
+FG = [(0, 64), (64, 64), (128, 16)]
+SG3 = [(144, 32, "TB", 0), (176, 32, "TB", 512), (208, 32, "TA", 0), (240, 16, "TA", 512)]
+CNT = [(0, 64), (64, 64), (128, 16), (144, 64), (208, 48)]
 PART = [(0, 128, "P6", "P7"), (128, 128, "P4", "P5")]
 CYC, CALL, HOP, PE, GATHER, SCATTER = 0.00083, 0.03, 0.11, 0.00042, 1.56, 3.0
-PW = max(p[1] for p in PART)
-EN = sum(p[1] * p[1] // 16 for p in PART)
+PASSES = 3
+EN = sum((p[1] + 2) * p[1] // 16 for p in PART)
 
 _sb = {
     "OLU": (256, "uint16"), "OCN": (256, "int32"), "OCH": (256, "float16"), "WHO": (4096, "float16"), "OL0": (32, "uint16"),
@@ -26,12 +25,12 @@ _sb = {
     "TRI": (128, "bfloat16"), "UP": (128, "bfloat16"), "UN": (128, "bfloat16"), "W3": (128, "bfloat16"), "IB": (128, "bfloat16"),
     "PI": (1, "int32"), "PA": (1, "int32"), "XC": (1, "float32"), "SC": (2, "float32"), "ZR": (16, "float32"), "XM": (16, "float32"), "LY": (32, "float32"),
     "KM": (16, "float16"), "KD": (32, "float32"), "ON16": (16, "float32"), "ZZ": (512, "bfloat16"), "OFFS": (256, "bfloat16"),
-    "D": (4096 + 16 * len(CH), "bfloat16"), "NC": (4096, "float16"), "R": (4096, "float16"),
+    "D": (4112, "bfloat16"), "NC": (4096, "float16"), "R": (4096, "float16"),
     "X": (4096, "float32"), "RR": (256, "float16"), "UL": (17, "bfloat16"), "SP": (16, "float32"), "OF": (16, "float32"), "OU": (16, "uint16"),
     "BS": (512, "bfloat16"), "BT": (256, "float16"), "BRF": (VL * 16, "float16"), "NL": (512, "bfloat16"),
     "CLF0": (256, "float16"), "CLU0": (256, "uint16"), "CLF1": (256, "float16"), "CLU1": (256, "uint16"),
     "IN3": (4096, "bfloat16"), "GA": (4096 - VL * 16, "bfloat16"),
-    "SM": (256, "bfloat16"), "FC": (512, "float16"), "CR": (256, "float16"), "VC": (16, "float32"), "VAL": (32, "float32"),
+    "SM": (256, "bfloat16"), "FC": (512, "float16"), "CR": (256, "float16"), "B8": (128, "bfloat16"),
     "E": (EN, "bfloat16"), "EM": (EN, "bfloat16"), "EZ": (EN, "bfloat16"), "EX": (16, "bfloat16"),
     "R3": (32, "float32"), "R4": (32, "float32"), "OFS": (32, "uint16"), "MLU": (16, "uint16"),
     "VB": (512, "float32"), "OV": (256, "float32"),
@@ -51,23 +50,49 @@ SEMAPHORES = ["cV", "cS", "cT", "cG"] + ["arr%d" % t for t in range(3)] + ["loc%
 
 def issue_order(calls):
     n = len(calls)
-    way = [0.0] * n
-    for k in range(n - 1, -1, -1):
-        way[k] += calls[k]["cost"] + calls[k]["lag"]
-        for p, hop in calls[k]["after"].items():
-            way[p] = max(way[p], way[k] + hop)
-    start, done, busy = [0.0] * n, [0.0] * n, {}
-    for k in sorted(range(n), key=lambda j: (-way[j], j)):
-        c = calls[k]
-        at = max([done[p] + hop for p, hop in c["after"].items()] + [0.0])
-        slots = busy.setdefault(c["q"], [])
-        i = 0
-        while i < len(slots) and slots[i][0] < at + c["cost"]:
-            at = max(at, slots[i][1])
-            i += 1
-        slots.insert(i, (at, at + c["cost"]))
-        start[k], done[k] = at, at + c["cost"] + c["lag"]
-    return sorted(range(n), key=lambda j: (start[j], j))
+    before = [[(p, calls[p]["lag"] + HOP if wait else 0.0) for p, wait in c["after"].items()] for c in calls]
+    behind = [[] for c in calls]
+    for k in range(n):
+        for p, hop in before[k]:
+            behind[p].append((k, hop))
+
+    def place(rank, links, onward, backwards):
+        end, left, ready, free = [0.0] * n, [len(x) for x in links], {}, {}
+        can = [c["lag"] if backwards else 0.0 for c in calls]
+        for k in range(n):
+            if not left[k]:
+                ready.setdefault(calls[k]["q"], []).append(k)
+        for step in range(n):
+            soon, q = min((max(free.get(q, 0.0), can[k]) + calls[k]["cost"], q) for q in ready for k in ready[q])
+            at = free.get(q, 0.0)
+            rivals = [k for k in ready[q] if max(at, can[k]) < soon or max(at, can[k]) + calls[k]["cost"] <= soon]
+            k = max(rivals, key=lambda j: (rank[j], -j))
+            ready[q].remove(k)
+            end[k] = free[q] = max(at, can[k]) + calls[k]["cost"]
+            for s, hop in onward[k]:
+                can[s] = max(can[s], end[k] + hop)
+                left[s] -= 1
+                if not left[s]:
+                    ready.setdefault(calls[s]["q"], []).append(s)
+        return end
+
+    way, left = [0.0] * n, [len(x) for x in behind]
+    todo = [k for k in range(n) if not left[k]]
+    for k in todo:
+        way[k] = calls[k]["cost"] + max([way[s] + hop for s, hop in behind[k]] + [calls[k]["lag"]])
+        for p, hop in before[k]:
+            left[p] -= 1
+            if not left[p]:
+                todo.append(p)
+    best = None
+    for turn in range(PASSES):
+        end = place(way, before, behind, False)
+        span = max(end[k] + calls[k]["lag"] for k in range(n))
+        if best is None or span < best[0]:
+            best = (span, end)
+        way = place(end, behind, before, True)
+    end = best[1]
+    return sorted(range(n), key=lambda j: (end[j] - calls[j]["cost"], j))
 
 
 def rank_program(g, core, T, topo):
@@ -96,7 +121,7 @@ def rank_program(g, core, T, topo):
         return x >= b or y <= a or (s == z and s > 1 and (a - x) % s != 0)
 
     def emit(q, fn, reads, writes, cost, lag=0.0, kind="compute", after=()):
-        me, dep = len(calls), {p: HOP for p in after}
+        me, dep = len(calls), {p: True for p in after}
         for ops, w in ((reads, False), (writes, True)):
             for o in ops:
                 for region in o[1]:
@@ -106,15 +131,15 @@ def rank_program(g, core, T, topo):
                             x, y, z, p, pq, pw = r
                             if p != me and not apart(lo, hi, st, x, y, z) and (pw or w or (bank and pq != q)):
                                 if bank and pq == q == "T":
-                                    dep.setdefault(p, 0.0)
+                                    dep.setdefault(p, False)
                                 else:
-                                    dep[p] = HOP
+                                    dep[p] = True
                                 if w and lo <= x and y <= hi and (st == 1 or st == z):
                                     continue
                             keep.append(r)
                         keep.append((lo, hi, st, me, q, w))
                         log[key] = keep
-        calls.append({"q": q, "fn": fn, "after": dep, "cost": cost, "lag": lag, "kind": kind})
+        calls.append({"name": writes[0][1][0][0] if writes else "", "q": q, "fn": fn, "after": dep, "cost": cost, "lag": lag, "kind": kind})
         return me
 
     def issue():
@@ -199,8 +224,12 @@ def rank_program(g, core, T, topo):
         else:
             emit("S", lambda: S.activation(out[0], i[0], fn, bias=bias, scale=scale), [i], [out], cost(out, [i], 1.0) + more)
 
+    def mms(group):
+        emit("T", lambda: [TE.matmul(o[0], l[0], r[0], start, stop) for o, l, r, start, stop in group][-1],
+             [x for m in group for x in m[1:3]], [m[0] for m in group], sum(0.005 + max(64, m[2][2]) * PE for m in group))
+
     def mm(out, l, r, start=True, stop=True):
-        emit("T", lambda: TE.matmul(out[0], l[0], r[0], start, stop), [l, r], [out], 0.005 + max(64, r[2]) * PE)
+        mms([(out, l, r, start, stop)])
 
     def sel(out, i, pattern, op, fill, base, mult):
         emit("G", lambda: g.affine_select(out[0], i[0], pattern, op, fill, base, mult), [i], [out], 0.17 + 2 * out[2] * CYC)
@@ -218,8 +247,7 @@ def rank_program(g, core, T, topo):
         return A(name, 15 - x, 143 - x)
 
     def collect(out, name, rhs, first=0):
-        for x in range(first, 16):
-            mm(out, EX(name, x), rhs(x), x == first, x == 15)
+        mms([(out, EX(name, x), rhs(x), x == first, x == 15) for x in range(first, 16)])
 
     d0 = dma(T.OCN[:, :], T.occ[:, :], [], [A("OCN")], 2.6)
     d1 = dma(T.CI[:, 0:256], T.cards[:, 0:256], [], [A("CI", 0, 256)], 3.2)
@@ -228,7 +256,7 @@ def rank_program(g, core, T, topo):
     d4 = dma(T.COV[:, :], T.cover[:, :], [], [A("COV")], 12.5, [d2])
     d5 = dma(T.CI[:, 256:1024], T.cards[:, 256:1024], [], [A("CI", 256, 1024)], 14.5, [d2])
     for a, b in ((d0, d1), (d1, d2), (d2, d3), (d3, d4), (d4, d5)):
-        calls[b]["after"].setdefault(a, -calls[a]["lag"])
+        calls[b]["after"].setdefault(a, False)
 
     vms(A("ONE"), 1.0)
     iota(A("PI"), [[0, 1]], 0, 1, False)
@@ -243,7 +271,7 @@ def rank_program(g, core, T, topo):
     for z in ("Z0", "ZB", "Z15"):
         vms(A(z), 0.0)
     vts(A("PA"), A("PI"), 15, OP.bitwise_and)
-    vms(A("D", 0, None, 16), 2 * CAP)
+    vms(A("D", 4096, 4112), 2 * CAP)
     vcp(A("XC"), A("PA"))
     vms(A("SK", 4096, 4112), CAP / 8)
     vts(A("XM"), A("ZR"), A("XC"), OP.is_equal)
@@ -277,21 +305,26 @@ def rank_program(g, core, T, topo):
     vtt(A("CB"), A("CB"), A("S1"), OP.add)
     vcp(A("ZB", 15, 143, 16), A("B", 0, 128, 16))
     vcp(A("Z15", 15, 143, 16), A("G15"))
-    vts(A("KD"), A("LY"), A("XC"), OP.add)
+    vts(A("KD"), A("LY"), A("XC"), OP.add, -2560.0, OP.add)
     vts(A("ZH"), A("ZB"), 0.5, OP.mult)
     vts(A("BH"), A("B"), -0.5, OP.mult)
-    vts(A("KM"), A("KD", 0, 16), 256.0, OP.add)
+    vts(A("KM"), A("KD", 0, 16), 2816.0, OP.add)
+    vts(A("TRI"), A("TRI"), 16.0, OP.mult)
+    vts(A("B8"), A("B"), -0.125, OP.mult)
     vts(A("NI"), A("I"), -1.0, OP.mult)
     vts(A("IB"), A("I"), -2048.0, OP.mult)
     vtt(A("W3"), A("B"), A("UP"), OP.subtract)
     vts(A("EX"), A("XM"), -1024.0, OP.mult, 1.0, OP.add)
-    eat = [sum(p[1] * p[1] // 16 for p in PART[:k]) for k in range(len(PART))]
+    eat = [sum((p[1] + 2) * p[1] // 16 for p in PART[:k]) for k in range(len(PART))]
     for e, (l0, n, p, row) in zip(eat, PART):
-        iota(A("EM", e, e + n * n // 16), [[0, n * n // 16]], 1, 0)
-        iota(A("E", e, e + n * n // 16), [[0, n * n // 16]], 0, 0)
-        for y in range(n // 16):
-            gcp(A("EM", e + (n + 16) * y, e + (n + 16) * y + 16), A("EX"), 16)
-        iota(A("EM", e, e + n * n // 16, n), [[0, n // 16]], 0, 0)
+        w, ny = n + 2, n // 16
+        iota(A("EM", e, e + w * ny), [[0, w * ny]], 1, 0)
+        iota(A("E", e, e + w * ny), [[0, w * ny]], 0, 0)
+        for y in range(ny):
+            gcp(A("EM", e + (w + 16) * y, e + (w + 16) * y + 16), A("EX"), 16)
+        iota(A("EM", e, e + w * ny, w), [[0, ny]], 0, 0)
+        iota(A("EM", e + n, e + w * ny, w), [[0, ny]], 8192, 0)
+        iota(A("E", e + n, e + w * ny, w), [[0, ny]], -4096, 0)
     vts(A("OCH"), A("OCN"), -2048.0, OP.add)
     vcp(A("CU", 0, 256), A("CI", 0, 256))
     banks = (("P6", 0), ("P7", 0), ("TA", 0), ("TA", 512), ("TB", 0), ("TB", 512), ("P4", 0), ("P5", 0))
@@ -317,8 +350,6 @@ def rank_program(g, core, T, topo):
     for h in range(2):
         collect(A("TB", 512 * h, 512 * h + 8), "Z0", lambda x: A("WHO", 2048 * h + 16 * x + 15, 2048 * h + 2048, 256))
         vts(A("OL0", 16 + 8 * h, 24 + 8 * h), A("TB", 512 * h, 512 * h + 8), 2048.0, OP.add)
-    collect(A("TB", 512, 528), "Z0", lambda x: A("WHO", 16 * x, 4096, 256))
-    vts(A("OL0", 0, 16), A("TB", 512, 528), 2048.0, OP.add)
     vms(A("SK", 4095, 4096), -MARK / 16)
 
     def cards(t):
@@ -333,7 +364,7 @@ def rank_program(g, core, T, topo):
             vts(A("LS", 32 * t, 32 * t + 32), A("P7", 256, 288), 2048.0, OP.add)
         else:
             vts(A("LS", 0, 16), A("P7", 256, 272), 2048.0, OP.add)
-        act(A("KS", 16 * t, 16 * t + 16), A("P7", 256, 272), FN.Identity, 2560.0)
+        act(A("KS", 16 * t, 16 * t + 16), A("P7", 256, 272), FN.Copy)
 
     def covers(t):
         f, u = "CLF%d" % (t % 2), "CLU%d" % (t % 2)
@@ -366,42 +397,61 @@ def rank_program(g, core, T, topo):
         if t == 3:
             dma(T.OFN[:, :], T.OO[0:128:16, 512:4608], [A("OO", 512, 4608)], [A("OFN")], 2.6)
             vts(A("OI"), A("OFN"), -32.0, OP.add)
+        else:
+            cards(t + 1)
+            covers(t + 1)
         lst, at = ("LS", 32 * t) if t else ("OL0", 0)
         for h in range(2):
             fetch(A("BS", 256 + 128 * h, 384 + 128 * h), A(lst, at + 16 + 8 * h, at + 24 + 8 * h), "S")
-        fetch(A("BS", 0, 256), A(lst, at, at + 16), "S")
-        act(A("BT"), A("BS", 0, 256), FN.Relu, -8.0)
-        for i in range(16):
-            gcp(A("BRF", i, VL * 16, 16), A("BT", 0, VL), VL)
         if t:
             av = A("AV%d" % (t - 1))
             emit("N", ("arr%d" % (t - 1), len(topo.engines(T.cores[rank - 1], core))), [], [av], 0.0, 0.0, "arrival", [sent])
             vts(A("NC", 3072, 4096, 16), av, -16.0, OP.mult)
+        got = []
+        for l0, n, q, ps, off in CH:
+            fetch(A("D", 16 * l0, 16 * (l0 + n)), A("CS", 256 * t + l0, 256 * t + l0 + n) if t else A("OLU", l0, l0 + n), q)
+            got.append(len(calls) - 1)
+        line = got[:1]
+        for a, b in ((0, VL), (VL, 192), (192, 256)):
+            vts(A("BT", a, b), A("D", 16 * a + 1, 16 * b, 16), -8.0, OP.add, 0.0, OP.max)
+        for i in range(16):
+            gcp(A("BRF", i, VL * 16, 16), A("BT", 0, VL), VL)
+            if i:
+                calls[-1]["after"].setdefault(len(calls) - 2, False)
         for c, (l0, n, q, ps, off) in enumerate(CH):
-            d = 16 * (l0 + c)
-            fetch(A("D", d, d + 16 * n), A("CS", 256 * t + l0, 256 * t + l0 + n) if t else A("OLU", l0, l0 + n), q)
+            d = 16 * l0
             halves = [(a, min(32, n - a)) for a in range(0, n, 32)]
             for a, m in halves:
                 mm(A(ps, off + 16 * a, off + 16 * (a + m)), A("CB"), A("PAT", 0, 16 * m), True, False)
             scan_(A("R", 16 * l0, 16 * (l0 + n)), A("D", d, d + 16 * n), A("NC", 16 * l0, 16 * (l0 + n)), 0.0, OP.add, OP.min)
+            line.insert(len(line) - (c > 1), len(calls) - 1)
+            if c == 0 and CH[1][2] == "V":
+                line.append(got[1])
+            if c < 2:
+                line.append(got[2 + c])
             for a, m in halves:
-                mm(A(ps, off + 16 * a, off + 16 * (a + m)), A("BB"), A("R", 16 * (l0 + a), 16 * (l0 + a + m)), False, False)
-                mm(A(ps, off + 16 * a + 15, off + 16 * (a + m), 16), A("I"), A("BS", 256 + l0 + a, 256 + l0 + a + m), False, True)
+                mms([(A(ps, off + 16 * a, off + 16 * (a + m)), A("BB"), A("R", 16 * (l0 + a), 16 * (l0 + a + m)), False, False),
+                     (A(ps, off + 16 * a + 15, off + 16 * (a + m), 16), A("I"), A("BS", 256 + l0 + a, 256 + l0 + a + m), False, True)])
             vtt(A("X", 16 * l0, 16 * l0 + 16 * n), A("D", d + 1, d + 1 + 16 * n), A(ps, off, off + 16 * n), OP.add)
+            if 1 < c < len(CH) - 2:
+                line.append(got[c + 2])
+            line.append(len(calls) - 1)
             act(ind(nst, A("CU", 256 * t + l0, 256 * t + l0 + n)), A("X", 16 * l0, 16 * l0 + 16 * n), FN.Silu)
+        for a, b in zip(line, line[1:]):
+            calls[b]["after"].setdefault(a, False)
         mm(A("P6", 256, 512), A("B"), A("NC", 0, 4096, 16))
-        vts(A("NL", 256, 512), A("BS", 0, 256), THR, OP.is_lt)
+        vts(A("NL", 256, 512), A("D", 1, 4096, 16), THR, OP.is_lt)
         vts(A("NL", 0, 256), A("P6", 256, 512), MET, OP.is_ge)
         if t < 3:
-            mm(A("P4", 0, 256), A("I"), A("R", 15, 4096, 16), True, False)
-            mm(A("P4", 0, 256), A("I"), A("BS", 256, 512), False, True)
+            mm(A("P4", 0, 256), A("B8"), A("ONE", 0, 256), True, False)
+            mm(A("P4", 0, 256), A("I"), A("BS", 256, 512), False, False)
+            mm(A("P4", 0, 256), A("I"), A("R", 15, 4096, 16), False, True)
             vts(A("RR"), A("P4", 0, 256), CAP, OP.min, -1.0 / 16, OP.mult)
             collect(A("P5", 0, 16), "ZB", lambda x: A("RR", x, 256, 16))
             vts(A("UL", 1, 17), A("P5", 0, 16), 0.5 - CAP, OP.is_gt)
-            mm(A("P5", 16, 32), A("W3"), A("UL", 1, 17), True, False)
-            mm(A("P5", 16, 32), A("UP"), A("UL", 0, 16), False, True)
-            mm(A("P5", 32, 48), A("IB"), A("UL", 1, 17), True, False)
-            mm(A("P5", 32, 48), A("I"), A("KM"), False, True)
+            mms([(A("P5", 16, 32), A("W3"), A("UL", 1, 17), True, False), (A("P5", 16, 32), A("UP"), A("UL", 0, 16), False, True),
+                 (A("P5", 32, 48), A("IB"), A("UL", 1, 17), True, False), (A("P5", 32, 48), A("I"), A("KM"), False, True)])
+            slots = len(calls) - 1
             scan_(A("SP"), A("ON16"), A("P5", 16, 32), -1.0)
             vtt(A("OF"), A("SP"), A("P5", 32, 48), OP.max)
             vcp(A("OU"), A("OF"))
@@ -419,12 +469,15 @@ def rank_program(g, core, T, topo):
             for l0, n, p, row in PART:
                 iota(A("VB", 2 * l0 + n, 2 * l0 + 2 * n), [[0, n]], 4095, 0)
 
+        line = []
         for l0, n in FG:
             vtt(A("IN3", 16 * l0, 16 * (l0 + n)), ind(nst, A(clu, l0, l0 + n)), A("BRF", 16 * l0, 16 * (l0 + n)), OP.is_gt)
+            line.append(len(calls) - 1)
         for l0, n, ps, off in SG3:
             mm(A(ps, off, off + 16 * n), A("I"), A("ZZ", 0, 16 * n), True, False)
-            for i in range(16):
-                mm(A(ps, off + i, off + 16 * n, 16), A("NI"), A("BT", l0, l0 + n), False, False)
+            mms([(A(ps, off + i, off + 16 * n, 16), A("NI"), A("BT", l0, l0 + n), False, False) for i in range(16)])
+            if ps == "TA" and t < 3:
+                calls[-1]["after"].setdefault(slots, False)
             ga = A("GA", 16 * (l0 - VL), 16 * (l0 - VL + n))
             act(ga, ind(nst, A(clu, l0, l0 + n)), FN.Copy)
             mm(A(ps, off, off + 16 * n), A("I"), ga, False, True)
@@ -435,11 +488,14 @@ def rank_program(g, core, T, topo):
             mm(A(p, 0, n), A("IB"), A("NL", l0, l0 + n), False, False)
             mm(A(p, 0, n), A("IB"), A("NL", 256 + l0, 256 + l0 + n), False, False)
             for a, m in CNT:
-                for i in range(16):
-                    if l0 <= a < l0 + n:
-                        mm(A(p, a - l0, a - l0 + m), EX("ZB" if a < VL else "ZH", i), A("IN3", 16 * a + i, 16 * (a + m), 16), False, i == 15 and a + m == l0 + n)
+                if l0 <= a < l0 + n:
+                    mms([(A(p, a - l0, a - l0 + m), EX("ZB" if a < VL else "ZH", i), A("IN3", 16 * a + i, 16 * (a + m), 16), False,
+                          i == 15 and a + m == l0 + n) for i in range(16)])
             f = A("FC", 2 * l0 + n, 2 * l0 + 2 * n)
-            vts(f, A(p, 0, n), 0.5, OP.is_ge, 8192.0, OP.mult)
+            if l0 + n < 256:
+                vts(f, A(p, 0, n), 0.0, OP.max)
+            else:
+                act(f, A(p, 0, n), FN.Relu)
             mm(A(p, 256, 256 + n), A("TRI"), f)
             vtt(A("SM", l0, l0 + n), f, A(p, 256, 256 + n), OP.is_gt)
             vtt(A("FC", 2 * l0, 2 * l0 + n), A("SM", l0, l0 + n), A(clf, l0, l0 + n), OP.mult)
@@ -449,26 +505,31 @@ def rank_program(g, core, T, topo):
             act(A("CR", l0, l0 + n), A(row, 0, n), FN.Identity, 0.5)
             mlu = A("MLU", y0, y0 + ny)
             vts(mlu, A(p, 448, 448 + ny), 2048.0, OP.add)
-            vts(A("VC", y0, y0 + ny), A(p, 448, 448 + ny), 2560.0, OP.add)
-            ok = A(p, 448 + ny, 448 + 2 * ny)
-            vtt(A("VAL", 2 * y0, 2 * y0 + ny), A("KS", 16 * t + y0, 16 * t + y0 + ny), ok, OP.min)
-            vtt(A("VAL", 2 * y0 + ny, 2 * y0 + 2 * ny), A("VC", y0, y0 + ny), ok, OP.min)
+            w = n + 2
+            vts(A("E", e + n + 1, e + w * ny, w), A(p, 448 + ny, 448 + 2 * ny), 0.5, OP.is_lt, -64 * CAP, OP.mult)
             for y in range(ny):
-                vts(A("E", e + n * y, e + n * y + 16 * y + 16), A("CR", l0, l0 + 16 * y + 16), A(p, 448 + y, 449 + y), OP.is_equal, 8192.0, OP.mult)
-            scan_(A("EZ", e, e + n * ny), A("EM", e, e + n * ny), A("E", e, e + n * ny), 0.0)
-            for h in range(2):
-                vtt(A("R3", 2 * y0 + h * ny, 2 * y0 + h * ny + ny), A("VAL", 2 * y0 + h * ny, 2 * y0 + h * ny + ny), A("EZ", e + n - 1, e + n * ny, n), OP.min)
+                vts(A("E", e + w * y, e + w * y + 16 * y + 16), A("CR", l0, l0 + 16 * y + 16), A(p, 448 + y, 449 + y), OP.is_equal)
+                line.append(len(calls) - 1)
+            scan_(A("EZ", e, e + w * ny), A("EM", e, e + w * ny), A("E", e, e + w * ny), 0.0)
+            line.append(len(calls) - 1)
+            z = A("EZ", e + n + 1, e + w * ny, w)
+            vtt(A("R3", 2 * y0, 2 * y0 + ny), A("KS", 16 * t + y0, 16 * t + y0 + ny), z, OP.min)
+            vtt(A("R3", 2 * y0 + ny, 2 * y0 + 2 * ny), A(p, 448, 448 + ny), z, OP.min)
             vtt(A("R4", 2 * y0, 2 * y0 + 2 * ny), A("R3", 2 * y0, 2 * y0 + 2 * ny), A("KD", 2 * y0, 2 * y0 + 2 * ny), OP.max)
-            vcp(A("OFS", 2 * y0, 2 * y0 + 2 * ny), A("R4", 2 * y0, 2 * y0 + 2 * ny))
+            ofs = A("OFS", 2 * y0, 2 * y0 + 2 * ny)
+            vts(ofs, A("R4", 2 * y0, 2 * y0 + 2 * ny), 2560.0, OP.add)
             src = N if t < 3 else "YR"
             act(A("VB", 2 * l0, 2 * l0 + n), ind(A(src, 512, 4608), mlu), FN.Copy)
-            vcp(ind(A(src, 0, 4608), A("OFS", 2 * y0, 2 * y0 + 2 * ny)), A("VB", 2 * l0, 2 * l0 + 2 * n))
+            if t < 3 and l0 + n < 256:
+                act(ind(A(src, 0, 4608), ofs), A("VB", 2 * l0, 2 * l0 + 2 * n), FN.Silu)
+            else:
+                vcp(ind(A(src, 0, 4608), ofs), A("VB", 2 * l0, 2 * l0 + 2 * n))
+            if t < 3:
+                act(A("OV", l0, l0 + n), ind(A("OO", 512, 4608), mlu), FN.Copy)
+                act(ind(A("OO"), A("OFS", 2 * y0, 2 * y0 + ny)), A("OV", l0, l0 + n), FN.Silu)
+        for a, b in zip(line, line[1:]):
+            calls[b]["after"].setdefault(a, False)
         if t < 3:
-            act(A("OV"), ind(A("OO", 512, 4608), A("MLU")), FN.Copy)
-            for l0, n, p, row in PART:
-                act(ind(A("OO"), A("OFS", l0 // 8, l0 // 8 + n // 16)), A("OV", l0, l0 + n), FN.Silu)
-            cards(t + 1)
-            covers(t + 1)
             needs(t + 1)
     dma(T.y[:, :], T.YR[0:128:16, 512:4608], [A("YR")], [], 2.6)
     issue()

@@ -4,35 +4,59 @@ OP = AluOpType
 FN = ActivationFunctionType
 MARK, THR, CAP = 15.0 / 64, 1.0 / 2048, 32768.0
 MET = 16 * CAP - 8
-CH = [(0, 16, "V", "TA", 0), (16, 32, "S", "TA", 512), (48, 16, "V", "TA", 0)] + [(l, 32, "V", "TA", 512 - 16 * l % 1024) for l in range(64, 256, 32)]
-VL = 144
-FG = [(0, 64), (64, 64), (128, 16)]
-SG3 = [(144, 32, "TB", 0), (176, 32, "TB", 512), (208, 32, "TA", 0), (240, 16, "TA", 512)]
-CNT = [(0, 64), (64, 64), (128, 16), (144, 64), (208, 48)]
+GET = [(0, 24, "V"), (24, 40, "S"), (64, 32, "V"), (96, 32, "S"), (128, 64, "V"), (192, 64, "V")]
+CH = [(0, 24, "TA", 0), (24, 40, "TB", 0), (64, 64, "TA", 0), (128, 64, "TB", 0), (192, 64, "TA", 0)]
+GET2 = [(0, 32, "V"), (32, 32, "S"), (64, 64, "S"), (128, 64, "V"), (192, 64, "S")]
+CH2 = [(0, 32, "TA", 0, "V"), (32, 32, "TA", 512, "V"), (64, 64, "TB", 0, "S"), (128, 64, "TA", 0, "V"), (192, 64, "TB", 0, "V")]
+GET3 = [(0, 32, "V"), (32, 64, "S"), (96, 32, "V"), (128, 64, "S"), (192, 32, "V"), (224, 32, "S")]
+CH3 = [(0, 32, "TA", 0, "V"), (32, 32, "TA", 512, "V"), (64, 32, "TB", 0, "S"), (96, 32, "TB", 512, "S"), (128, 32, "P4", 0, "V"),
+       (160, 32, "P5", 0, "S"), (192, 32, "P7", 0, "S"), (224, 32, "TA", 0, "V")]
+BACK = [(0, 128, "V"), (128, 128, "S")]
+INV = [[(3, 0, 32, "V"), (3, 32, 32, "V"), (3, 64, 16, "S"), (3, 80, 16, "S")],
+       [(3, 96, 32, "V"), (3, 128, 32, "V"), (3, 160, 16, "S"), (3, 176, 16, "S")],
+       [(3, 192, 32, "V"), (3, 224, 16, "S"), (3, 240, 16, "S")], []]
+TURN = 3
+VR = [(0, 96), (128, 192)]
+OWN = [0, 96, 192, 256]
+FG = [(0, 64), (64, 32), (128, 64)]
+SG3 = [(96, 32, "TB", 0), (192, 32, "TB", 512), (224, 32, "TA", 0)]
+CNT = [(0, 64), (64, 64), (128, 64), (192, 64)]
 PART = [(0, 128, "P6", "P7"), (128, 128, "P4", "P5")]
-CYC, CALL, HOP, PE, GATHER, SCATTER = 0.00083, 0.03, 0.11, 0.00042, 1.56, 3.0
+COST = (0.00083, 0.01, 0.24, 0.00042, 1.2, 2.4)
+CYC, CALL, HOP, PE, GATHER, SCATTER = COST
+VIEWS = [(1.0, 0.0, 0.0), (1.3, 0.4, 2.6)]
 PASSES = 3
-EN = sum((p[1] + 2) * p[1] // 16 for p in PART)
+MOVES = 30000
+SLACK = 0.0004
+ORDER = {}
+SPLIT = 1
+WHO = "SSSSS"
+LAST = [(0, 4), (4, 16)]
+FILL = 4
+TAIL = [[("x192 i3.%d c0" if q == "V" else "s2 i3.%d") % l for u, l, n, q in pieces] for pieces in INV[:3]] + [["b0 d32"]]
+EW = 130
+EN = 8 * EW
 
 _sb = {
-    "OLU": (256, "uint16"), "OCN": (256, "int32"), "OCH": (256, "float16"), "WHO": (4096, "float16"), "OL0": (32, "uint16"),
+    "OLU": (256, "uint16"), "OCN": (256, "int32"), "OCH": (256, "float16"), "OL0": (32, "uint16"),
     "SK": (4112, "bfloat16"), "COV": (4096, "int32"), "CI": (1024, "int32"), "CU": (1024, "uint16"), "CF": (1024, "float16"), "CS": (1024, "uint16"),
     "ND": (768, "bfloat16"), "LS": (128, "uint16"), "KS": (64, "float32"),
-    "WA": (4624, "float32"), "WB": (4624, "float32"), "OO": (4608, "float32"), "YR": (4608, "float32"),
+    "WA": (4624, "float32"), "INV0": (4608, "float32"), "WB": (4624, "float32"), "IOTA": (4096, "float32"), "IL": (256, "float32"),
+    "IU0": (256, "uint16"), "IU1": (256, "uint16"), "HI": (256, "int32"), "HF": (256, "bfloat16"), "I8": (128, "bfloat16"), "OO": (4608, "float32"),
     "ONE": (512, "bfloat16"), "I": (128, "bfloat16"), "NI": (128, "bfloat16"), "B": (128, "bfloat16"), "BB": (128, "bfloat16"), "CB": (128, "bfloat16"),
     "PX": (2048, "bfloat16"), "ZB": (144, "bfloat16"), "ZH": (144, "bfloat16"), "BH": (128, "bfloat16"), "PAT": (512, "bfloat16"),
-    "Z0": (144, "bfloat16"), "Z15": (144, "bfloat16"), "G8": (8, "bfloat16"), "G15": (8, "bfloat16"), "SH": (128, "bfloat16"), "S1": (128, "bfloat16"),
+    "Z0": (144, "bfloat16"), "Z15": (144, "bfloat16"), "G8": (8, "bfloat16"), "G15": (8, "bfloat16"), "S1": (128, "bfloat16"),
     "TRI": (128, "bfloat16"), "UP": (128, "bfloat16"), "UN": (128, "bfloat16"), "W3": (128, "bfloat16"), "IB": (128, "bfloat16"),
     "PI": (1, "int32"), "PA": (1, "int32"), "XC": (1, "float32"), "SC": (2, "float32"), "ZR": (16, "float32"), "XM": (16, "float32"), "LY": (32, "float32"),
-    "KM": (16, "float16"), "KD": (32, "float32"), "ON16": (16, "float32"), "ZZ": (512, "bfloat16"), "OFFS": (256, "bfloat16"),
+    "KM": (16, "float16"), "KD": (32, "float32"), "ON16": (16, "float32"), "OFFS": (256, "bfloat16"),
     "D": (4112, "bfloat16"), "NC": (4096, "float16"), "R": (4096, "float16"),
     "X": (4096, "float32"), "RR": (256, "float16"), "UL": (17, "bfloat16"), "SP": (16, "float32"), "OF": (16, "float32"), "OU": (16, "uint16"),
-    "BS": (512, "bfloat16"), "BT": (256, "float16"), "BRF": (VL * 16, "float16"), "NL": (512, "bfloat16"),
+    "BS": (512, "bfloat16"), "BT": (256, "float16"), "BRF": (4096, "float16"), "NL": (512, "bfloat16"),
     "CLF0": (256, "float16"), "CLU0": (256, "uint16"), "CLF1": (256, "float16"), "CLU1": (256, "uint16"),
-    "IN3": (4096, "bfloat16"), "GA": (4096 - VL * 16, "bfloat16"),
-    "SM": (256, "bfloat16"), "FC": (512, "float16"), "CR": (256, "float16"), "B8": (128, "bfloat16"),
-    "E": (EN, "bfloat16"), "EM": (EN, "bfloat16"), "EZ": (EN, "bfloat16"), "EX": (16, "bfloat16"),
-    "R3": (32, "float32"), "R4": (32, "float32"), "OFS": (32, "uint16"), "MLU": (16, "uint16"),
+    "IN3": (4096, "bfloat16"), "GA": (4096, "bfloat16"),
+    "F": (256, "bfloat16"), "TRM": (128, "bfloat16"), "TRN": (128, "bfloat16"), "FC": (512, "float16"), "CR": (256, "float16"), "B8": (128, "bfloat16"),
+    "E": (EN, "bfloat16"), "EM": (EN, "bfloat16"), "EZ": (2 * EN, "bfloat16"), "EX": (16, "bfloat16"),
+    "R3": (32, "float32"), "R4": (32, "float32"), "OFS0": (32, "uint16"), "MLU0": (32, "uint16"), "OFS1": (32, "uint16"), "MLU1": (32, "uint16"),
     "VB": (512, "float32"), "OV": (256, "float32"),
     "ZF": (256, "float32"), "OFN": (256, "float32"), "OI": (256, "int32"), "EF": (256, "float32"), "YF": (256, "float32"),
 }
@@ -45,7 +69,7 @@ SCRATCH["TB"] = ("psum", [128, 1024], "float32")
 for _t in range(4, 8):
     SCRATCH["P%d" % _t] = ("psum", [128, 512], "float32")
 PS = ("TA", "TB", "P4", "P5", "P6", "P7")
-SEMAPHORES = ["cV", "cS", "cT", "cG"] + ["arr%d" % t for t in range(3)] + ["loc%d" % t for t in range(3)] + ["d%d" % k for k in range(12)]
+SEMAPHORES = ["cV", "cS", "cT", "cG"] + ["arr%d" % t for t in range(3)] + ["loc%d" % t for t in range(3)] + ["d%d" % k for k in range(18)]
 
 
 def issue_order(calls):
@@ -92,7 +116,85 @@ def issue_order(calls):
             best = (span, end)
         way = place(end, behind, before, True)
     end = best[1]
-    return sorted(range(n), key=lambda j: (end[j] - calls[j]["cost"], j))
+    return polish(calls, sorted(range(n), key=lambda j: (end[j] - calls[j]["cost"], j)))
+
+
+def polish(calls, order):
+    n = len(calls)
+    queue, lag = [c["q"] for c in calls], [c["lag"] for c in calls]
+    behind = [[] for c in calls]
+    for k, c in enumerate(calls):
+        for p in c["after"]:
+            behind[p].append(k)
+    views = []
+    for slow, gather, scatter in VIEWS:
+        views.append([slow * (c["cost"] + CYC * (gather * c["gathered"] + scatter * c["scattered"])) for c in calls])
+    before = [[(p, lag[p] + HOP if wait else 0.0) for p, wait in c["after"].items()] for c in calls]
+
+    def run(order, cost, first, end, why):
+        end, why, free, last = list(end), list(why), {q: 0.0 for q in queue}, {q: -1 for q in queue}
+        for k in order[:first]:
+            last[queue[k]] = k
+        for q, k in last.items():
+            free[q] = end[k] if k >= 0 else 0.0
+        for k in order[first:]:
+            q = queue[k]
+            at, by = free[q], last[q]
+            for p, hop in before[k]:
+                if end[p] + hop > at:
+                    at, by = end[p] + hop, p
+            end[k] = free[q] = at + cost[k]
+            why[k], last[q] = by, k
+        return end, why, max(end[k] + lag[k] for k in order[-40:])
+
+    now = [run(order, cost, 0, [0.0] * n, [-1] * n) for cost in views]
+    unit = [r[2] for r in now]
+    seed, fresh, best = 1, True, (len(views), order)
+    mark = best[0]
+    for turn in range(MOVES):
+        if fresh:
+            pos = {k: i for i, k in enumerate(order)}
+            pairs = []
+            for end, why, span in now:
+                k = max(order[-40:], key=lambda j: end[j] + lag[j])
+                while k >= 0:
+                    u = why[k]
+                    if u >= 0 and queue[u] == queue[k] and u not in calls[k]["after"]:
+                        pairs.append((u, k))
+                    k = u
+            fresh = False
+        seed = seed * 6364136223846793005 % (1 << 64) + 1442695040888963407
+        a, b, c = (seed >> 20) % 10, (seed >> 24) % 65536, (seed >> 40) % 65536
+        u, v = pairs[b % len(pairs)]
+        i, j = pos[u], pos[v]
+        if a < 4:
+            need = {v}
+            for k in reversed(order[i:j + 1]):
+                if k in need:
+                    need.update(p for p in calls[k]["after"] if pos[p] >= i)
+            if u in need:
+                continue
+            first, new = i, order[:i] + [k for k in order[i:j + 1] if k in need] + [k for k in order[i:j + 1] if k not in need] + order[j + 1:]
+        elif a < 7:
+            same = [x for x in range(i + 1, min([pos[s] for s in behind[u]] + [n, i + 200])) if queue[order[x]] == queue[u]]
+            if not same:
+                continue
+            x = same[c % len(same)]
+            first, new = i, order[:i] + order[i + 1:x + 1] + [u] + order[x + 1:]
+        else:
+            same = [x for x in range(max([pos[p] + 1 for p in calls[u]["after"]] + [0, i - 200]), i) if queue[order[x]] == queue[u]]
+            if not same:
+                continue
+            first = same[c % len(same)]
+            new = order[:first] + [u] + order[first:i] + order[i + 1:]
+        then = [run(new, cost, first, r[0], r[1]) for cost, r in zip(views, now)]
+        score = sum(r[2] / z for r, z in zip(then, unit))
+        if score <= mark + SLACK * (1 - turn / MOVES):
+            end, cost = then[0][0], views[0]
+            order, now, mark, fresh = sorted(new, key=lambda k: end[k] - cost[k]), then, score, True
+            if mark < best[0]:
+                best = (mark, order)
+    return best[1]
 
 
 def rank_program(g, core, T, topo):
@@ -118,7 +220,10 @@ def rank_program(g, core, T, topo):
         return [(name, a, b, s, False)]
 
     def apart(a, b, s, x, y, z):
-        return x >= b or y <= a or (s == z and s > 1 and (a - x) % s != 0)
+        if s == 1 or z == 1:
+            lo, hi, at, step = (a, b, x, z) if s == 1 else (x, y, a, s)
+            return max(a, x) >= min(b, y) or at + max(0, -((at - lo) // step)) * step >= min(b, y)
+        return x >= b or y <= a or (s == z and (a - x) % s != 0)
 
     def emit(q, fn, reads, writes, cost, lag=0.0, kind="compute", after=()):
         me, dep = len(calls), {p: True for p in after}
@@ -139,7 +244,7 @@ def rank_program(g, core, T, topo):
                             keep.append(r)
                         keep.append((lo, hi, st, me, q, w))
                         log[key] = keep
-        calls.append({"name": writes[0][1][0][0] if writes else "", "q": q, "fn": fn, "after": dep, "cost": cost, "lag": lag, "kind": kind})
+        calls.append({"scattered": writes[0][2] if writes and writes[0][3] else 0, "gathered": reads[0][2] if reads and reads[0][3] else 0, "q": q, "fn": fn, "after": dep, "cost": cost, "lag": lag, "kind": kind})
         return me
 
     def issue():
@@ -155,7 +260,9 @@ def rank_program(g, core, T, topo):
             for s, v in list(clocks.get(ev, {}).items()) + [ev]:
                 k[s] = max(k.get(s, 0), v)
 
-        for k in issue_order(calls):
+        if len(calls) not in ORDER:
+            ORDER[len(calls)] = issue_order(calls)
+        for k in ORDER[len(calls)]:
             c = calls[k]
             q = c["q"]
             if c["kind"] == "arrival":
@@ -246,16 +353,20 @@ def rank_program(g, core, T, topo):
     def EX(name, x):
         return A(name, 15 - x, 143 - x)
 
-    def collect(out, name, rhs, first=0):
-        mms([(out, EX(name, x), rhs(x), x == first, x == 15) for x in range(first, 16)])
+    def collect(out, name, rhs, n=16):
+        mms([(out, EX(name, x), rhs(x), x == 0, x == n - 1) for x in range(n)])
 
     d0 = dma(T.OCN[:, :], T.occ[:, :], [], [A("OCN")], 2.6)
     d1 = dma(T.CI[:, 0:256], T.cards[:, 0:256], [], [A("CI", 0, 256)], 3.2)
-    d2 = dma(T.SK[:, 0:4096], T.skill[:, :], [], [A("SK", 0, 4096)], 8.4)
-    d3 = dma(T.ND[:, :], T.need[:, :], [], [A("ND")], 9.3)
+    d3 = dma(T.ND[:, 0:192], T.need[:, 0:192], [], [A("ND", 0, 192)], 3.5)
+    d2 = dma(T.SK[:, 0:4096], T.skill[:, :], [], [A("SK", 0, 4096)], 8.6)
     d4 = dma(T.COV[:, :], T.cover[:, :], [], [A("COV")], 12.5, [d2])
-    d5 = dma(T.CI[:, 256:1024], T.cards[:, 256:1024], [], [A("CI", 256, 1024)], 14.5, [d2])
-    for a, b in ((d0, d1), (d1, d2), (d2, d3), (d3, d4), (d4, d5)):
+    u, v = TURN, 5 - TURN
+    d7 = dma(T.CI[:, 256 * u:256 * u + 256], T.cards[:, 256 * u:256 * u + 256], [], [A("CI", 256 * u, 256 * u + 256)], 9.3)
+    d5 = dma(T.CI[:, 256:512], T.cards[:, 256:512], [], [A("CI", 256, 512)], 13.5, [d2])
+    d6 = dma(T.ND[:, 192:768], T.need[:, 192:768], [], [A("ND", 192, 768)], 14.2, [d2])
+    d8 = dma(T.CI[:, 256 * v:256 * v + 256], T.cards[:, 256 * v:256 * v + 256], [], [A("CI", 256 * v, 256 * v + 256)], 15.0, [d2])
+    for a, b in ((d0, d1), (d1, d3), (d3, d2), (d2, d7), (d7, d4), (d4, d5), (d5, d6), (d6, d8)):
         calls[b]["after"].setdefault(a, False)
 
     vms(A("ONE"), 1.0)
@@ -264,14 +375,16 @@ def rank_program(g, core, T, topo):
     sel(A("UN"), A("ONE", 0, 128), [[-16, 8], [0, 16]], OP.is_ge, 0.0, 0, 1)
     sel(A("B"), A("UN"), [[16, 8], [0, 16]], OP.is_ge, 0.0, 15, -1)
     sel(A("G8"), A("ONE", 0, 8), [[-16, 8]], OP.is_equal, 0.0, 0, 1)
-    for k in range(4):
+    for k in range(FILL):
         act(A("NC", 512 * k, 512 * k + 512), A("ONE"), FN.Silu, 0.0, CAP, 0.0 if k else 1.3)
-    for k in range(4, 8):
+    for k in range(FILL, 8):
         vms(A("NC", 512 * k, 512 * k + 512), CAP)
+    for k in range(2):
+        iota(A("IOTA", 1024 * k, 1024 * k + 1024), [[1, 1024]], 32 + 1024 * k, 0)
     for z in ("Z0", "ZB", "Z15"):
         vms(A(z), 0.0)
     vts(A("PA"), A("PI"), 15, OP.bitwise_and)
-    vms(A("D", 4096, 4112), 2 * CAP)
+    vms(A("D", 0, 16), 2 * CAP)
     vcp(A("XC"), A("PA"))
     vms(A("SK", 4096, 4112), CAP / 8)
     vts(A("XM"), A("ZR"), A("XC"), OP.is_equal)
@@ -282,22 +395,22 @@ def rank_program(g, core, T, topo):
     sel(A("PAT"), A("ONE"), [[0, 32], [1, 16]], OP.is_equal, 0.0, -15, 0)
     iota(A("LY"), [[16, 32]], 0, 0)
     sel(A("G15"), A("ONE", 0, 8), [[-16, 8]], OP.is_equal, 0.0, -15, 1)
-    iota(A("WB", 4608, 4624), [[0, 16]], int(2 * CAP), 0)
     iota(A("WA", 4608, 4624), [[0, 16]], int(2 * CAP), 0)
+    iota(A("WB", 4608, 4624), [[0, 16]], int(2 * CAP), 0)
+    vts(A("I8"), A("I"), 256.0, OP.mult)
     sel(A("UP"), A("B"), [[-1, 128]], OP.is_gt, 0.0, 0, 1)
     sel(A("TRI"), A("B"), [[1, 128]], OP.is_gt, 0.0, 0, -1)
-    sel(A("SH"), A("B"), [[1, 128]], OP.is_equal, 0.0, -1, -1)
-    iota(A("VB"), [[0, 512]], 0, 0)
+    for l0, n, p, row in PART:
+        iota(A("VB", 2 * l0 + n, 2 * l0 + 2 * n), [[0, n]], 0, 0)
     iota(A("ON16"), [[0, 16]], 1, 0)
-    iota(A("ZZ"), [[0, 512]], 0, 0)
     iota(A("UL"), [[0, 17]], 0, 0)
-    iota(A("OFFS", 0, VL), [[0, VL]], -8, 0)
-    iota(A("OFFS", VL, 256), [[0, 256 - VL]], 0, 0)
+    iota(A("OFFS"), [[0, 256]], 0, 0)
+    for a, b in VR:
+        iota(A("OFFS", a, b), [[0, b - a]], -4, 0)
     for t in range(3):
         iota(A("SW%d" % t, 0, 64), [[0, 64]], -2048, 0, False)
-    for k in range(9):
-        iota(A("YR", 512 * k, 512 * k + 512), [[0, 512]], 0, 0)
-    vts(A("SC", 0, 1), A("XM", 0, 1), 2048.0, OP.mult, 2048.0, OP.add)
+    vts(A("SC", 0, 1), A("XM", 15, 16), 2048.0, OP.mult, 2048.0, OP.add)
+    vts(A("SC", 1, 2), A("XM", 15, 16), -1.0, OP.mult, 1.0, OP.add)
     vts(A("CB"), A("B"), A("XM", 0, 1), OP.mult, -2 * CAP, OP.mult)
     vts(A("S1"), A("B"), A("XM", 1, 2), OP.mult, -16384 * CAP, OP.mult)
     vts(A("PAT"), A("PAT"), A("XM", 1, 2), OP.max)
@@ -309,80 +422,122 @@ def rank_program(g, core, T, topo):
     vts(A("ZH"), A("ZB"), 0.5, OP.mult)
     vts(A("BH"), A("B"), -0.5, OP.mult)
     vts(A("KM"), A("KD", 0, 16), 2816.0, OP.add)
-    vts(A("TRI"), A("TRI"), 16.0, OP.mult)
+    vtt(A("TRM"), A("I"), A("TRI"), OP.subtract)
+    vts(A("TRN"), A("TRI"), -1.0, OP.mult)
     vts(A("B8"), A("B"), -0.125, OP.mult)
     vts(A("NI"), A("I"), -1.0, OP.mult)
     vts(A("IB"), A("I"), -2048.0, OP.mult)
     vtt(A("W3"), A("B"), A("UP"), OP.subtract)
     vts(A("EX"), A("XM"), -1024.0, OP.mult, 1.0, OP.add)
-    eat = [sum((p[1] + 2) * p[1] // 16 for p in PART[:k]) for k in range(len(PART))]
-    for e, (l0, n, p, row) in zip(eat, PART):
-        w, ny = n + 2, n // 16
-        iota(A("EM", e, e + w * ny), [[0, w * ny]], 1, 0)
-        iota(A("E", e, e + w * ny), [[0, w * ny]], 0, 0)
-        for y in range(ny):
-            gcp(A("EM", e + (w + 16) * y, e + (w + 16) * y + 16), A("EX"), 16)
-        iota(A("EM", e, e + w * ny, w), [[0, ny]], 0, 0)
-        iota(A("EM", e + n, e + w * ny, w), [[0, ny]], 8192, 0)
-        iota(A("E", e + n, e + w * ny, w), [[0, ny]], -4096, 0)
+    iota(A("EM"), [[0, EN]], 1, 0)
+    vms(A("E"), 0.0)
+    for y in range(8):
+        gcp(A("EM", (EW + 16) * y, (EW + 16) * y + 16), A("EX"), 16)
+    iota(A("EM", 0, EN, EW), [[0, 8]], 0, 0)
+    iota(A("EM", 128, EN, EW), [[0, 8]], 8192, 0)
+    iota(A("E", 128, EN, EW), [[0, 8]], -4096, 0)
+    early = [k for k, c in enumerate(calls) if c["q"] == "G"]
+    for k in range(2, 4):
+        iota(A("IOTA", 1024 * k, 1024 * k + 1024), [[1, 1024]], 32 + 1024 * k, 0)
+    iota(A("INV0", 4096, 4608), [[0, 512]], 0, 0)
     vts(A("OCH"), A("OCN"), -2048.0, OP.add)
     vcp(A("CU", 0, 256), A("CI", 0, 256))
     banks = (("P6", 0), ("P7", 0), ("TA", 0), ("TA", 512), ("TB", 0), ("TB", 512), ("P4", 0), ("P5", 0))
     for k in range(8):
         ps, c = banks[k]
-        for h in range(2):
-            x = 2 * k + h
-            mm(A(ps, c + 256 * h, c + 256 * h + 256), A("PX", 128 * x, 128 * x + 128), A("OCH"))
+        mms([(A(ps, c + 256 * h, c + 256 * h + 256), A("PX", 256 * k + 128 * h, 256 * k + 128 * h + 128), A("OCH"), True, True) for h in range(2)])
+        if k:
+            calls[-1]["after"].setdefault(len(calls) - 3, False)
         o = A("OO", 512 + 512 * k, 1024 + 512 * k)
         if k % 2 == 0:
             vts(o, A(ps, c, c + 512), 2080.0, OP.add)
         else:
             act(o, A(ps, c, c + 512), FN.Identity, 2080.0)
     for k in range(4):
-        o, i = A("WHO", 1024 * k, 1024 * k + 1024), ind(A("OO", 512, 4608), A("CU", 64 * k, 64 * k + 64))
+        o, i = A("BRF", 1024 * k, 1024 * k + 1024), ind(A("OO", 512, 4608), A("CU", 64 * k, 64 * k + 64))
         if k % 2 == 0:
             vts(o, i, -2080.0, OP.add)
         else:
             act(o, i, FN.Identity, -2080.0)
     for k in range(4):
-        collect(A("P%d" % (4 + k), 0, 64), "Z0", lambda x: A("WHO", 1024 * k + x - 1, 1024 * k + 1024, 16), 1)
+        collect(A("P%d" % (4 + k), 0, 64), "Z0", lambda x: A("BRF", 1024 * k + x, 1024 * k + 1024, 16), 15)
         vts(A("OLU", 64 * k, 64 * k + 64), A("P%d" % (4 + k), 0, 64), A("SC", 0, 1), OP.add)
-    for h in range(2):
-        collect(A("TB", 512 * h, 512 * h + 8), "Z0", lambda x: A("WHO", 2048 * h + 16 * x + 15, 2048 * h + 2048, 256))
-        vts(A("OL0", 16 + 8 * h, 24 + 8 * h), A("TB", 512 * h, 512 * h + 8), 2048.0, OP.add)
+    for h, (a, b) in enumerate(LAST):
+        collect(A("TB", 512 * h, 512 * h + b - a), "Z0", lambda x: A("BRF", 256 * a + 16 * x + 15, 256 * b, 256))
+        vts(A("OL0", 16 + a, 16 + b), A("TB", 512 * h, 512 * h + b - a), 2048.0, OP.add)
     vms(A("SK", 4095, 4096), -MARK / 16)
 
     def cards(t):
         a, b = 256 * t, 256 * t + 256
-        act(A("CF", a, b), A("CI", a, b), FN.Identity, -2048.0)
         collect(A("P7", 256, 272), "Z0", lambda x: A("CF", a + x, b, 16))
+        tag("k0")
         if t:
             collect(A("P7", 272, 288), "Z15", lambda x: A("CF", a + x, b, 16))
-            mm(A("P7", 0, 256), A("SH"), A("CF", a, b))
-            vts(A("CU", a, b), A("CF", a, b), 2048.0, OP.add)
-            vts(A("CS", a, b), A("P7", 0, 256), A("SC", 0, 1), OP.add)
+            tag("k1")
+            if t < TURN:
+                vts(A("CU", a, b), A("CF", a, b), 2048.0, OP.add)
+            vts(A("CS", a, b), A("CF", a, b), A("SC", 1, 2), OP.mult, A("SC", 0, 1), OP.add)
+            tag("cs")
             vts(A("LS", 32 * t, 32 * t + 32), A("P7", 256, 288), 2048.0, OP.add)
+            tag("ls")
         else:
             vts(A("LS", 0, 16), A("P7", 256, 272), 2048.0, OP.add)
-        act(A("KS", 16 * t, 16 * t + 16), A("P7", 256, 272), FN.Copy)
+        vcp(A("KS", 16 * t, 16 * t + 16), A("P7", 256, 272))
+        tag("ks")
+
+    def turned(t):
+        a, b = 256 * t, 256 * t + 256
+        vts(A("HI"), A("CI", a, b), 4, OP.arith_shift_right)
+        act(A("HF"), A("HI"), FN.Copy)
+        mms([(A("P7", 0, 256), A("I8"), A("CF", a, b), True, False), (A("P7", 0, 256), A("I"), A("HF"), False, False),
+             (A("P7", 0, 256), A("IB"), A("HF"), False, False), (A("P7", 0, 256), A("IB"), A("HF"), False, True)])
+        vts(A("CU", a, b), A("P7", 0, 256), 524288.0, OP.add)
+
+    def places(t, l0, n, q):
+        name = ("INV0", "WA")[t - 2] if TURN == 2 else "WA" if False else "INV0"
+        row = A(name, 0, 4096)
+        o, i = ind(row, A("CU", 256 * t + l0, 256 * t + l0 + n)), A("IOTA", 16 * l0, 16 * (l0 + n))
+        if q == "V":
+            vcp(o, i)
+        else:
+            act(o, i, FN.Silu)
+        tag("i%d.%d" % (t, l0))
+        if l0 + n == 256:
+            dma(T.IL[:, :], T[name][0:128:16, 0:4096], [row], [A("IL")], 3.0)
+            vts(A("IU%d" % (t % 2)), A("IL"), -31.75, OP.add)
+
+    def numbers(t):
+        act(A("CF", 256 * t, 256 * t + 256), A("CI", 256 * t, 256 * t + 256), FN.Identity, -2048.0)
+        tag("cf")
 
     def covers(t):
-        f, u = "CLF%d" % (t % 2), "CLU%d" % (t % 2)
-        act(A(f), ind(A("COV"), A("LS", 32 * t, 32 * t + 16)), FN.Identity, -2048.0)
-        vts(A(u), A(f), 2048.0, OP.add)
+        act(A("CLF%d" % (t % 2)), ind(A("COV"), A("LS", 32 * t, 32 * t + 16)), FN.Identity, -2048.0)
+        tag("cl")
 
     def needs(t):
         act(A("NC", 0, 3072, 16), A("ND", 192 * t, 192 * t + 192), FN.Identity, CAP, -16.0)
+        tag("nd")
+
+    tags = {}
+
+    def tag(name):
+        tags[name] = len(calls) - 1
 
     needs(0)
+    numbers(0)
     cards(0)
     covers(0)
-    win = ["WA", "WB"]
+    for t in range(1, 4):
+        numbers(t)
+    turned(TURN)
     sent = None
     for t in range(4):
-        W, N = win[t % 2], win[1 - t % 2]
+        W, N = (("WA", "WA"), ("WA", "WB"), ("WB", "WB" if TURN == 2 else "WA"), ("WB", "WB") if TURN == 2 else ("WA", "WA"))[t]
         wst, nst = A(W, 512, 4624), A(N, 512, 4608)
         clf, clu = "CLF%d" % (t % 2), "CLU%d" % (t % 2)
+        tags.clear()
+        vts(A(clu), A(clf), 2048.0, OP.add)
+        tag("cv")
 
         def fetch(o, lst, q):
             if t == 0 and q == "V":
@@ -400,138 +555,189 @@ def rank_program(g, core, T, topo):
         else:
             cards(t + 1)
             covers(t + 1)
+            if t == 1 and TURN == 2:
+                turned(3)
         lst, at = ("LS", 32 * t) if t else ("OL0", 0)
-        for h in range(2):
-            fetch(A("BS", 256 + 128 * h, 384 + 128 * h), A(lst, at + 16 + 8 * h, at + 24 + 8 * h), "S")
+        for h, (a, b) in enumerate(LAST):
+            fetch(A("BS", 256 + 16 * a, 256 + 16 * b), A(lst, at + 16 + a, at + 16 + b), "S")
+            tag("b%d" % h)
         if t:
             av = A("AV%d" % (t - 1))
             emit("N", ("arr%d" % (t - 1), len(topo.engines(T.cores[rank - 1], core))), [], [av], 0.0, 0.0, "arrival", [sent])
             vts(A("NC", 3072, 4096, 16), av, -16.0, OP.mult)
-        got = []
-        for l0, n, q, ps, off in CH:
-            fetch(A("D", 16 * l0, 16 * (l0 + n)), A("CS", 256 * t + l0, 256 * t + l0 + n) if t else A("OLU", l0, l0 + n), q)
-            got.append(len(calls) - 1)
-        line = got[:1]
-        for a, b in ((0, VL), (VL, 192), (192, 256)):
-            vts(A("BT", a, b), A("D", 16 * a + 1, 16 * b, 16), -8.0, OP.add, 0.0, OP.max)
-        for i in range(16):
-            gcp(A("BRF", i, VL * 16, 16), A("BT", 0, VL), VL)
-            if i:
-                calls[-1]["after"].setdefault(len(calls) - 2, False)
-        for c, (l0, n, q, ps, off) in enumerate(CH):
-            d = 16 * l0
+            tag("av")
+        for l0, n, q in GET if t < TURN else (GET2, GET3)[t - 2]:
+            fetch(A("D", 16 * (l0 + 1), 16 * (l0 + n + 1)), A("CS", 256 * t + l0, 256 * t + l0 + n) if t else A("OLU", l0, l0 + n), q)
+            tag("d%d" % l0)
+        for a, b in zip(OWN, OWN[1:]):
+            vts(A("BT", a, b), A("D", 16 * a + 16, 16 * b + 16, 16), -8.0, OP.add, 0.0, OP.max)
+            tag("B%d" % a)
+        for a, b in VR:
+            for i in range(16):
+                gcp(A("BRF", 16 * a + i, 16 * b, 16), A("BT", a, b), b - a)
+                for k in [len(calls) - 2] if a + i else early:
+                    calls[-1]["after"].setdefault(k, False)
+        tag("rep")
+        for piece in INV[t]:
+            places(*piece)
+        for l0, n, ps, off, q in [c + ("V",) for c in CH] if t < TURN else (CH2, CH3)[t - 2]:
+            d = 16 * l0 + 15
             halves = [(a, min(32, n - a)) for a in range(0, n, 32)]
             for a, m in halves:
                 mm(A(ps, off + 16 * a, off + 16 * (a + m)), A("CB"), A("PAT", 0, 16 * m), True, False)
             scan_(A("R", 16 * l0, 16 * (l0 + n)), A("D", d, d + 16 * n), A("NC", 16 * l0, 16 * (l0 + n)), 0.0, OP.add, OP.min)
-            line.insert(len(line) - (c > 1), len(calls) - 1)
-            if c == 0 and CH[1][2] == "V":
-                line.append(got[1])
-            if c < 2:
-                line.append(got[2 + c])
+            tag("z%d" % l0)
             for a, m in halves:
                 mms([(A(ps, off + 16 * a, off + 16 * (a + m)), A("BB"), A("R", 16 * (l0 + a), 16 * (l0 + a + m)), False, False),
-                     (A(ps, off + 16 * a + 15, off + 16 * (a + m), 16), A("I"), A("BS", 256 + l0 + a, 256 + l0 + a + m), False, True)])
-            vtt(A("X", 16 * l0, 16 * l0 + 16 * n), A("D", d + 1, d + 1 + 16 * n), A(ps, off, off + 16 * n), OP.add)
-            if 1 < c < len(CH) - 2:
-                line.append(got[c + 2])
-            line.append(len(calls) - 1)
-            act(ind(nst, A("CU", 256 * t + l0, 256 * t + l0 + n)), A("X", 16 * l0, 16 * l0 + 16 * n), FN.Silu)
-        for a, b in zip(line, line[1:]):
-            calls[b]["after"].setdefault(a, False)
+                     (A(ps, off + 16 * a + 15, off + 16 * (a + m), 16), A("I"), A("BS", 256 + l0 + a, 256 + l0 + a + m), False, q == "V")]
+                    + [(A(ps, off + 16 * a, off + 16 * (a + m)), A("I"), A("D", d + 1 + 16 * a, d + 1 + 16 * (a + m)), False, True)] * (q == "S"))
+            if q == "V":
+                vtt(A("X", 16 * l0, 16 * l0 + 16 * n), A("D", d + 1, d + 1 + 16 * n), A(ps, off, off + 16 * n), OP.add)
+            else:
+                act(A("X", 16 * l0, 16 * l0 + 16 * n), A(ps, off, off + 16 * n), FN.Copy)
+            tag("x%d" % l0)
+            if t < TURN:
+                act(ind(nst, A("CU", 256 * t + l0, 256 * t + l0 + n)), A("X", 16 * l0, 16 * (l0 + n)), FN.Silu)
+        for a, n, q in BACK if t >= TURN else []:
+            o, i = A(N, 512 + 16 * a, 512 + 16 * (a + n)), ind(A("X"), A("IU%d" % (t % 2), a, a + n))
+            if q == "V":
+                vts(o, i, 0.0, OP.max)
+            else:
+                act(o, i, FN.Relu)
+                tag("K")
         mm(A("P6", 256, 512), A("B"), A("NC", 0, 4096, 16))
-        vts(A("NL", 256, 512), A("D", 1, 4096, 16), THR, OP.is_lt)
+        vts(A("NL", 256, 512), A("D", 16, 4112, 16), THR, OP.is_lt)
+        tag("ne")
         vts(A("NL", 0, 256), A("P6", 256, 512), MET, OP.is_ge)
+        tag("nn")
         if t < 3:
             mm(A("P4", 0, 256), A("B8"), A("ONE", 0, 256), True, False)
             mm(A("P4", 0, 256), A("I"), A("BS", 256, 512), False, False)
             mm(A("P4", 0, 256), A("I"), A("R", 15, 4096, 16), False, True)
+            tag("p")
             vts(A("RR"), A("P4", 0, 256), CAP, OP.min, -1.0 / 16, OP.mult)
             collect(A("P5", 0, 16), "ZB", lambda x: A("RR", x, 256, 16))
+            tag("q")
             vts(A("UL", 1, 17), A("P5", 0, 16), 0.5 - CAP, OP.is_gt)
+            tag("ul")
             mms([(A("P5", 16, 32), A("W3"), A("UL", 1, 17), True, False), (A("P5", 16, 32), A("UP"), A("UL", 0, 16), False, True),
                  (A("P5", 32, 48), A("IB"), A("UL", 1, 17), True, False), (A("P5", 32, 48), A("I"), A("KM"), False, True)])
-            slots = len(calls) - 1
+            tag("u")
             scan_(A("SP"), A("ON16"), A("P5", 16, 32), -1.0)
+            tag("sp")
             vtt(A("OF"), A("SP"), A("P5", 32, 48), OP.max)
+            tag("of")
             vcp(A("OU"), A("OF"))
+            tag("ou")
             vcp(ind(A("SW%d" % t), A("OU")), A("RR"))
+            tag("w")
             dst = T.cores[(rank + 1) % len(T.cores)]
             rid, pid = topo.addr(dst)[:2]
             sent = emit("G", lambda t=t, dst=dst, rid=rid, pid=pid: g.remote_dma(
                 out_ap=T["AV%d" % t][:, :], in_ap=T["SW%d" % t][:, 0:64], remote_sem=T.sem["arr%d" % t], local_sem=T.sem["loc%d" % t],
-                pid=pid, routing_id=rid, dma_engine_mask=topo.mask(core, dst)), [A("SW%d" % t, 0, 64)], [], 1.0, 6.0, "remote")
+                pid=pid, routing_id=rid, dma_engine_mask=topo.mask(core, dst)), [A("SW%d" % t, 0, 64)], [], 1.0, 12.0, "remote")
+            calls[sent]["after"][tags["rep"]] = False
         else:
             dma(T.ZF[:, :], T[N][0:128:16, 512:4608], [nst], [A("ZF")], 2.6)
             vts(A("EF"), A("ZF"), THR, OP.is_lt, 4095.0, OP.mult)
             vtt(A("YF"), A("OI"), A("EF"), OP.max)
-            dma(T.YR[0:128:16, 512:4608], T.YF[:, :], [A("YF")], [A("YR")], 2.6)
+            dma(T.INV0[0:128:16, 512:4608], T.YF[:, :], [A("YF")], [A("INV0")], 2.6)
             for l0, n, p, row in PART:
                 iota(A("VB", 2 * l0 + n, 2 * l0 + 2 * n), [[0, n]], 4095, 0)
 
         line = []
-        for l0, n in FG:
+        for k, (l0, n) in enumerate(FG):
             vtt(A("IN3", 16 * l0, 16 * (l0 + n)), ind(nst, A(clu, l0, l0 + n)), A("BRF", 16 * l0, 16 * (l0 + n)), OP.is_gt)
-            line.append(len(calls) - 1)
-        for l0, n, ps, off in SG3:
-            mm(A(ps, off, off + 16 * n), A("I"), A("ZZ", 0, 16 * n), True, False)
-            mms([(A(ps, off + i, off + 16 * n, 16), A("NI"), A("BT", l0, l0 + n), False, False) for i in range(16)])
-            if ps == "TA" and t < 3:
-                calls[-1]["after"].setdefault(slots, False)
-            ga = A("GA", 16 * (l0 - VL), 16 * (l0 - VL + n))
+            tag("c%d" % k)
+        for k, (l0, n, ps, off) in enumerate(SG3):
+            mms([(A(ps, off + i, off + 16 * n, 16), A("NI"), A("BT", l0, l0 + n), i == 0, False) for i in range(16)])
+            tag("h%d" % k)
+            ga = A("GA", 16 * l0, 16 * (l0 + n))
             act(ga, ind(nst, A(clu, l0, l0 + n)), FN.Copy)
+            tag("g%d" % k)
             mm(A(ps, off, off + 16 * n), A("I"), ga, False, True)
+            tag("a%d" % k)
             act(A("IN3", 16 * l0, 16 * (l0 + n)), A(ps, off, off + 16 * n), FN.Sign, -THR)
-        for e, (l0, n, p, row) in zip(eat, PART):
+            tag("s%d" % k)
+        for part, (l0, n, p, row) in enumerate(PART):
             y0, ny = l0 // 16, n // 16
             mm(A(p, 0, n), A("I"), A("OFFS", l0, l0 + n), True, False)
             mm(A(p, 0, n), A("IB"), A("NL", l0, l0 + n), False, False)
             mm(A(p, 0, n), A("IB"), A("NL", 256 + l0, 256 + l0 + n), False, False)
-            for a, m in CNT:
+            for k, (a, m) in enumerate(CNT):
                 if l0 <= a < l0 + n:
-                    mms([(A(p, a - l0, a - l0 + m), EX("ZB" if a < VL else "ZH", i), A("IN3", 16 * a + i, 16 * (a + m), 16), False,
-                          i == 15 and a + m == l0 + n) for i in range(16)])
-            f = A("FC", 2 * l0 + n, 2 * l0 + 2 * n)
-            if l0 + n < 256:
-                vts(f, A(p, 0, n), 0.0, OP.max)
+                    mms([(A(p, a - l0, a - l0 + m), EX("ZH", i), A("IN3", 16 * a + i, 16 * (a + m), 16), False, i == 15 and a + m == l0 + n)
+                         for i in range(16)])
+                    tag("n%d" % k)
+            f, sm = A("F", l0, l0 + n), A("FC", 2 * l0 + n, 2 * l0 + 2 * n)
+            if l0 + n < 256 or WHO[0] == "V":
+                vts(f, A(p, 0, n), 0.25, OP.is_ge)
+                tag("F%d" % part)
+                mm(A(p, 256, 256 + n), A("TRI"), f)
+                tag("t%d" % part)
+                vtt(sm, f, A(p, 256, 256 + n), OP.is_gt)
             else:
-                act(f, A(p, 0, n), FN.Relu)
-            mm(A(p, 256, 256 + n), A("TRI"), f)
-            vtt(A("SM", l0, l0 + n), f, A(p, 256, 256 + n), OP.is_gt)
-            vtt(A("FC", 2 * l0, 2 * l0 + n), A("SM", l0, l0 + n), A(clf, l0, l0 + n), OP.mult)
-            mm(A(row, 0, n), A("BH"), A("SM", l0, l0 + n), True, False)
+                mm(A(row, 256, 256 + n), A("TRN"), A("ONE", 0, n), True, False)
+                act(f, A(p, 0, n), FN.Sign, -0.25)
+                tag("F%d" % part)
+                mm(A(row, 256, 256 + n), A("TRM"), f, False, True)
+                tag("t%d" % part)
+                act(sm, A(row, 256, 256 + n), FN.Relu)
+            tag("S%d" % part)
+            vtt(A("FC", 2 * l0, 2 * l0 + n), sm, A(clf, l0, l0 + n), OP.mult)
+            tag("C%d" % part)
+            mm(A(row, 0, n), A("BH"), sm, True, False)
             mm(A(row, 0, n), A("B"), A("FC", 2 * l0, 2 * l0 + n), False, True)
+            tag("r%d" % part)
             collect(A(p, 448, 448 + 2 * ny), "ZB", lambda x: A("FC", 2 * l0 + x, 2 * l0 + 2 * n, 16))
-            act(A("CR", l0, l0 + n), A(row, 0, n), FN.Identity, 0.5)
-            mlu = A("MLU", y0, y0 + ny)
+            tag("l%d" % part)
+            if WHO[1 + part] == "V":
+                vts(A("CR", l0, l0 + n), A(row, 0, n), 0.5, OP.add)
+            else:
+                act(A("CR", l0, l0 + n), A(row, 0, n), FN.Identity, 0.5)
+            tag("R%d" % part)
+            mlu = A("MLU%d" % (t % 2), 2 * y0, 2 * y0 + ny)
             vts(mlu, A(p, 448, 448 + ny), 2048.0, OP.add)
-            w = n + 2
-            vts(A("E", e + n + 1, e + w * ny, w), A(p, 448 + ny, 448 + 2 * ny), 0.5, OP.is_lt, -64 * CAP, OP.mult)
+            vts(A("E", n + 1, EN, EW), A(p, 448 + ny, 448 + 2 * ny), 0.5, OP.is_lt, -64 * CAP, OP.mult)
             for y in range(ny):
-                vts(A("E", e + w * y, e + w * y + 16 * y + 16), A("CR", l0, l0 + 16 * y + 16), A(p, 448 + y, 449 + y), OP.is_equal)
+                vts(A("E", EW * y, EW * y + 16 * y + 16), A("CR", l0, l0 + 16 * y + 16), A(p, 448 + y, 449 + y), OP.is_equal)
+                tag("e%d%d" % (part, y))
                 line.append(len(calls) - 1)
-            scan_(A("EZ", e, e + w * ny), A("EM", e, e + w * ny), A("E", e, e + w * ny), 0.0)
+            scan_(A("EZ", EN * part, EN * part + EN), A("EM"), A("E"), 0.0)
             line.append(len(calls) - 1)
-            z = A("EZ", e + n + 1, e + w * ny, w)
+            tag("Z%d" % part)
+            z = A("EZ", EN * part + n + 1, EN * part + EN, EW)
             vtt(A("R3", 2 * y0, 2 * y0 + ny), A("KS", 16 * t + y0, 16 * t + y0 + ny), z, OP.min)
             vtt(A("R3", 2 * y0 + ny, 2 * y0 + 2 * ny), A(p, 448, 448 + ny), z, OP.min)
             vtt(A("R4", 2 * y0, 2 * y0 + 2 * ny), A("R3", 2 * y0, 2 * y0 + 2 * ny), A("KD", 2 * y0, 2 * y0 + 2 * ny), OP.max)
-            ofs = A("OFS", 2 * y0, 2 * y0 + 2 * ny)
+            ofs = A("OFS%d" % (t % 2), 2 * y0, 2 * y0 + 2 * ny)
             vts(ofs, A("R4", 2 * y0, 2 * y0 + 2 * ny), 2560.0, OP.add)
-            src = N if t < 3 else "YR"
-            act(A("VB", 2 * l0, 2 * l0 + n), ind(A(src, 512, 4608), mlu), FN.Copy)
-            if t < 3 and l0 + n < 256:
-                act(ind(A(src, 0, 4608), ofs), A("VB", 2 * l0, 2 * l0 + 2 * n), FN.Silu)
+            tag("o%d" % part)
+            src = N if t < 3 else "INV0"
+            if WHO[3 + part] == "V":
+                vcp(A("VB", 2 * l0, 2 * l0 + n), ind(A(src, 512, 4608), mlu))
+            else:
+                act(A("VB", 2 * l0, 2 * l0 + n), ind(A(src, 512, 4608), mlu), FN.Copy)
+            if t < 3 and part and SPLIT == 1:
+                act(ind(A(src, 0, 4608), A("OFS%d" % (t % 2), 0, y0)), A("VB", 0, l0), FN.Silu)
+            if t < 3 and l0 + n < 256 and SPLIT < 2:
+                h = ny if SPLIT else 0
+                act(ind(A(src, 0, 4608), A("OFS%d" % (t % 2), h, 2 * ny)), A("VB", 16 * h, 2 * n), FN.Silu)
             else:
                 vcp(ind(A(src, 0, 4608), ofs), A("VB", 2 * l0, 2 * l0 + 2 * n))
-            if t < 3:
-                act(A("OV", l0, l0 + n), ind(A("OO", 512, 4608), mlu), FN.Copy)
-                act(ind(A("OO"), A("OFS", 2 * y0, 2 * y0 + ny)), A("OV", l0, l0 + n), FN.Silu)
-        for a, b in zip(line, line[1:]):
-            calls[b]["after"].setdefault(a, False)
+        for u in ([], [0], [1, 2], [])[t]:
+            for l0, n, p, row in PART:
+                act(A("OV", l0, l0 + n), ind(A("OO", 512, 4608), A("MLU%d" % (u % 2), l0 // 8, l0 // 8 + n // 16)), FN.Copy)
+                if u < t and not l0:
+                    tag("m")
+            for l0, n, p, row in PART:
+                act(ind(A("OO"), A("OFS%d" % (u % 2), l0 // 8, l0 // 8 + n // 16)), A("OV", l0, l0 + n), FN.Silu)
         if t < 3:
             needs(t + 1)
-    dma(T.y[:, :], T.YR[0:128:16, 512:4608], [A("YR")], [], 2.6)
+        for order in [line] + [[tags[w] for w in x.split() if w in tags] for x in TAIL[t]]:
+            for a, b in zip(order, order[1:]):
+                calls[b]["after"].setdefault(a, False)
+    dma(T.y[:, :], T.INV0[0:128:16, 512:4608], [A("INV0")], [], 2.6)
     issue()
     for t in range(3):
         g.wait_ge(T.sem["loc%d" % t], len(topo.engines(core, T.cores[(rank + 1) % len(T.cores)])))

from concourse.mybir import AluOpType, ActivationFunctionType

OP = AluOpType
FN = ActivationFunctionType
MARK, THR, CAP = 15.0 / 64, 1.0 / 2048, 32768.0
MET = 16 * CAP - 8
GET = [(0, 24, "V"), (24, 40, "S"), (64, 32, "V"), (96, 32, "S"), (128, 64, "V"), (192, 64, "V")]
CH = [(0, 24, "TA", 0), (24, 40, "TB", 0), (64, 64, "TA", 0), (128, 64, "TB", 0), (192, 64, "TA", 0)]
GET2 = [(0, 32, "V"), (32, 32, "S"), (64, 64, "S"), (128, 64, "V"), (192, 64, "S")]
CH2 = [(0, 32, "TA", 0, "V"), (32, 32, "TA", 512, "V"), (64, 64, "TB", 0, "S"), (128, 64, "TA", 0, "V"), (192, 64, "TB", 0, "V")]
GET3 = [(0, 32, "V"), (32, 64, "S"), (96, 32, "V"), (128, 64, "S"), (192, 32, "V"), (224, 32, "S")]
CH3 = [(0, 32, "TA", 0, "V"), (32, 32, "TA", 512, "V"), (64, 32, "TB", 0, "S"), (96, 32, "TB", 512, "S"), (128, 32, "P4", 0, "V"),
       (160, 32, "P5", 0, "S"), (192, 32, "P7", 0, "S"), (224, 32, "TA", 0, "V")]
BACK = [(0, 128, "V"), (128, 128, "S")]
INV = [[(3, 0, 32, "V"), (3, 32, 32, "V"), (3, 64, 16, "S"), (3, 80, 16, "S")],
       [(3, 96, 32, "V"), (3, 128, 32, "V"), (3, 160, 16, "S"), (3, 176, 16, "S")],
       [(3, 192, 32, "V"), (3, 224, 16, "S"), (3, 240, 16, "S")], []]
TURN = 3
VR = [(0, 96), (128, 192)]
OWN = [0, 96, 192, 256]
FG = [(0, 64), (64, 32), (128, 64)]
SG3 = [(96, 32, "TB", 0), (192, 32, "TB", 512), (224, 32, "TA", 0)]
CNT = [(0, 64), (64, 64), (128, 64), (192, 64)]
PART = [(0, 128, "P6", "P7"), (128, 128, "P4", "P5")]
COST = (0.00083, 0.01, 0.24, 0.00042, 1.2, 2.4)
CYC, CALL, HOP, PE, GATHER, SCATTER = COST
VIEWS = [(1.0, 0.0, 0.0), (1.3, 0.4, 2.6)]
PASSES = 3
MOVES = 30000
SLACK = 0.0004
ORDER = {}
SPLIT = 1
WHO = "SSSSS"
LAST = [(0, 4), (4, 16)]
FILL = 4
TAIL = [[("x192 i3.%d c0" if q == "V" else "s2 i3.%d") % l for u, l, n, q in pieces] for pieces in INV[:3]] + [["b0 d32"]]
EW = 130
EN = 8 * EW

_sb = {
    "OLU": (256, "uint16"), "OCN": (256, "int32"), "OCH": (256, "float16"), "OL0": (32, "uint16"),
    "SK": (4112, "bfloat16"), "COV": (4096, "int32"), "CI": (1024, "int32"), "CU": (1024, "uint16"), "CF": (1024, "float16"), "CS": (1024, "uint16"),
    "ND": (768, "bfloat16"), "LS": (128, "uint16"), "KS": (64, "float32"),
    "WA": (4624, "float32"), "INV0": (4608, "float32"), "WB": (4624, "float32"), "IOTA": (4096, "float32"), "IL": (256, "float32"),
    "IU0": (256, "uint16"), "IU1": (256, "uint16"), "HI": (256, "int32"), "HF": (256, "bfloat16"), "I8": (128, "bfloat16"), "OO": (4608, "float32"),
    "ONE": (512, "bfloat16"), "I": (128, "bfloat16"), "NI": (128, "bfloat16"), "B": (128, "bfloat16"), "BB": (128, "bfloat16"), "CB": (128, "bfloat16"),
    "PX": (2048, "bfloat16"), "ZB": (144, "bfloat16"), "ZH": (144, "bfloat16"), "BH": (128, "bfloat16"), "PAT": (512, "bfloat16"),
    "Z0": (144, "bfloat16"), "Z15": (144, "bfloat16"), "G8": (8, "bfloat16"), "G15": (8, "bfloat16"), "S1": (128, "bfloat16"),
    "TRI": (128, "bfloat16"), "UP": (128, "bfloat16"), "UN": (128, "bfloat16"), "W3": (128, "bfloat16"), "IB": (128, "bfloat16"),
    "PI": (1, "int32"), "PA": (1, "int32"), "XC": (1, "float32"), "SC": (2, "float32"), "ZR": (16, "float32"), "XM": (16, "float32"), "LY": (32, "float32"),
    "KM": (16, "float16"), "KD": (32, "float32"), "ON16": (16, "float32"), "OFFS": (256, "bfloat16"),
    "D": (4112, "bfloat16"), "NC": (4096, "float16"), "R": (4096, "float16"),
    "X": (4096, "float32"), "RR": (256, "float16"), "UL": (17, "bfloat16"), "SP": (16, "float32"), "OF": (16, "float32"), "OU": (16, "uint16"),
    "BS": (512, "bfloat16"), "BT": (256, "float16"), "BRF": (4096, "float16"), "NL": (512, "bfloat16"),
    "CLF0": (256, "float16"), "CLU0": (256, "uint16"), "CLF1": (256, "float16"), "CLU1": (256, "uint16"),
    "IN3": (4096, "bfloat16"), "GA": (4096, "bfloat16"),
    "F": (256, "bfloat16"), "TRM": (128, "bfloat16"), "TRN": (128, "bfloat16"), "FC": (512, "float16"), "CR": (256, "float16"), "B8": (128, "bfloat16"),
    "E": (EN, "bfloat16"), "EM": (EN, "bfloat16"), "EZ": (2 * EN, "bfloat16"), "EX": (16, "bfloat16"),
    "R3": (32, "float32"), "R4": (32, "float32"), "OFS0": (32, "uint16"), "MLU0": (32, "uint16"), "OFS1": (32, "uint16"), "MLU1": (32, "uint16"),
    "VB": (512, "float32"), "OV": (256, "float32"),
    "ZF": (256, "float32"), "OFN": (256, "float32"), "OI": (256, "int32"), "EF": (256, "float32"), "YF": (256, "float32"),
}
SCRATCH = {k: ("sbuf", [128, n], d) for k, (n, d) in _sb.items()}
for _t in range(3):
    SCRATCH["SW%d" % _t] = ("sbuf", [128, 512], "int32")
    SCRATCH["AV%d" % _t] = ("sbuf", [128, 64], "int32")
SCRATCH["TA"] = ("psum", [128, 1024], "float32")
SCRATCH["TB"] = ("psum", [128, 1024], "float32")
for _t in range(4, 8):
    SCRATCH["P%d" % _t] = ("psum", [128, 512], "float32")
PS = ("TA", "TB", "P4", "P5", "P6", "P7")
SEMAPHORES = ["cV", "cS", "cT", "cG"] + ["arr%d" % t for t in range(3)] + ["loc%d" % t for t in range(3)] + ["d%d" % k for k in range(18)]


def issue_order(calls):
    n = len(calls)
    before = [[(p, calls[p]["lag"] + HOP if wait else 0.0) for p, wait in c["after"].items()] for c in calls]
    behind = [[] for c in calls]
    for k in range(n):
        for p, hop in before[k]:
            behind[p].append((k, hop))

    def place(rank, links, onward, backwards):
        end, left, ready, free = [0.0] * n, [len(x) for x in links], {}, {}
        can = [c["lag"] if backwards else 0.0 for c in calls]
        for k in range(n):
            if not left[k]:
                ready.setdefault(calls[k]["q"], []).append(k)
        for step in range(n):
            soon, q = min((max(free.get(q, 0.0), can[k]) + calls[k]["cost"], q) for q in ready for k in ready[q])
            at = free.get(q, 0.0)
            rivals = [k for k in ready[q] if max(at, can[k]) < soon or max(at, can[k]) + calls[k]["cost"] <= soon]
            k = max(rivals, key=lambda j: (rank[j], -j))
            ready[q].remove(k)
            end[k] = free[q] = max(at, can[k]) + calls[k]["cost"]
            for s, hop in onward[k]:
                can[s] = max(can[s], end[k] + hop)
                left[s] -= 1
                if not left[s]:
                    ready.setdefault(calls[s]["q"], []).append(s)
        return end

    way, left = [0.0] * n, [len(x) for x in behind]
    todo = [k for k in range(n) if not left[k]]
    for k in todo:
        way[k] = calls[k]["cost"] + max([way[s] + hop for s, hop in behind[k]] + [calls[k]["lag"]])
        for p, hop in before[k]:
            left[p] -= 1
            if not left[p]:
                todo.append(p)
    best = None
    for turn in range(PASSES):
        end = place(way, before, behind, False)
        span = max(end[k] + calls[k]["lag"] for k in range(n))
        if best is None or span < best[0]:
            best = (span, end)
        way = place(end, behind, before, True)
    end = best[1]
    return polish(calls, sorted(range(n), key=lambda j: (end[j] - calls[j]["cost"], j)))


def polish(calls, order):
    n = len(calls)
    queue, lag = [c["q"] for c in calls], [c["lag"] for c in calls]
    behind = [[] for c in calls]
    for k, c in enumerate(calls):
        for p in c["after"]:
            behind[p].append(k)
    views = []
    for slow, gather, scatter in VIEWS:
        views.append([slow * (c["cost"] + CYC * (gather * c["gathered"] + scatter * c["scattered"])) for c in calls])
    before = [[(p, lag[p] + HOP if wait else 0.0) for p, wait in c["after"].items()] for c in calls]

    def run(order, cost, first, end, why):
        end, why, free, last = list(end), list(why), {q: 0.0 for q in queue}, {q: -1 for q in queue}
        for k in order[:first]:
            last[queue[k]] = k
        for q, k in last.items():
            free[q] = end[k] if k >= 0 else 0.0
        for k in order[first:]:
            q = queue[k]
            at, by = free[q], last[q]
            for p, hop in before[k]:
                if end[p] + hop > at:
                    at, by = end[p] + hop, p
            end[k] = free[q] = at + cost[k]
            why[k], last[q] = by, k
        return end, why, max(end[k] + lag[k] for k in order[-40:])

    now = [run(order, cost, 0, [0.0] * n, [-1] * n) for cost in views]
    unit = [r[2] for r in now]
    seed, fresh, best = 1, True, (len(views), order)
    mark = best[0]
    for turn in range(MOVES):
        if fresh:
            pos = {k: i for i, k in enumerate(order)}
            pairs = []
            for end, why, span in now:
                k = max(order[-40:], key=lambda j: end[j] + lag[j])
                while k >= 0:
                    u = why[k]
                    if u >= 0 and queue[u] == queue[k] and u not in calls[k]["after"]:
                        pairs.append((u, k))
                    k = u
            fresh = False
        seed = seed * 6364136223846793005 % (1 << 64) + 1442695040888963407
        a, b, c = (seed >> 20) % 10, (seed >> 24) % 65536, (seed >> 40) % 65536
        u, v = pairs[b % len(pairs)]
        i, j = pos[u], pos[v]
        if a < 4:
            need = {v}
            for k in reversed(order[i:j + 1]):
                if k in need:
                    need.update(p for p in calls[k]["after"] if pos[p] >= i)
            if u in need:
                continue
            first, new = i, order[:i] + [k for k in order[i:j + 1] if k in need] + [k for k in order[i:j + 1] if k not in need] + order[j + 1:]
        elif a < 7:
            same = [x for x in range(i + 1, min([pos[s] for s in behind[u]] + [n, i + 200])) if queue[order[x]] == queue[u]]
            if not same:
                continue
            x = same[c % len(same)]
            first, new = i, order[:i] + order[i + 1:x + 1] + [u] + order[x + 1:]
        else:
            same = [x for x in range(max([pos[p] + 1 for p in calls[u]["after"]] + [0, i - 200]), i) if queue[order[x]] == queue[u]]
            if not same:
                continue
            first = same[c % len(same)]
            new = order[:first] + [u] + order[first:i] + order[i + 1:]
        then = [run(new, cost, first, r[0], r[1]) for cost, r in zip(views, now)]
        score = sum(r[2] / z for r, z in zip(then, unit))
        if score <= mark + SLACK * (1 - turn / MOVES):
            end, cost = then[0][0], views[0]
            order, now, mark, fresh = sorted(new, key=lambda k: end[k] - cost[k]), then, score, True
            if mark < best[0]:
                best = (mark, order)
    return best[1]


def rank_program(g, core, T, topo):
    rank = T.rank_of(core)
    if rank is None:
        return
    queues = {"V": g.vector, "S": g.scalar, "T": g.tensor, "G": g, "Y": g.sync}
    calls = []
    log = {}

    def A(name, a=0, b=None, s=1):
        n = SCRATCH[name][1][1]
        b = n if b is None else b
        ap = T[name][:, a:b] if s == 1 else T[name][:, a:b:s]
        return (ap, [(name, a, b, s)], len(range(a, b, s)), False)

    def ind(win, off):
        return (win[0].indirect(off[0]), win[1] + off[1], 16 * off[2], True)

    def keys(name, a, b, s=1):
        if name in PS:
            return [("%s.%d" % (name, k), 0, 512, 1, True) for k in range(a // 512, (b - 1) // 512 + 1)]
        return [(name, a, b, s, False)]

    def apart(a, b, s, x, y, z):
        if s == 1 or z == 1:
            lo, hi, at, step = (a, b, x, z) if s == 1 else (x, y, a, s)
            return max(a, x) >= min(b, y) or at + max(0, -((at - lo) // step)) * step >= min(b, y)
        return x >= b or y <= a or (s == z and (a - x) % s != 0)

    def emit(q, fn, reads, writes, cost, lag=0.0, kind="compute", after=()):
        me, dep = len(calls), {p: True for p in after}
        for ops, w in ((reads, False), (writes, True)):
            for o in ops:
                for region in o[1]:
                    for key, lo, hi, st, bank in keys(*region):
                        keep = []
                        for r in log.get(key, []):
                            x, y, z, p, pq, pw = r
                            if p != me and not apart(lo, hi, st, x, y, z) and (pw or w or (bank and pq != q)):
                                if bank and pq == q == "T":
                                    dep.setdefault(p, False)
                                else:
                                    dep[p] = True
                                if w and lo <= x and y <= hi and (st == 1 or st == z):
                                    continue
                            keep.append(r)
                        keep.append((lo, hi, st, me, q, w))
                        log[key] = keep
        calls.append({"scattered": writes[0][2] if writes and writes[0][3] else 0, "gathered": reads[0][2] if reads and reads[0][3] else 0, "q": q, "fn": fn, "after": dep, "cost": cost, "lag": lag, "kind": kind})
        return me

    def issue():
        count = {"cV": 0, "cS": 0, "cT": 0, "cG": 0}
        known = {q: {} for q in queues}
        clocks, event, nd = {}, {}, [0]

        def need(q, ev):
            if known[q].get(ev[0], 0) >= ev[1]:
                return
            queues[q].wait_ge(T.sem[ev[0]], ev[1])
            k = known[q]
            for s, v in list(clocks.get(ev, {}).items()) + [ev]:
                k[s] = max(k.get(s, 0), v)

        if len(calls) not in ORDER:
            ORDER[len(calls)] = issue_order(calls)
        for k in ORDER[len(calls)]:
            c = calls[k]
            q = c["q"]
            if c["kind"] == "arrival":
                event[k] = c["fn"]
                continue
            want = {}
            for p, hop in c["after"].items():
                if hop and p in event:
                    want[event[p][0]] = max(want.get(event[p][0], 0), event[p][1])
            for s, v in sorted(want.items(), key=lambda e: -e[1]):
                need(q, (s, v))
            inst = c["fn"]()
            if c["kind"] == "remote":
                continue
            if c["kind"] == "dma":
                ev = ("d%d" % nd[0], 16)
                nd[0] += 1
                inst.then_inc(T.sem[ev[0]], 16)
            else:
                count["c" + q] += 1
                ev = ("c" + q, count["c" + q])
                inst.then_inc(T.sem[ev[0]], 1)
            event[k] = ev
            clocks[ev] = dict(known[q])
        for k in range(nd[0]):
            need("Y", ("d%d" % k, 16))
        for s in count:
            need("G", (s, count[s]))

    def dma(out, in_, reads, writes, lag, after=()):
        return emit("Y", lambda: g.sync.dma_start(out, in_), reads, writes, 0.05, lag, "dma", after)

    V, S, TE = g.vector, g.scalar, g.tensor

    def cost(out, ins, rate=None):
        if out[3] or (ins and ins[0][3]):
            return 0.06 + out[2] * (SCATTER if out[3] else GATHER) * CYC
        if rate is None:
            rate = 0.5 if all(SCRATCH[o[1][0][0]][2] in ("bfloat16", "float16", "uint16") for o in [out] + ins) else 1.0
        return CALL + max(64, out[2] * rate) * CYC

    def vts(out, i, s1, op0, s2=None, op1=None):
        rd = [i] + [s for s in (s1, s2) if isinstance(s, tuple)]
        a1 = s1[0] if isinstance(s1, tuple) else s1
        a2 = s2[0] if isinstance(s2, tuple) else s2
        if op1 is None:
            emit("V", lambda: V.tensor_scalar(out[0], i[0], a1, None, op0), rd, [out], cost(out, [i]))
        else:
            emit("V", lambda: V.tensor_scalar(out[0], i[0], a1, a2, op0, op1), rd, [out], cost(out, [i]))

    def vtt(out, i, j, op):
        emit("V", lambda: V.tensor_tensor(out[0], i[0], j[0], op), [i, j], [out], cost(out, [i, j], 1.0))

    def vcp(out, i):
        emit("V", lambda: V.tensor_copy(out[0], i[0]), [i], [out], cost(out, [i]))

    def vms(out, c):
        emit("V", lambda: V.memset(out[0], c), [], [out], cost(out, []))

    def scan_(out, m, d, first, op0=OP.mult, op1=OP.add):
        emit("V", lambda: V.tensor_tensor_scan(out[0], m[0], d[0], first, op0, op1), [m, d], [out], cost(out, [m, d]))

    def act(out, i, fn, bias=0.0, scale=1.0, more=0.0):
        if bias == 0.0 and scale == 1.0:
            emit("S", lambda: S.activation(out[0], i[0], fn), [i], [out], cost(out, [i], 1.0) + more)
        else:
            emit("S", lambda: S.activation(out[0], i[0], fn, bias=bias, scale=scale), [i], [out], cost(out, [i], 1.0) + more)

    def mms(group):
        emit("T", lambda: [TE.matmul(o[0], l[0], r[0], start, stop) for o, l, r, start, stop in group][-1],
             [x for m in group for x in m[1:3]], [m[0] for m in group], sum(0.005 + max(64, m[2][2]) * PE for m in group))

    def mm(out, l, r, start=True, stop=True):
        mms([(out, l, r, start, stop)])

    def sel(out, i, pattern, op, fill, base, mult):
        emit("G", lambda: g.affine_select(out[0], i[0], pattern, op, fill, base, mult), [i], [out], 0.17 + 2 * out[2] * CYC)

    def gcp(out, i, n):
        sel(out, i, [[0, n]], OP.is_ge, 0.0, 0, 0)

    def iota(out, pattern, base, mult, small=True):
        if small:
            emit("G", lambda: g.iota(out[0], pattern, base, mult, allow_small_or_imprecise_dtypes=True), [], [out], 0.13 + 2 * out[2] * CYC)
        else:
            emit("G", lambda: g.iota(out[0], pattern, base, mult), [], [out], 0.13 + 2 * out[2] * CYC)

    def EX(name, x):
        return A(name, 15 - x, 143 - x)

    def collect(out, name, rhs, n=16):
        mms([(out, EX(name, x), rhs(x), x == 0, x == n - 1) for x in range(n)])

    d0 = dma(T.OCN[:, :], T.occ[:, :], [], [A("OCN")], 2.6)
    d1 = dma(T.CI[:, 0:256], T.cards[:, 0:256], [], [A("CI", 0, 256)], 3.2)
    d3 = dma(T.ND[:, 0:192], T.need[:, 0:192], [], [A("ND", 0, 192)], 3.5)
    d2 = dma(T.SK[:, 0:4096], T.skill[:, :], [], [A("SK", 0, 4096)], 8.6)
    d4 = dma(T.COV[:, :], T.cover[:, :], [], [A("COV")], 12.5, [d2])
    u, v = TURN, 5 - TURN
    d7 = dma(T.CI[:, 256 * u:256 * u + 256], T.cards[:, 256 * u:256 * u + 256], [], [A("CI", 256 * u, 256 * u + 256)], 9.3)
    d5 = dma(T.CI[:, 256:512], T.cards[:, 256:512], [], [A("CI", 256, 512)], 13.5, [d2])
    d6 = dma(T.ND[:, 192:768], T.need[:, 192:768], [], [A("ND", 192, 768)], 14.2, [d2])
    d8 = dma(T.CI[:, 256 * v:256 * v + 256], T.cards[:, 256 * v:256 * v + 256], [], [A("CI", 256 * v, 256 * v + 256)], 15.0, [d2])
    for a, b in ((d0, d1), (d1, d3), (d3, d2), (d2, d7), (d7, d4), (d4, d5), (d5, d6), (d6, d8)):
        calls[b]["after"].setdefault(a, False)

    vms(A("ONE"), 1.0)
    iota(A("PI"), [[0, 1]], 0, 1, False)
    iota(A("ZR"), [[1, 16]], 0, 0)
    sel(A("UN"), A("ONE", 0, 128), [[-16, 8], [0, 16]], OP.is_ge, 0.0, 0, 1)
    sel(A("B"), A("UN"), [[16, 8], [0, 16]], OP.is_ge, 0.0, 15, -1)
    sel(A("G8"), A("ONE", 0, 8), [[-16, 8]], OP.is_equal, 0.0, 0, 1)
    for k in range(FILL):
        act(A("NC", 512 * k, 512 * k + 512), A("ONE"), FN.Silu, 0.0, CAP, 0.0 if k else 1.3)
    for k in range(FILL, 8):
        vms(A("NC", 512 * k, 512 * k + 512), CAP)
    for k in range(2):
        iota(A("IOTA", 1024 * k, 1024 * k + 1024), [[1, 1024]], 32 + 1024 * k, 0)
    for z in ("Z0", "ZB", "Z15"):
        vms(A(z), 0.0)
    vts(A("PA"), A("PI"), 15, OP.bitwise_and)
    vms(A("D", 0, 16), 2 * CAP)
    vcp(A("XC"), A("PA"))
    vms(A("SK", 4096, 4112), CAP / 8)
    vts(A("XM"), A("ZR"), A("XC"), OP.is_equal)
    vcp(A("Z0", 15, 143, 16), A("G8"))
    for x in range(16):
        vts(A("PX", 128 * x, 128 * x + 128), A("B"), A("XM", x, x + 1), OP.mult)
    sel(A("I"), A("ONE", 0, 128), [[-1, 128]], OP.is_equal, 0.0, 0, 1)
    sel(A("PAT"), A("ONE"), [[0, 32], [1, 16]], OP.is_equal, 0.0, -15, 0)
    iota(A("LY"), [[16, 32]], 0, 0)
    sel(A("G15"), A("ONE", 0, 8), [[-16, 8]], OP.is_equal, 0.0, -15, 1)
    iota(A("WA", 4608, 4624), [[0, 16]], int(2 * CAP), 0)
    iota(A("WB", 4608, 4624), [[0, 16]], int(2 * CAP), 0)
    vts(A("I8"), A("I"), 256.0, OP.mult)
    sel(A("UP"), A("B"), [[-1, 128]], OP.is_gt, 0.0, 0, 1)
    sel(A("TRI"), A("B"), [[1, 128]], OP.is_gt, 0.0, 0, -1)
    for l0, n, p, row in PART:
        iota(A("VB", 2 * l0 + n, 2 * l0 + 2 * n), [[0, n]], 0, 0)
    iota(A("ON16"), [[0, 16]], 1, 0)
    iota(A("UL"), [[0, 17]], 0, 0)
    iota(A("OFFS"), [[0, 256]], 0, 0)
    for a, b in VR:
        iota(A("OFFS", a, b), [[0, b - a]], -4, 0)
    for t in range(3):
        iota(A("SW%d" % t, 0, 64), [[0, 64]], -2048, 0, False)
    vts(A("SC", 0, 1), A("XM", 15, 16), 2048.0, OP.mult, 2048.0, OP.add)
    vts(A("SC", 1, 2), A("XM", 15, 16), -1.0, OP.mult, 1.0, OP.add)
    vts(A("CB"), A("B"), A("XM", 0, 1), OP.mult, -2 * CAP, OP.mult)
    vts(A("S1"), A("B"), A("XM", 1, 2), OP.mult, -16384 * CAP, OP.mult)
    vts(A("PAT"), A("PAT"), A("XM", 1, 2), OP.max)
    vts(A("BB"), A("B"), 1024.0, OP.mult)
    vtt(A("CB"), A("CB"), A("S1"), OP.add)
    vcp(A("ZB", 15, 143, 16), A("B", 0, 128, 16))
    vcp(A("Z15", 15, 143, 16), A("G15"))
    vts(A("KD"), A("LY"), A("XC"), OP.add, -2560.0, OP.add)
    vts(A("ZH"), A("ZB"), 0.5, OP.mult)
    vts(A("BH"), A("B"), -0.5, OP.mult)
    vts(A("KM"), A("KD", 0, 16), 2816.0, OP.add)
    vtt(A("TRM"), A("I"), A("TRI"), OP.subtract)
    vts(A("TRN"), A("TRI"), -1.0, OP.mult)
    vts(A("B8"), A("B"), -0.125, OP.mult)
    vts(A("NI"), A("I"), -1.0, OP.mult)
    vts(A("IB"), A("I"), -2048.0, OP.mult)
    vtt(A("W3"), A("B"), A("UP"), OP.subtract)
    vts(A("EX"), A("XM"), -1024.0, OP.mult, 1.0, OP.add)
    iota(A("EM"), [[0, EN]], 1, 0)
    vms(A("E"), 0.0)
    for y in range(8):
        gcp(A("EM", (EW + 16) * y, (EW + 16) * y + 16), A("EX"), 16)
    iota(A("EM", 0, EN, EW), [[0, 8]], 0, 0)
    iota(A("EM", 128, EN, EW), [[0, 8]], 8192, 0)
    iota(A("E", 128, EN, EW), [[0, 8]], -4096, 0)
    early = [k for k, c in enumerate(calls) if c["q"] == "G"]
    for k in range(2, 4):
        iota(A("IOTA", 1024 * k, 1024 * k + 1024), [[1, 1024]], 32 + 1024 * k, 0)
    iota(A("INV0", 4096, 4608), [[0, 512]], 0, 0)
    vts(A("OCH"), A("OCN"), -2048.0, OP.add)
    vcp(A("CU", 0, 256), A("CI", 0, 256))
    banks = (("P6", 0), ("P7", 0), ("TA", 0), ("TA", 512), ("TB", 0), ("TB", 512), ("P4", 0), ("P5", 0))
    for k in range(8):
        ps, c = banks[k]
        mms([(A(ps, c + 256 * h, c + 256 * h + 256), A("PX", 256 * k + 128 * h, 256 * k + 128 * h + 128), A("OCH"), True, True) for h in range(2)])
        if k:
            calls[-1]["after"].setdefault(len(calls) - 3, False)
        o = A("OO", 512 + 512 * k, 1024 + 512 * k)
        if k % 2 == 0:
            vts(o, A(ps, c, c + 512), 2080.0, OP.add)
        else:
            act(o, A(ps, c, c + 512), FN.Identity, 2080.0)
    for k in range(4):
        o, i = A("BRF", 1024 * k, 1024 * k + 1024), ind(A("OO", 512, 4608), A("CU", 64 * k, 64 * k + 64))
        if k % 2 == 0:
            vts(o, i, -2080.0, OP.add)
        else:
            act(o, i, FN.Identity, -2080.0)
    for k in range(4):
        collect(A("P%d" % (4 + k), 0, 64), "Z0", lambda x: A("BRF", 1024 * k + x, 1024 * k + 1024, 16), 15)
        vts(A("OLU", 64 * k, 64 * k + 64), A("P%d" % (4 + k), 0, 64), A("SC", 0, 1), OP.add)
    for h, (a, b) in enumerate(LAST):
        collect(A("TB", 512 * h, 512 * h + b - a), "Z0", lambda x: A("BRF", 256 * a + 16 * x + 15, 256 * b, 256))
        vts(A("OL0", 16 + a, 16 + b), A("TB", 512 * h, 512 * h + b - a), 2048.0, OP.add)
    vms(A("SK", 4095, 4096), -MARK / 16)

    def cards(t):
        a, b = 256 * t, 256 * t + 256
        collect(A("P7", 256, 272), "Z0", lambda x: A("CF", a + x, b, 16))
        tag("k0")
        if t:
            collect(A("P7", 272, 288), "Z15", lambda x: A("CF", a + x, b, 16))
            tag("k1")
            if t < TURN:
                vts(A("CU", a, b), A("CF", a, b), 2048.0, OP.add)
            vts(A("CS", a, b), A("CF", a, b), A("SC", 1, 2), OP.mult, A("SC", 0, 1), OP.add)
            tag("cs")
            vts(A("LS", 32 * t, 32 * t + 32), A("P7", 256, 288), 2048.0, OP.add)
            tag("ls")
        else:
            vts(A("LS", 0, 16), A("P7", 256, 272), 2048.0, OP.add)
        vcp(A("KS", 16 * t, 16 * t + 16), A("P7", 256, 272))
        tag("ks")

    def turned(t):
        a, b = 256 * t, 256 * t + 256
        vts(A("HI"), A("CI", a, b), 4, OP.arith_shift_right)
        act(A("HF"), A("HI"), FN.Copy)
        mms([(A("P7", 0, 256), A("I8"), A("CF", a, b), True, False), (A("P7", 0, 256), A("I"), A("HF"), False, False),
             (A("P7", 0, 256), A("IB"), A("HF"), False, False), (A("P7", 0, 256), A("IB"), A("HF"), False, True)])
        vts(A("CU", a, b), A("P7", 0, 256), 524288.0, OP.add)

    def places(t, l0, n, q):
        name = ("INV0", "WA")[t - 2] if TURN == 2 else "WA" if False else "INV0"
        row = A(name, 0, 4096)
        o, i = ind(row, A("CU", 256 * t + l0, 256 * t + l0 + n)), A("IOTA", 16 * l0, 16 * (l0 + n))
        if q == "V":
            vcp(o, i)
        else:
            act(o, i, FN.Silu)
        tag("i%d.%d" % (t, l0))
        if l0 + n == 256:
            dma(T.IL[:, :], T[name][0:128:16, 0:4096], [row], [A("IL")], 3.0)
            vts(A("IU%d" % (t % 2)), A("IL"), -31.75, OP.add)

    def numbers(t):
        act(A("CF", 256 * t, 256 * t + 256), A("CI", 256 * t, 256 * t + 256), FN.Identity, -2048.0)
        tag("cf")

    def covers(t):
        act(A("CLF%d" % (t % 2)), ind(A("COV"), A("LS", 32 * t, 32 * t + 16)), FN.Identity, -2048.0)
        tag("cl")

    def needs(t):
        act(A("NC", 0, 3072, 16), A("ND", 192 * t, 192 * t + 192), FN.Identity, CAP, -16.0)
        tag("nd")

    tags = {}

    def tag(name):
        tags[name] = len(calls) - 1

    needs(0)
    numbers(0)
    cards(0)
    covers(0)
    for t in range(1, 4):
        numbers(t)
    turned(TURN)
    sent = None
    for t in range(4):
        W, N = (("WA", "WA"), ("WA", "WB"), ("WB", "WB" if TURN == 2 else "WA"), ("WB", "WB") if TURN == 2 else ("WA", "WA"))[t]
        wst, nst = A(W, 512, 4624), A(N, 512, 4608)
        clf, clu = "CLF%d" % (t % 2), "CLU%d" % (t % 2)
        tags.clear()
        vts(A(clu), A(clf), 2048.0, OP.add)
        tag("cv")

        def fetch(o, lst, q):
            if t == 0 and q == "V":
                vts(o, ind(A("SK"), lst), 16.0, OP.mult, MARK, OP.add)
            elif t == 0:
                act(o, ind(A("SK"), lst), FN.Identity, MARK, 16.0)
            elif q == "V":
                vcp(o, ind(wst, lst))
            else:
                act(o, ind(wst, lst), FN.Copy)

        if t == 3:
            dma(T.OFN[:, :], T.OO[0:128:16, 512:4608], [A("OO", 512, 4608)], [A("OFN")], 2.6)
            vts(A("OI"), A("OFN"), -32.0, OP.add)
        else:
            cards(t + 1)
            covers(t + 1)
            if t == 1 and TURN == 2:
                turned(3)
        lst, at = ("LS", 32 * t) if t else ("OL0", 0)
        for h, (a, b) in enumerate(LAST):
            fetch(A("BS", 256 + 16 * a, 256 + 16 * b), A(lst, at + 16 + a, at + 16 + b), "S")
            tag("b%d" % h)
        if t:
            av = A("AV%d" % (t - 1))
            emit("N", ("arr%d" % (t - 1), len(topo.engines(T.cores[rank - 1], core))), [], [av], 0.0, 0.0, "arrival", [sent])
            vts(A("NC", 3072, 4096, 16), av, -16.0, OP.mult)
            tag("av")
        for l0, n, q in GET if t < TURN else (GET2, GET3)[t - 2]:
            fetch(A("D", 16 * (l0 + 1), 16 * (l0 + n + 1)), A("CS", 256 * t + l0, 256 * t + l0 + n) if t else A("OLU", l0, l0 + n), q)
            tag("d%d" % l0)
        for a, b in zip(OWN, OWN[1:]):
            vts(A("BT", a, b), A("D", 16 * a + 16, 16 * b + 16, 16), -8.0, OP.add, 0.0, OP.max)
            tag("B%d" % a)
        for a, b in VR:
            for i in range(16):
                gcp(A("BRF", 16 * a + i, 16 * b, 16), A("BT", a, b), b - a)
                for k in [len(calls) - 2] if a + i else early:
                    calls[-1]["after"].setdefault(k, False)
        tag("rep")
        for piece in INV[t]:
            places(*piece)
        for l0, n, ps, off, q in [c + ("V",) for c in CH] if t < TURN else (CH2, CH3)[t - 2]:
            d = 16 * l0 + 15
            halves = [(a, min(32, n - a)) for a in range(0, n, 32)]
            for a, m in halves:
                mm(A(ps, off + 16 * a, off + 16 * (a + m)), A("CB"), A("PAT", 0, 16 * m), True, False)
            scan_(A("R", 16 * l0, 16 * (l0 + n)), A("D", d, d + 16 * n), A("NC", 16 * l0, 16 * (l0 + n)), 0.0, OP.add, OP.min)
            tag("z%d" % l0)
            for a, m in halves:
                mms([(A(ps, off + 16 * a, off + 16 * (a + m)), A("BB"), A("R", 16 * (l0 + a), 16 * (l0 + a + m)), False, False),
                     (A(ps, off + 16 * a + 15, off + 16 * (a + m), 16), A("I"), A("BS", 256 + l0 + a, 256 + l0 + a + m), False, q == "V")]
                    + [(A(ps, off + 16 * a, off + 16 * (a + m)), A("I"), A("D", d + 1 + 16 * a, d + 1 + 16 * (a + m)), False, True)] * (q == "S"))
            if q == "V":
                vtt(A("X", 16 * l0, 16 * l0 + 16 * n), A("D", d + 1, d + 1 + 16 * n), A(ps, off, off + 16 * n), OP.add)
            else:
                act(A("X", 16 * l0, 16 * l0 + 16 * n), A(ps, off, off + 16 * n), FN.Copy)
            tag("x%d" % l0)
            if t < TURN:
                act(ind(nst, A("CU", 256 * t + l0, 256 * t + l0 + n)), A("X", 16 * l0, 16 * (l0 + n)), FN.Silu)
        for a, n, q in BACK if t >= TURN else []:
            o, i = A(N, 512 + 16 * a, 512 + 16 * (a + n)), ind(A("X"), A("IU%d" % (t % 2), a, a + n))
            if q == "V":
                vts(o, i, 0.0, OP.max)
            else:
                act(o, i, FN.Relu)
                tag("K")
        mm(A("P6", 256, 512), A("B"), A("NC", 0, 4096, 16))
        vts(A("NL", 256, 512), A("D", 16, 4112, 16), THR, OP.is_lt)
        tag("ne")
        vts(A("NL", 0, 256), A("P6", 256, 512), MET, OP.is_ge)
        tag("nn")
        if t < 3:
            mm(A("P4", 0, 256), A("B8"), A("ONE", 0, 256), True, False)
            mm(A("P4", 0, 256), A("I"), A("BS", 256, 512), False, False)
            mm(A("P4", 0, 256), A("I"), A("R", 15, 4096, 16), False, True)
            tag("p")
            vts(A("RR"), A("P4", 0, 256), CAP, OP.min, -1.0 / 16, OP.mult)
            collect(A("P5", 0, 16), "ZB", lambda x: A("RR", x, 256, 16))
            tag("q")
            vts(A("UL", 1, 17), A("P5", 0, 16), 0.5 - CAP, OP.is_gt)
            tag("ul")
            mms([(A("P5", 16, 32), A("W3"), A("UL", 1, 17), True, False), (A("P5", 16, 32), A("UP"), A("UL", 0, 16), False, True),
                 (A("P5", 32, 48), A("IB"), A("UL", 1, 17), True, False), (A("P5", 32, 48), A("I"), A("KM"), False, True)])
            tag("u")
            scan_(A("SP"), A("ON16"), A("P5", 16, 32), -1.0)
            tag("sp")
            vtt(A("OF"), A("SP"), A("P5", 32, 48), OP.max)
            tag("of")
            vcp(A("OU"), A("OF"))
            tag("ou")
            vcp(ind(A("SW%d" % t), A("OU")), A("RR"))
            tag("w")
            dst = T.cores[(rank + 1) % len(T.cores)]
            rid, pid = topo.addr(dst)[:2]
            sent = emit("G", lambda t=t, dst=dst, rid=rid, pid=pid: g.remote_dma(
                out_ap=T["AV%d" % t][:, :], in_ap=T["SW%d" % t][:, 0:64], remote_sem=T.sem["arr%d" % t], local_sem=T.sem["loc%d" % t],
                pid=pid, routing_id=rid, dma_engine_mask=topo.mask(core, dst)), [A("SW%d" % t, 0, 64)], [], 1.0, 12.0, "remote")
            calls[sent]["after"][tags["rep"]] = False
        else:
            dma(T.ZF[:, :], T[N][0:128:16, 512:4608], [nst], [A("ZF")], 2.6)
            vts(A("EF"), A("ZF"), THR, OP.is_lt, 4095.0, OP.mult)
            vtt(A("YF"), A("OI"), A("EF"), OP.max)
            dma(T.INV0[0:128:16, 512:4608], T.YF[:, :], [A("YF")], [A("INV0")], 2.6)
            for l0, n, p, row in PART:
                iota(A("VB", 2 * l0 + n, 2 * l0 + 2 * n), [[0, n]], 4095, 0)

        line = []
        for k, (l0, n) in enumerate(FG):
            vtt(A("IN3", 16 * l0, 16 * (l0 + n)), ind(nst, A(clu, l0, l0 + n)), A("BRF", 16 * l0, 16 * (l0 + n)), OP.is_gt)
            tag("c%d" % k)
        for k, (l0, n, ps, off) in enumerate(SG3):
            mms([(A(ps, off + i, off + 16 * n, 16), A("NI"), A("BT", l0, l0 + n), i == 0, False) for i in range(16)])
            tag("h%d" % k)
            ga = A("GA", 16 * l0, 16 * (l0 + n))
            act(ga, ind(nst, A(clu, l0, l0 + n)), FN.Copy)
            tag("g%d" % k)
            mm(A(ps, off, off + 16 * n), A("I"), ga, False, True)
            tag("a%d" % k)
            act(A("IN3", 16 * l0, 16 * (l0 + n)), A(ps, off, off + 16 * n), FN.Sign, -THR)
            tag("s%d" % k)
        for part, (l0, n, p, row) in enumerate(PART):
            y0, ny = l0 // 16, n // 16
            mm(A(p, 0, n), A("I"), A("OFFS", l0, l0 + n), True, False)
            mm(A(p, 0, n), A("IB"), A("NL", l0, l0 + n), False, False)
            mm(A(p, 0, n), A("IB"), A("NL", 256 + l0, 256 + l0 + n), False, False)
            for k, (a, m) in enumerate(CNT):
                if l0 <= a < l0 + n:
                    mms([(A(p, a - l0, a - l0 + m), EX("ZH", i), A("IN3", 16 * a + i, 16 * (a + m), 16), False, i == 15 and a + m == l0 + n)
                         for i in range(16)])
                    tag("n%d" % k)
            f, sm = A("F", l0, l0 + n), A("FC", 2 * l0 + n, 2 * l0 + 2 * n)
            if l0 + n < 256 or WHO[0] == "V":
                vts(f, A(p, 0, n), 0.25, OP.is_ge)
                tag("F%d" % part)
                mm(A(p, 256, 256 + n), A("TRI"), f)
                tag("t%d" % part)
                vtt(sm, f, A(p, 256, 256 + n), OP.is_gt)
            else:
                mm(A(row, 256, 256 + n), A("TRN"), A("ONE", 0, n), True, False)
                act(f, A(p, 0, n), FN.Sign, -0.25)
                tag("F%d" % part)
                mm(A(row, 256, 256 + n), A("TRM"), f, False, True)
                tag("t%d" % part)
                act(sm, A(row, 256, 256 + n), FN.Relu)
            tag("S%d" % part)
            vtt(A("FC", 2 * l0, 2 * l0 + n), sm, A(clf, l0, l0 + n), OP.mult)
            tag("C%d" % part)
            mm(A(row, 0, n), A("BH"), sm, True, False)
            mm(A(row, 0, n), A("B"), A("FC", 2 * l0, 2 * l0 + n), False, True)
            tag("r%d" % part)
            collect(A(p, 448, 448 + 2 * ny), "ZB", lambda x: A("FC", 2 * l0 + x, 2 * l0 + 2 * n, 16))
            tag("l%d" % part)
            if WHO[1 + part] == "V":
                vts(A("CR", l0, l0 + n), A(row, 0, n), 0.5, OP.add)
            else:
                act(A("CR", l0, l0 + n), A(row, 0, n), FN.Identity, 0.5)
            tag("R%d" % part)
            mlu = A("MLU%d" % (t % 2), 2 * y0, 2 * y0 + ny)
            vts(mlu, A(p, 448, 448 + ny), 2048.0, OP.add)
            vts(A("E", n + 1, EN, EW), A(p, 448 + ny, 448 + 2 * ny), 0.5, OP.is_lt, -64 * CAP, OP.mult)
            for y in range(ny):
                vts(A("E", EW * y, EW * y + 16 * y + 16), A("CR", l0, l0 + 16 * y + 16), A(p, 448 + y, 449 + y), OP.is_equal)
                tag("e%d%d" % (part, y))
                line.append(len(calls) - 1)
            scan_(A("EZ", EN * part, EN * part + EN), A("EM"), A("E"), 0.0)
            line.append(len(calls) - 1)
            tag("Z%d" % part)
            z = A("EZ", EN * part + n + 1, EN * part + EN, EW)
            vtt(A("R3", 2 * y0, 2 * y0 + ny), A("KS", 16 * t + y0, 16 * t + y0 + ny), z, OP.min)
            vtt(A("R3", 2 * y0 + ny, 2 * y0 + 2 * ny), A(p, 448, 448 + ny), z, OP.min)
            vtt(A("R4", 2 * y0, 2 * y0 + 2 * ny), A("R3", 2 * y0, 2 * y0 + 2 * ny), A("KD", 2 * y0, 2 * y0 + 2 * ny), OP.max)
            ofs = A("OFS%d" % (t % 2), 2 * y0, 2 * y0 + 2 * ny)
            vts(ofs, A("R4", 2 * y0, 2 * y0 + 2 * ny), 2560.0, OP.add)
            tag("o%d" % part)
            src = N if t < 3 else "INV0"
            if WHO[3 + part] == "V":
                vcp(A("VB", 2 * l0, 2 * l0 + n), ind(A(src, 512, 4608), mlu))
            else:
                act(A("VB", 2 * l0, 2 * l0 + n), ind(A(src, 512, 4608), mlu), FN.Copy)
            if t < 3 and part and SPLIT == 1:
                act(ind(A(src, 0, 4608), A("OFS%d" % (t % 2), 0, y0)), A("VB", 0, l0), FN.Silu)
            if t < 3 and l0 + n < 256 and SPLIT < 2:
                h = ny if SPLIT else 0
                act(ind(A(src, 0, 4608), A("OFS%d" % (t % 2), h, 2 * ny)), A("VB", 16 * h, 2 * n), FN.Silu)
            else:
                vcp(ind(A(src, 0, 4608), ofs), A("VB", 2 * l0, 2 * l0 + 2 * n))
        for u in ([], [0], [1, 2], [])[t]:
            for l0, n, p, row in PART:
                act(A("OV", l0, l0 + n), ind(A("OO", 512, 4608), A("MLU%d" % (u % 2), l0 // 8, l0 // 8 + n // 16)), FN.Copy)
                if u < t and not l0:
                    tag("m")
            for l0, n, p, row in PART:
                act(ind(A("OO"), A("OFS%d" % (u % 2), l0 // 8, l0 // 8 + n // 16)), A("OV", l0, l0 + n), FN.Silu)
        if t < 3:
            needs(t + 1)
        for order in [line] + [[tags[w] for w in x.split() if w in tags] for x in TAIL[t]]:
            for a, b in zip(order, order[1:]):
                calls[b]["after"].setdefault(a, False)
    dma(T.y[:, :], T.INV0[0:128:16, 512:4608], [A("INV0")], [], 2.6)
    issue()
    for t in range(3):
        g.wait_ge(T.sem["loc%d" % t], len(topo.engines(core, T.cores[(rank + 1) % len(T.cores)])))
